import numpy as np, ml_dtypes
CORES = [23,119,17,113]
N = 4
import mx_ref
BF = ml_dtypes.bfloat16
def gcols(t, e):
    v = np.concatenate([t.reshape(8, 16, -1, 4), np.zeros((8, 16, 1, 4), BF)], axis=2)
    return np.ascontiguousarray(np.stack([v[g][:, e[g]] for g in range(8)])).reshape(128, -1)
def tile(rs):
    return np.stack(rs, axis=2).reshape(128, -1).astype(BF)
def cut(t, i, w=512):
    return t[:, w * i:w * i + w]
def pick(q, e):
    c = np.concatenate([q[0].reshape(128, -1, 4), np.zeros((128, 1, 4), np.uint8)], axis=1); s = np.concatenate([q[1], np.ones((16, 1), np.uint8)], axis=1)
    return (np.ascontiguousarray(c[:, e].reshape(128, -1)), np.ascontiguousarray(s[:, e]))
def join(*qs):
    return (np.concatenate([q[0] for q in qs], axis=1), np.concatenate([q[1] for q in qs], axis=1))
def put(q, e, v):
    c, s = q[0].reshape(128, -1, 4).copy(), q[1].copy(); c[:, e] = v[0].reshape(128, -1, 4); s[:, e] = v[1]
    return (c.reshape(128, -1), s)
def pk(c, s):
    return (np.ascontiguousarray(c), mx_ref.live(s))
def emit(q):
    return q[0], q[1]
def packed(v, rng):
    q = [mx_ref.quantize(np.ascontiguousarray(v[r])) for r in range(N)]
    return np.stack([a for a, b in q]), np.stack([mx_ref.plane(b, rng) for a, b in q])
def values_of_codes():
    e, c = np.zeros((128, 128, 4), np.float32), np.zeros((128, 2, 4), np.uint8)
    e[np.arange(128), np.arange(128), 0] = 1
    c[:127, :, 0] = np.arange(256).reshape(2, 128).T[:127]
    return mx_ref.matmul(mx_ref.quantize(e.reshape(128, 512).astype(BF)), (c.reshape(128, 8), np.full((16, 2), 127, np.uint8))).T.reshape(-1).astype(np.float64)
CODE_VALUE, SCALE_VALUE = values_of_codes(), 2.0 ** (np.arange(256) - 127.0)
def decode(q):
    return (CODE_VALUE[q[0]].reshape(16, 8, -1, 4) * SCALE_VALUE[q[1]][:, None, :, None] + 0.0).reshape(128, -1).astype(np.float32)
def f(rng, *shape):
    return mx_ref.flush((rng.standard_normal(shape, dtype=np.float32) * np.exp2(rng.integers(-2, 3, shape[:-1] + (1,)))).astype(BF))
def wide(rng, *shape, cols=0):
    v = rng.standard_normal(shape, dtype=np.float32) * np.exp2(rng.integers(-12, 13, shape)).astype(np.float32)
    if cols: v *= np.repeat(np.exp2(rng.integers(-cols, cols + 1, shape[:-2] + (1, shape[-1] // 4))) * (rng.random(shape[:-2] + (1, shape[-1] // 4)) > 0.0625), 4, axis=-1).astype(np.float32)
    return mx_ref.flush(v.astype(BF))
C, H, E, R = 320, 96, 416, 3
def big(v):
    v = v.astype(np.float32)
    v[np.abs(v) < np.float32(2.0 ** -16)] = 0
    return v.astype(BF)
def numbers_of(rng):
    return {"x": big(f(rng, N, 128, 4 * C)), "u": np.array(f(rng, N, 128, 512)), "v": np.array(f(rng, N, 128, 512))}
def layers(rng):
    return big(f(rng, N, 128, 2048)).reshape(N, 8, 16, 4, 8, 16, 4)
def weights(rng, w):
    c, p = packed(np.ascontiguousarray(w).reshape(N, 128, 2048), rng)
    return {"wc": c, "ws": p}
def setup_inputs(rng):
    return {**numbers_of(rng), **weights(rng, layers(rng))}
def setup_inputs_ties(rng):
    d = numbers_of(rng)
    e = rng.permutation(N)
    x = d["x"].reshape(N, 8, 16, C, 4)
    for r in range(N):
        k = rng.permutation(C) % 3
        if r == e[0]: k = np.zeros(C, int)
        elif r in e[2::2]: k = rng.permutation(3)[np.arange(C) % 3]
        a = x[r][:, :8, :3].copy()
        a[:, :, 2] = 0
        x[r][:, :8] = a[:, :, k]
    x[e[1]] = 0
    u = d["u"].reshape(N, 8, 16, 128, 4)
    u[:, :, 8:, ::16] = 0
    u[:, :, 8:, 1::16] = 0
    w = layers(rng)
    w[:, :, :, :, :, :8] = 0
    return {"x": x.reshape(N, 128, 4 * C), "u": u.reshape(N, 128, 512), "v": d["v"], **weights(rng, w)}
def setup_inputs_near(rng):
    d = numbers_of(rng)
    x = d["x"].reshape(N, 8, 16, C, 4)
    u = d["u"].reshape(N, 128, 128, 4)
    o = rng.permutation(N) % 4
    x[:, :, :8] = 0
    u[:, :, ::16] = 0
    u[:, :, 1::16] = 0
    for r in range(N):
        s = rng.integers(-1, 2, (8, 2, C)).astype(np.float32)
        if o[r] % 2 == 1: s = s[:, :, np.arange(C) // 16]
        if o[r] < 2: s = s * np.float32(2.0 ** -29)
        for g in rng.permutation(8)[:4]: s[g, :, rng.integers(C)] = 2.0 ** 29 * rng.choice([-1.0, 1.0], 2)
        x[r, :, :2, :, 0] = s.astype(BF)
        for h in range(0, 128, 16):
            u[r, h, h, 0] = 2.0 ** -30 if o[r] < 2 else 1.0
            u[r, h + 1, h + 1, 0] = 2.0 ** -30 if o[r] < 2 else 1.0
    w = layers(rng)
    w[:, :, :8] = 0
    w[:, :, :, :, :, :8] = 0
    return {"x": x.reshape(N, 128, 4 * C), "u": u.reshape(N, 128, 512), "v": d["v"], **weights(rng, w)}
def setup_inputs_late(rng):
    d = numbers_of(rng)
    x = d["x"].reshape(N, 8, 16, C, 4)
    c = (rng.permutation(N) % 2 * 2.0 - 1.0).astype(np.float32).astype(BF)
    x[:, :, 0] = c[:, None, None, None]
    u = d["u"].reshape(N, 128, 128, 4)
    u[:, :, ::16] = 0
    u[:, :, 1::16] = 0
    for h in range(0, 128, 16):
        u[:, h, h, 0] = 1
        u[:, h, h + 1, 1] = 1
    return {"x": x.reshape(N, 128, 4 * C), "u": u.reshape(N, 128, 512), "v": d["v"], **weights(rng, layers(rng))}
def setup_inputs_huge(rng):
    d = numbers_of(rng)
    h = rng.permutation(8)
    x = -0.95 - 0.05 * rng.random((N, 8, 16, C, 4))
    x[:, h[4:]] = (0.75 + 0.1 * rng.random((N, 4, 16, C, 4))) * rng.choice([-1.0, 1.0], (N, 4, 1, C, 1))
    u = d["u"].reshape(N, 128, 128, 4)
    u[:, :, ::16] = 0
    u[:, :, 1::16] = 0
    for r in range(N):
        for g in range(8):
            for b in range(2):
                a = 16 * int(rng.choice(h[4:]))
                u[r, a:a + 16, 16 * g + b] = (2.0 ** 30 * (1 - 0.1 * rng.random((16, 4))) * rng.choice([-1.0, 1.0])).astype(np.float32).astype(BF)
    w = np.zeros((N, 128, 4, 128, 4), np.float32)
    i = np.arange(128)
    for b in range(4): w[:, i, b, i, b] = -1
    return {"x": (2.0 ** 30 * x).astype(np.float32).reshape(N, 128, 4 * C).astype(BF), "u": u.reshape(N, 128, 512), "v": d["v"], **weights(rng, w.astype(BF))}
def setup_inputs_spread(rng):
    d = setup_inputs(rng)
    d["x"] = big(wide(rng, N, 128, 4 * C, cols=6))
    return d
def check_inputs(d):
    b = []
    for k in ("x", "u", "v"):
        a = np.abs(d[k].astype(np.float32))
        if not (np.isfinite(a).all() and ((a == 0) | (a >= 2.0 ** -30) & (a <= 2.0 ** 30)).all()): b.append("a value of " + k)
    none, least, most = [emit(mx_ref.quantize(np.full((128, 16), k, np.float32).astype(BF)))[1][0, 0] for k in (0.0, 2.0 ** -30, 2.0 ** 30)]
    for r in range(N):
        if ((d["wc"][r] == 0x7F) | (d["wc"][r] == 0xFF)).any(): b.append("wc: a code that is no number")
        s = mx_ref.live(d["ws"][r])
        if ((s != none) & ((s < least) | (s > most))).any(): b.append("ws: a scale out of range")
    return b
def reference(x, u, v, wc, ws):
    qu = [mx_ref.quantize(u[r]) for r in range(N)]
    lay = [pk(wc[r], ws[r]) for r in range(N)]
    now = [x[r] for r in range(N)]
    level = np.zeros((N, 8, E), np.int64)
    for t in range(R):
        d = 2 ** t
        q = [mx_ref.quantize(now[r]) for r in range(N)]
        halo = [pick(q[r], np.arange(H)) for r in range(N)]
        came = decode(join(*halo)).astype(BF)
        made = []
        for r in range(N):
            e = (r + 1) % N
            s = mx_ref.matmul(qu[r], join(q[r], halo[e]))
            if t == 0: word = 2 * (s[::16] > 0) + (s[1::16] > 0)
            else: word = 2 * level[r] + (s[::16] > 0)
            key = 1024 * word
            key[:, :E - d] += 1 + word[:, d:]
            o = np.argsort(key, axis=1, kind="stable")
            for g in range(8): level[r, g] = np.searchsorted(key[g, o[g]], key[g])
            n, m = np.zeros((8, E), np.int64), np.zeros((8, E), np.int64)
            np.put_along_axis(n, o, np.concatenate([o[:, :1], o[:, :-1]], axis=1), axis=1)
            np.put_along_axis(m, o, np.concatenate([o[:, 1:], o[:, -1:]], axis=1), axis=1)
            a = np.concatenate([now[r], cut(came, e, 4 * H)], axis=1)
            most = np.maximum(gcols(a, n[:, :C]).astype(np.float32), gcols(a, m[:, :C]).astype(np.float32))
            z = mx_ref.quantize(((now[r].astype(np.float32) + most) * np.float32(0.5)).astype(BF))
            made.append(tile([mx_ref.matmul(pick(lay[r], np.arange(128 * b, 128 * b + 128)), z) * np.float32(0.03125) + now[r][:, b::4].astype(np.float32) for b in range(4)]))
        now = made
    y, lv = np.zeros((N, 128, C), np.float32), np.zeros((N, 8, E), np.float32)
    oc, osc = np.zeros((N, 128, 4 * C), np.uint8), np.zeros((N, 16, C), np.uint8)
    for r in range(N):
        q = mx_ref.quantize(now[r])
        y[r] = mx_ref.matmul(mx_ref.quantize(v[r]), q)
        lv[r] = level[r]
        oc[r], osc[r] = emit(q)
    return {"y": y, "lv": lv, "oc": oc, "osc": osc}

@@ -1,0 +1,489 @@
+from concourse.mybir import dt, AluOpType, ActivationFunctionType
+
+A = AluOpType
+F = ActivationFunctionType
+C, H, E, R = 320, 96, 416, 3
+C0 = 192
+NB, AB, EB = 26, 11, 18
+PARTS = (".a", ".b", ".l")
+MUL = (5.0, 41.0, 3281.0)
+WC = 1640.0
+CEN = (0.0, 0.0, 5380000.0 - 3282.0 * WC)
+NT = 496
+BIG = 11010048.0
+BIGV = 2048.0
+TILES = (((0, 23, 24, 25), 416), ((7, 8, 9, 10), 160), ((11, 12, 13, 14), 224), ((15, 16, 17, 18), 288),
+         ((19, 20, 21, 22), 352), ((3, 4, 5, 6), 128), ((1, 2), 128))
+TD, DC = 0, 23
+LATE = (None, (3, 18, 19, 20, 21, 22, 4, 5, 6, 1, 2), (3, 4, 23, 18, 19, 20, 21, 22, 5, 6, 1, 2))
+TOFF = [sum(w for _, w in TILES[:k]) for k in range(len(TILES) + 1)]
+Q4, U8, BF, F16, F32, I32, U16 = "float8_e4m3fn_x4", "uint8", "bfloat16", "float16", "float32", "int32", "uint16"
+
+
+def _sb(n, d):
+    return ("sbuf", [128, n], d)
+
+
+SCRATCH = {
+    "xt": _sb(4 * C, BF), "x32": _sb(4 * C, BF), "ut": _sb(512, BF), "vt": _sb(512, BF),
+    "qw": _sb(512, Q4), "sw": _sb(512, U8), "qu": _sb(128, Q4), "su": _sb(128, U8),
+    "qa": _sb(128, Q4), "sa": _sb(128, U8), "qb": _sb(128, Q4), "sb": _sb(128, U8), "qv": _sb(128, Q4), "sv": _sb(128, U8),
+    "et": _sb(2048, BF), "qe": _sb(512, Q4), "se": _sb(512, U8), "ct": _sb(1536, BF), "qc": _sb(384, Q4), "sc": _sb(384, U8),
+    "tr": _sb(512, BF), "qr": _sb(128, Q4), "sr": _sb(128, U8),
+    "i4": _sb(528, F32), "jm": _sb(E, BF), "pi": _sb(8, I32), "ci": _sb(8, I32), "cf": _sb(8, F32),
+    "cj": _sb(32, F32), "cv": _sb(32, F32), "cw": _sb(32, I32), "ob": _sb(32, U16),
+    "col": _sb(8, F32), "vv": _sb(16, F32), "d0a": _sb(E, BF), "d0b": _sb(E, BF), "d0k": _sb(E, BF), "d0v": _sb(C, BF),
+    "tie": _sb(E, BF), "zr": _sb(512, BF), "oab": _sb(16, U16), "od": _sb(32, U16),
+    "xo": _sb(4 * NT, BF), "qo": _sb(NT, Q4), "so": _sb(NT, U8), "oi": _sb(32, U16), "tab": _sb(NT, F32), "gt": _sb(E, F32),
+    "ab": _sb(E, BF), "k2b": _sb(E, BF), "k2f": _sb(E, F16), "wb": _sb(E + 16, BF), "wf": _sb(E + 16, F16),
+    "mb": _sb(E, BF), "mh": _sb(E, F16), "mf": _sb(E, F32), "kb": _sb(E, BF), "kh": _sb(E, F16), "kf": _sb(E, F32),
+    "kth": _sb(E, F16), "ktf": _sb(E, F32), "jk": _sb(3 * E, F16),
+    "sk": _sb(E, F32), "kw": _sb(32, F32), "rw": _sb(32, F32), "rc": _sb(32, F32), "dd": _sb(32, F32),
+    "tb": _sb(4 * TOFF[-1], BF), "qt": _sb(TOFF[-1], Q4), "st": _sb(TOFF[-1], U8),
+    "pos": _sb(32, U16), "onm": _sb(40, U16), "ordr": _sb(E, F32), "gn": _sb(C, F32), "gm": _sb(C, F16),
+    "sn": _sb(C, F32), "sm": _sb(C, F16), "ov": _sb(160, U16),
+    "g1": _sb(4 * C, BF), "g3": _sb(4 * C, BF), "g2": _sb(4 * C, BF), "zt": _sb(4 * C, BF), "qz": _sb(C, Q4), "sz": _sb(C, U8),
+    "ow": _sb(32, U16), "ks": _sb(E, F32), "dk": _sb(E, F32), "ls": _sb(E, F32), "lr": _sb(E, F32), "ys": _sb(C, F32),
+    "pa": ("psum", [128, 2048], F32), "pb": ("psum", [128, 2048], F32),
+}
+for _t in range(R):
+    SCRATCH["vh%d" % _t] = _sb(4 * E, BF)
+for _t in range(R + 1):
+    SCRATCH["q%d" % _t] = _sb(E, Q4)
+    SCRATCH["s%d" % _t] = _sb(E, U8)
+SEMAPHORES = ["pe", "dve", "act", "gp", "snd", "arr0", "arr1", "arr2"] + ["d%d" % k for k in range(20)]
+
+
+def rank_program(g, core, T, topo):
+    rank = T.rank_of(core)
+    if rank is None:
+        return
+    cores = list(T.cores)
+    before = cores[(rank - 1) % len(cores)]
+    rid, pid, _ = topo.addr(before)
+    mask = topo.mask(core, before)
+    neng = len(topo.engines(core, before))
+    V, S, P = g.vector, g.scalar, g.tensor
+    queue = {"pe": P, "dve": V, "act": S, "gp": g, "sp": g.sync}
+    cnt, know, snap, lastw, readers = {}, {k: {} for k in queue}, {}, {}, {}
+    ndma = [0]
+    spare = []
+
+    def need(eng, r, w):
+        deps = {}
+        for t in list(r) + list(w):
+            assert t in w or t in lastw, t
+            for d in [lastw.get(t)] + (readers.get(t, []) if t in w else []):
+                if d is not None and not (eng == "pe" and d[0] == "pe"):
+                    deps[d[0]] = max(deps.get(d[0], 0), d[1])
+        for s, v in sorted(deps.items(), key=lambda e: e[0] == eng):
+            if know[eng].get(s, 0) < v:
+                queue[eng].wait_ge(T.sem[s], v)
+                know[eng][s] = v
+                for s2, v2 in snap.get((s, v), {}).items():
+                    know[eng][s2] = max(know[eng].get(s2, 0), v2)
+
+    def done(eng, src, val, r, w):
+        snap[(src, val)] = dict(know[eng])
+        for t in r:
+            readers.setdefault(t, []).append((src, val))
+        for t in w:
+            lastw[t] = (src, val)
+            readers[t] = []
+
+    def op(eng, fn, r=(), w=()):
+        need(eng, r, w)
+        cnt[eng] = cnt.get(eng, 0) + 1
+        fn().then_inc(T.sem[eng], 1)
+        done(eng, eng, cnt[eng], r, w)
+
+    def gap(n=1):
+        for _ in range(min(n, len(spare))):
+            spare.pop(0)()
+
+    def dma(eng, out, in_, r=(), w=()):
+        need(eng, r, w)
+        s = "d%d" % ndma[0]
+        ndma[0] += 1
+        cnt[s] = 16
+        queue[eng].dma_start(out, in_).then_inc(T.sem[s], 16)
+        done(eng, s, 16, r, w)
+
+    def ts(out, in0, s1, s2, o0, o1=None, r=(), w=()):
+        if o1 is None:
+            op("dve", lambda: V.tensor_scalar(out, in0, s1, None, o0), r, w)
+        else:
+            op("dve", lambda: V.tensor_scalar(out, in0, s1, s2, o0, o1), r, w)
+
+    def tt(out, a, b, o, r=(), w=()):
+        op("dve", lambda: V.tensor_tensor(out, a, b, o), r, w)
+
+    def cp(out, a, r=(), w=()):
+        op("dve", lambda: V.tensor_copy(out, a), r, w)
+
+    def ms(out, c, w=()):
+        op("dve", lambda: V.memset(out, c), (), w)
+
+    def scan(out, d0, d1, o0, o1, r=(), w=()):
+        op("dve", lambda: V.tensor_tensor_scan(out, d0, d1, 0.0, o0, o1), r, w)
+
+    def quant(q, s, a, b, tile, r=(), w=()):
+        op("dve", lambda: V.quantize_mx(q[:, a:b], s[:, a:b], tile[:, 4 * a:4 * b]), r, w)
+
+    def act(out, in_, func, r=(), w=(), **kw):
+        op("act", lambda: S.activation(out, in_, func, **kw), r, w)
+
+    def mm(out, q, s, a, q2, s2, b0, b1, r=(), w=(), start=True, stop=True):
+        op("pe", lambda: P.matmul_mx(out, q[:, a:a + 128], s[:, a:a + 128], q2[:, b0:b1], s2[:, b0:b1], start, stop), r, w)
+
+    def bank(p, k, a, b):
+        return p[:, 512 * k + a:512 * k + b]
+
+    def iota(out, pat, base, cm, w, small=True):
+        if small:
+            op("gp", lambda: g.iota(out, pat, base, cm, allow_small_or_imprecise_dtypes=True), (), w)
+        else:
+            op("gp", lambda: g.iota(out, pat, base, cm), (), w)
+
+    def keep(out, in_, pat, cmp, base, cm, r, w):
+        op("gp", lambda: g.affine_select(out, in_, pat, cmp, 0.0, base, cm), r, w)
+
+    def send(t):
+        q, s = T["q%d" % t], T["s%d" % t]
+        need("gp", ["q%d.0" % t], [])
+        g.remote_dma(q[:, C:E].bitcast(dt.uint8), q[:, 0:H].bitcast(dt.uint8), T.sem["arr%d" % t], T.sem.snd, pid, rid, mask)
+        g.remote_dma(s[:, C:E], s[:, 0:H], T.sem["arr%d" % t], T.sem.snd, pid, rid, mask)
+        cnt["snd"] = cnt.get("snd", 0) + 2 * neng
+        lastw["q%d.h" % t] = ("arr%d" % t, 2 * neng)
+
+    def weave(*lists):
+        for k in range(max(len(x) for x in lists)):
+            for x in lists:
+                if k < len(x):
+                    x[k]()
+
+    CH = ((0, C0), (C0, C))
+    cf, col = T.cf, T.col
+    four = range(4)
+    x0 = ["xt.0.%d" % b for b in four]
+    dma("sp", T.xt[:, 0:512], T.x[:, 0:512], w=x0)
+    dma("act", T.ut[:], T.u[:], w=["ut"])
+    dma("sp", T.xt[:, 512:4 * C], T.x[:, 512:4 * C], w=["xt.1"])
+    dma("sp", T.qw[:].bitcast(dt.uint8), T.wc[:], r=["xt.1"], w=["qw"])
+    dma("sp", T.sw[:], T.ws[:], w=["sw"])
+    dma("sp", T.vt[:], T.v[:], w=["vt"])
+    iota(T.pi[:, 0:4], [[0, 2], [1, 2]], 0, 1, ["pi"], False)
+    iota(T.jm[:], [[0, NB], [1, 16]], 0, 0, ["jm"])
+    iota(T.i4[:], [[4, 528]], 0, 0, ["i4"])
+    ms(T.xo[:], 0.0, w=["xo0", "xo1"])
+    ts(T.ci[:, 0:2], T.pi[:, 0:2], 15, None, A.bitwise_and, r=["pi"], w=["ci0"])
+    ts(T.ci[:, 2:3], T.pi[:, 0:1], 2, 3, A.arith_shift_right, A.bitwise_and, r=["pi"], w=["ci1"])
+    ts(T.ci[:, 3:4], T.pi[:, 0:1], 3, None, A.bitwise_and, r=["pi"], w=["ci2"])
+    ms(T.zr[:], 0.0, w=["zr"])
+    cp(cf[:, 0:4], T.ci[:, 0:4], r=["ci0", "ci1", "ci2"], w=["cf"])
+    ts(T.oab[:, 0:8], T.jm[:, 0:8], 16.0, None, A.mult, r=["jm"], w=["oa"])
+    ts(T.oab[:, 8:16], T.jm[:, 0:8], 16.0, 1.0, A.mult, A.add, r=["jm"], w=["ob"])
+    ts(T.d0a[:], T.jm[:], cf[:, 0:1], -2.0 * BIG, A.is_equal, A.mult, r=["jm", "cf"], w=["d0a"])
+    ts(T.d0b[:], T.jm[:], cf[:, 1:2], BIG, A.is_equal, A.mult, r=["jm", "cf"], w=["d0b"])
+    act(T.tr[:], T.zr[:], F.Copy, r=["zr"], w=["tr0", "tr1"])
+    act(T.ct[:, 0:512], T.zr[:], F.Identity, bias=1.0, r=["zr"], w=["ct0"])
+    quant(T.q0, T.s0, 0, 128, T.xt, r=x0, w=["q0.0"])
+    send(0)
+    keep(T.ct[:, 0:512], T.ct[:, 0:512], [[-16, 8], [0, 64]], A.is_ge, 0, 1, [], ["ct0"])
+    keep(T.ct[:, 0:512], T.ct[:, 0:512], [[16, 8], [0, 64]], A.is_ge, 15, -1, [], ["ct0"])
+    keep(T.tr[:, 0:512:4], T.ct[:, 0:512:4], [[1, 128]], A.is_gt, 0, -1, ["ct0"], ["tr0"])
+    keep(T.tr[:, 1:512:4], T.ct[:, 0:512:4], [[-1, 128]], A.is_ge, 0, 1, ["ct0"], ["tr1"])
+    quant(T.qu, T.su, 0, 128, T.ut, r=["ut"], w=["qu"])
+    tt(T.d0k[:], T.d0a[:], T.d0b[:], A.add, r=["d0a", "d0b"], w=["d0k"])
+    for q, s, lo, tok in ((T.qa, T.sa, 0, "a"), (T.qb, T.sb, 8, "b")):
+        cp(q[:, 0:128].bitcast(dt.uint32), T.qu[:, 0:128].bitcast(dt.uint32).indirect(T.oab[:, lo:lo + 8]), r=["qu", "o" + tok], w=["q" + tok])
+        act(s[:, 0:128], T.su[:, 0:128].indirect(T.oab[:, lo:lo + 8]), F.Copy, r=["qu", "o" + tok], w=["s" + tok])
+    quant(T.q0, T.s0, 128, C, T.xt, r=["xt.1"], w=["q0.1"])
+    for b in four:
+        act(T.et[:, 512 * b:512 * (b + 1)], T.zr[:], F.Copy, r=["zr"], w=["et%d" % b])
+        keep(T.et[:, 512 * b + b:512 * (b + 1):4], T.ct[:, 0:512:4], [[1, 128]], A.is_equal, 0, -1, ["ct0"], ["et%d" % b])
+    act(T.vh0[:, 0:4 * C], T.xt[:], F.Copy, scale=0.5, r=x0 + ["xt.1"], w=["vh0.0", "vh0.1"])
+    act(T.x32[:], T.xt[:], F.Copy, scale=32.0, r=x0 + ["xt.1"], w=["x32.%d.%d" % (h, b) for h in range(2) for b in four])
+
+    def hold_pattern():
+        tt(T.vv[:, 4:8], T.vv[:, 8:12], T.vv[:, 12:16], A.add, r=["vv1", "vv2"], w=["vv0"])
+        for b in four:
+            act(T.d0v[:, b:C:4], T.jm[:, 0:C // 4], F.Identity, scale=0.0, bias=T.vv[:, 4 + b:5 + b], r=["jm", "vv0"], w=["d0v%d" % b])
+
+    spare.extend([
+        lambda: ts(col[:, 0:1], cf[:, 0:1], 15.0, BIG, A.is_lt, A.mult, r=["cf"], w=["col0"]),
+        lambda: ts(T.cj[:, 0:31], T.i4[:, 0:31], 4.0, cf[:, 0:1], A.mult, A.add, r=["i4", "cf"], w=["cj"]),
+        lambda: ms(T.wb[:, E:E + 16], -1.0, w=["wb.p"]),
+        lambda: ts(T.cv[:, 0:31], T.cj[:, 0:31], 12.5, 1.0 / NB, A.add, A.mult, r=["cj"], w=["cv"]),
+        lambda: cp(T.cw[:, 0:31], T.cv[:, 0:31], r=["cv"], w=["cw"]),
+        lambda: ts(T.cv[:, 0:31], T.cw[:, 0:31], -1.0 * NB, NB - 1.0, A.mult, A.add, r=["cw"], w=["cv"]),
+        lambda: tt(T.cj[:, 0:31], T.cj[:, 0:31], T.cv[:, 0:31], A.add, r=["cv"], w=["cj"]),
+        lambda: cp(T.ob[:, 0:31], T.cj[:, 0:31], r=["cj"], w=["obk"]),
+        lambda: ts(T.vv[:, 0:4], T.jm[:, 0:4], cf[:, 2:3], None, A.subtract, r=["cf", "jm"], w=["vv0"]),
+        lambda: ts(T.vv[:, 8:12], T.vv[:, 0:4], 0.0, -2.0 * BIGV, A.is_equal, A.mult, r=["vv0"], w=["vv1"]),
+        lambda: ts(T.vv[:, 12:16], T.vv[:, 0:4], 1.0, BIGV, A.is_equal, A.mult, r=["vv0"], w=["vv2"]),
+        hold_pattern,
+        lambda: ts(col[:, 2:3], cf[:, 2:3], 3.0, -BIGV, A.is_lt, A.mult, r=["cf"], w=["col2"]),
+        lambda: tt(col[:, 3:4], col[:, 2:3], cf[:, 3:4], A.add, r=["col2", "cf"], w=["col3"]),
+        lambda: ts(T.od[:, 0:NB], T.i4[:, 0:NB], 0.25, None, A.mult, r=["i4"], w=["od"]),
+        lambda: ms(T.wf[:, E:E + 16], -1.0 - WC, w=["wf.p"]),
+        lambda: ms(T.rw[:, 0:1], 0.0, w=["rw0"]),
+        lambda: ms(T.dk[:, 0:1], 0.0, w=["dk0"]),
+        lambda: ts(col[:, 1:2], col[:, 0:1], 432.0, None, A.add, r=["col0"], w=["col1"]),
+    ])
+
+    for t in range(R):
+        d = 2 ** t
+        dc = DC + (t == 2)
+        q, s, vh = T["q%d" % t], T["s%d" % t], T["vh%d" % t]
+        qn = "q%d" % t
+        k2, k2n = (T.k2f, "k2f") if t == 2 else (T.k2b, "k2b")
+        wv, wn = (T.wf, "wf") if t == 2 else (T.wb, "wb")
+        kn = "bhf"[t]
+        mw, kk = T["m" + kn], T["k" + kn]
+        ka, kan = (T.kb, "kb") if t == 0 else (T.kf, "kf")
+
+        def signs(part, a, b, pk, o):
+            ts(T.ab[:, a:b], bank(T.pb, pk, o, o + b - a), 0.0, None, A.is_gt, w=["pb%d" % pk, "ab" + part])
+
+        def chain(part, wa, wb, c0, c1, ws):
+            a, b = 16 * c0, 16 * c1
+            ws = [wn + p for p in ws]
+            steps = [
+                lambda: tt(wv[:, wa:wb], k2[:, wa:wb], T.ab[:, wa:wb], A.add, r=[k2n + part, "ab" + part], w=[wn + part]),
+                lambda: ts(mw[:, a:b], wv[:, a:b], MUL[t], 1.0 - CEN[t], A.mult, A.add, r=ws, w=["m" + kn + part]),
+                lambda: tt(kk[:, a:b], mw[:, a:b], wv[:, a + d:b + d], A.add, r=ws + ["m" + kn + part], w=["k" + kn + part]),
+                lambda: scan(T.sk[:, a:b], T.d0k[:, a:b], kk[:, a:b], A.add, A.max, r=["d0k", "k" + kn + part], w=["sk" + part])]
+            if t == 1:
+                steps.append(lambda: cp(ka[:, a:b], kk[:, a:b], r=["k" + kn + part], w=[kan + part]))
+            if t:
+                steps.append(lambda: ts(T.kw[:, c0:c1], T.sk[:, a + 15:b:16], col[:, 0:1], 0.5, A.subtract, A.add, r=["sk" + part, "col0"], w=["kw" + part]))
+            return steps
+
+        def compare(c):
+            k = [c in cs for cs, _ in TILES].index(True)
+            j = TILES[k][0].index(c)
+            o = 4 * TOFF[k] + j
+            row, rn = (kk, "k" + kn) if c >= dc else (ka, kan)
+            rs = [rn + p for p, lo in zip(PARTS, (0, AB, EB)) if c > lo] + ["kw.l" if c >= EB else "kw.b" if c >= AB else "kw.a"]
+            out = T.tb[:, o:o + 64 * c - j:4]
+            if c >= dc:
+                ts(out, row[:, 0:16 * c], T.kw[:, c:c + 1], 0.5, A.is_lt, A.subtract, r=rs, w=["tb%d.%d" % (k, j)])
+            else:
+                act(out, row[:, 0:16 * c], F.Sign, scale=-1.0, bias=T.kw[:, c:c + 1], accum_out=T.rw[:, c:c + 1],
+                    r=rs, w=["tb%d.%d" % (k, j), "rw%d" % c])
+
+        def rowsum(c):
+            j = c - DC + 1
+            o = 4 * TOFF[TD] + j
+            scan(T.jk[:, E * j - 16 * c:E * j], T.tb[:, o:o + 64 * c - j:4], T.zr[:, 0:16 * c], A.add, A.add,
+                 r=["tb%d.%d" % (TD, j), "zr"], w=["jk%d" % j])
+
+        def tied(part, c0, c1):
+            a, b = 16 * c0, 16 * c1
+            tt(T["kt" + kn][:, a:b], kk[:, a:b], T.tie[:, a:b], A.add,
+               r=["k" + kn + p for p in (PARTS[:2] if part == ".e" else PARTS[2:])] + ["tie"], w=["kt" + kn + part])
+
+        def inside(part, c0, c1, w0, tok):
+            a, b = 16 * c0, 16 * c1
+            o = 4 * TOFF[TD]
+            tt(T.tb[:, o + 4 * a:o + 4 * b:4], T.kw[:, w0:c1].indirect(T.od[:, c0 - w0:c1 - w0]), T["kt" + kn][:, a:b], A.is_gt,
+               r=["kw.a", "kw.b", "od", "kt" + kn + part] + ["kw.l"] * (part == ".l"), w=[tok])
+
+        def fold(k):
+            wd = TILES[k][1]
+            quant(T.qt, T.st, TOFF[k], TOFF[k] + wd, T.tb, r=["tb%d.%d" % (k, j) for j in four] + (["tbe"] if k == TD else []), w=["qt%d" % k])
+
+        def total(k):
+            wd = TILES[k][1]
+            mm(bank(T.pb, 0, 0, wd), T.qc, T.sc, 128 * t if k == TD else 0, T.qt, T.st, TOFF[k], TOFF[k] + wd,
+               r=["qc", "qt%d" % k], w=["pb0"], start=k == 0, stop=k == len(TILES) - 1)
+
+        sks = ["sk" + p for p in PARTS]
+        late = chain(".l", C, E, EB, NB, [".b", ".l", ".p"])
+        if t == 0:
+            mm(bank(T.pb, 0, 0, C), T.qa, T.sa, 0, q, s, 0, C, r=["qa", "sa", qn + ".0", qn + ".1"], w=["pb0"])
+            mm(bank(T.pb, 1, 0, C), T.qb, T.sb, 0, q, s, 0, C, r=["qb", "sb", qn + ".0", qn + ".1"], w=["pb1"])
+            gap(3)
+            ts(k2[:, 0:C], bank(T.pb, 0, 0, C), 0.0, 2.0, A.is_gt, A.mult, w=["pb0", k2n + ".a", k2n + ".b"])
+            signs(".b", 0, C, 1, 0)
+            weave([gap] * 4, chain(".b", 0, C, 0, EB, [".b"]))
+            mm(bank(T.pb, 2, 0, 128), T.qa, T.sa, 0, q, s, E - 128, E, r=["qa", "sa", qn + ".1", qn + ".h"], w=["pb2"])
+            mm(bank(T.pb, 3, 0, 128), T.qb, T.sb, 0, q, s, E - 128, E, r=["qb", "sb", qn + ".1", qn + ".h"], w=["pb3"])
+            ts(T.tie[:], T.jm[:], cf[:, 0:1], None, A.is_gt, r=["jm", "cf"], w=["tie"])
+            ts(k2[:, C:E], bank(T.pb, 2, 128 - H, 128), 0.0, 2.0, A.is_gt, A.mult, w=["pb2", k2n + ".l"])
+            signs(".l", C, E, 3, 128 - H)
+            weave([gap] * 4, late)
+            for n in ("kb", "sk"):
+                lastw[n + ".a"] = lastw[n + ".b"]
+            gap()
+            ts(T.dd[:, 0:NB], T.sk[:, 15:E:16], col[:, 0:1], 4.0 * NB, A.subtract, A.mult, r=sks + ["col0"], w=["dd"])
+            gap()
+            tt(T.kw[:, 0:NB], T.dd[:, 0:NB], T.i4[:, 0:NB], A.add, r=["dd", "i4"], w=["kw" + p for p in PARTS])
+            gap()
+            tt(T.xo[:, 0:4 * NT:4], T.kw[:, 0:NB].indirect(T.ob[:, 0:31]), T.i4[:, NB - 1:NB - 1 + NT], A.is_equal,
+               r=["kw.a", "obk", "i4"], w=["xo0"])
+            ts(T.oi[:, 0:NB], T.kw[:, 0:NB], 0.25, NB - 1.0, A.mult, A.subtract, r=["kw.a"], w=["oi"])
+            cp(T.xo[:, 5:4 * NT:4], T.xo[:, 0:4 * NT - 4:4], r=["xo0"], w=["xo1"])
+            quant(T.qr, T.sr, 0, 128, T.tr, r=["tr0", "tr1"], w=["qr"])
+            quant(T.qo, T.so, 0, NT, T.xo, r=["xo0", "xo1"], w=["qo"])
+            mm(bank(T.pb, 0, 0, NT), T.qr, T.sr, 0, T.qo, T.so, 0, NT, r=["qr", "qo"], w=["pb0"])
+            act(T.ct[:, 512:1024], T.ct[:, 0:512], F.Copy, scale=2.0, r=["ct0"], w=["ct1"])
+            for b in four:
+                act(T.ct[:, 1024 + b:1536:4], T.ct[:, 0:512:4], F.Copy, scale=1.0 if b == 1 else 2.0, r=["ct0"], w=["ct2%d" % b])
+            quant(T.qv, T.sv, 0, 128, T.vt, r=["vt"], w=["qv"])
+            gap(2)
+            scan(T.tab[:], bank(T.pb, 0, 0, NT), T.zr[:, 0:NT], A.add, A.add, r=["zr"], w=["pb0", "tab"])
+            act(T.gt[:], T.tab[:, 0:NT].indirect(T.oi[:, 0:NB]), F.Copy, r=["tab", "oi"], w=["gt"])
+            quant(T.qe, T.se, 0, 512, T.et, r=["et%d" % b for b in four], w=["qe"])
+            gap(9)
+            scan(T.sk[:], T.d0k[:], T.gt[:], A.add, A.max, r=["d0k", "gt"], w=sks)
+            ts(T.pos[:, 0:NB], T.sk[:, 15:E:16], col[:, 0:1], None, A.subtract, r=["sk.a", "col0"], w=["pos"])
+            ts(T.onm[:, 0:20], T.sk[:, 15:C:16], col[:, 0:1], 1.0, A.subtract, A.subtract, r=["sk.a", "col0"], w=["on"])
+        else:
+            mm(bank(T.pb, 1, 0, C - C0), T.qa, T.sa, 0, q, s, C0, C, r=["qa", "sa", qn + ".1"], w=["pb1"])
+            second = chain(".b", C0, C, AB, EB, [".a", ".b"])
+            weave(chain(".a", 0, C0, 0, AB, [".a"]), [lambda: None, lambda: signs(".b", C0, C, 1, 0)] + second[:3])
+            for c in range(7, AB):
+                compare(c)
+            weave(second[3:])
+            for c in range(AB, EB):
+                compare(c)
+            mm(bank(T.pb, 2, 0, 128), T.qa, T.sa, 0, q, s, E - 128, E, r=["qa", "sa", qn + ".1", qn + ".h"], w=["pb2"])
+            tied(".e", 0, EB)
+            signs(".l", C, E, 2, 128 - H)
+            weave([lambda: inside(".e", 0, EB, 0, "tbe"), lambda: fold(1)], late)
+            for c in LATE[t]:
+                compare(c)
+            tied(".l", EB, NB)
+            compare(dc)
+            inside(".l", EB, NB, 16, "tb%d.0" % TD)
+            for c in range(dc + 1, NB):
+                compare(c)
+            if t == 2:
+                fold(2)
+            fold(TD)
+            total(TD)
+            total(1)
+            for k in (2, 3):
+                if k == 3 or t == 1:
+                    fold(k)
+                total(k)
+            for c in range(dc, NB):
+                rowsum(c)
+            fold(4)
+            total(4)
+            ts(T.rc[:, dc:NB], T.jk[:, E * (dc - DC + 1) - 1:3 * E:E], 2.0, col[:, 1:2], A.mult, A.add, r=["jk1", "jk2", "jk3", "col1"], w=["rc1"])
+            for k in (5, 6):
+                fold(k)
+                total(k)
+            ts(T.rc[:, 0:dc], T.rw[:, 0:dc], col[:, 1:2], None, A.add, r=["rw%d" % c for c in range(dc)] + ["col1"], w=["rc0"])
+            scan(T.sk[:], T.d0k[:], bank(T.pb, 0, 0, E), A.add, A.max, r=["d0k"], w=["pb0"] + sks)
+            tt(T.dd[:, 0:NB], T.rc[:, 0:NB], T.sk[:, 15:E:16], A.subtract, r=["rc0", "rc1"] + sks, w=["dd"])
+            ts(T.pos[:, 0:NB], T.dd[:, 0:NB], 0.5, None, A.mult, r=["dd"], w=["pos"])
+            ts(T.onm[:, 0:20], T.dd[:, 0:20], 0.5, 1.0, A.mult, A.subtract, r=["dd"], w=["on"])
+        for b in four:
+            mm(bank(T.pa, b, 0, 128), T.qe, T.se, 128 * b, q, s, E - 128, E, r=["qe", qn + ".1", qn + ".h"], w=["pa%d" % b])
+            act(vh[:, 4 * C + b:4 * E:4], bank(T.pa, b, 128 - H, 128), F.Copy, scale=0.5, w=["pa%d" % b, "vh%d.h%d" % (t, b)])
+        if t == 0:
+            act(T.k2b[:], ka[:], F.Copy, scale=2.0, r=["kb" + p for p in PARTS], w=["k2b" + p for p in PARTS])
+            for k, (cs, wd) in enumerate(TILES):
+                lo = 0 if len(cs) < 4 else 16 * min(c for c in cs if c)
+                if k < 5:
+                    act(T.tb[:, 4 * (TOFF[k] + lo):4 * (TOFF[k] + wd)], T.zr[:, 0:4 * (wd - lo)], F.Copy, r=["zr"],
+                        w=["tb%d.%d" % (k, j) for j in four] + (["tbe"] if k == TD else []))
+        cp(T.ordr[:, 0:E].indirect(T.pos[:, 0:NB]), T.i4[:, 0:E], r=["pos", "i4"], w=["ordr"])
+        act(T.gn[:], T.ordr[:, 0:E].indirect(T.onm[:, 0:20]), F.Copy, r=["ordr", "on"], w=["gn"])
+        ts(T.onm[:, 20:40], T.pos[:, 0:20], 1.0, E - 1.0, A.add, A.min, r=["pos"], w=["om"])
+        cp(T.gm[:], T.ordr[:, 0:E].indirect(T.onm[:, 20:40]), r=["ordr", "om"], w=["gm"])
+        dv = ["d0v%d" % b for b in four]
+        scan(T.sn[:], T.d0v[:], T.gn[:], A.add, A.max, r=["gn"] + dv, w=["sn"])
+        ts(T.ov[:, 0:80], T.sn[:, 3:C:4], col[:, 3:4], None, A.add, r=["sn", "col3"], w=["ovn"])
+        scan(T.sm[:], T.d0v[:], T.gm[:], A.add, A.max, r=["gm"] + dv, w=["sm"])
+        if t == 0:
+            quant(T.qc, T.sc, 0, 384, T.ct, r=["ct0", "ct1"] + ["ct2%d" % b for b in four], w=["qc"])
+        if t == 1:
+            ts(T.k2f[:], kk[:], 2.0, -WC, A.mult, A.add, r=["kh" + p for p in PARTS], w=["k2f" + p for p in PARTS])
+        if t == R - 1:
+            scan(T.sk[:], T.d0k[:], T.ordr[:], A.add, A.max, r=["d0k", "ordr"], w=sks)
+        ts(T.ov[:, 80:160], T.sm[:, 3:C:4], col[:, 3:4], None, A.add, r=["sm", "col3"], w=["ovm"])
+        vr = ["vh%d.0" % t, "vh%d.1" % t] + ["vh%d.h%d" % (t, b) for b in four]
+        pieces = ((0, 64), (64, C0), (C0, C))
+        for k, (a, b) in enumerate(pieces):
+            act(T.g1[:, 4 * a:4 * b], vh[:, 0:4 * E].indirect(T.ov[:, a // 4:b // 4]), F.Copy, r=vr + ["ovn"], w=["g1.%d" % k])
+        act(T.g3[:, 4 * C0:4 * C], vh[:, 0:4 * E].indirect(T.ov[:, 80 + C0 // 4:160]), F.Copy, r=vr + ["ovm"], w=["g3"])
+
+        def most(k):
+            a, b = pieces[k]
+            if k < 2:
+                tt(T.g2[:, 4 * a:4 * b], vh[:, 0:4 * E].indirect(T.ov[:, 80 + a // 4:80 + b // 4]), T.g1[:, 4 * a:4 * b], A.max,
+                   r=vr + ["ovm", "g1.%d" % k], w=["g2.%d" % k])
+            else:
+                tt(T.g2[:, 4 * a:4 * b], T.g3[:, 4 * a:4 * b], T.g1[:, 4 * a:4 * b], A.max, r=["g3", "g1.%d" % k], w=["g2.%d" % k])
+
+        def blend(k):
+            a, b = pieces[k]
+            tt(T.zt[:, 4 * a:4 * b], T.g2[:, 4 * a:4 * b], vh[:, 4 * a:4 * b], A.add, r=["g2.%d" % k] + vr, w=["zt%d" % k])
+
+        def layer(h, ks):
+            a, b = CH[h]
+            quant(T.qz, T.sz, a, b, T.zt, r=["zt%d" % k for k in ks], w=["qz%d" % h])
+            p, pn = ((T.pa, "pa"), (T.pb, "pb"))[h]
+            for j in four:
+                mm(bank(p, j, 0, b - a), T.qw, T.sw, 128 * j, T.qz, T.sz, a, b, r=["qw", "sw", "qz%d" % h], w=["%s%d" % (pn, j)])
+
+        def state(h, js):
+            a, b = CH[h]
+            p, pn = ((T.pa, "pa"), (T.pb, "pb"))[h]
+            for j in js:
+                x = T.x32[:, 4 * a + j:4 * b:4]
+                tt(x, bank(p, j, 0, b - a), x, A.add, w=["%s%d" % (pn, j), "x32.%d.%d" % (h, j)])
+                if h == 0:
+                    act(T.xt[:, j:4 * C0:4], x, F.Copy, scale=0.03125, r=["x32.0.%d" % j], w=["xt.0.%d" % j])
+
+        xs = [["x32.%d.%d" % (h, j) for j in four] for h in range(2)]
+        q2, s2, qm = T["q%d" % (t + 1)], T["s%d" % (t + 1)], "q%d" % (t + 1)
+        most(0)
+        if t == R - 1:
+            ts(T.ow[:, 0:NB], T.sk[:, 15:E:16], col[:, 0:1], 0.25, A.subtract, A.mult, r=sks + ["col0"], w=["ow"])
+            act(T.ks[:], ka[:, 0:E].indirect(T.ow[:, 0:NB]), F.Copy, scale=2048.0, r=["kf" + p for p in PARTS] + ["ow"], w=["ks"])
+        blend(0)
+        most(1)
+        blend(1)
+        layer(0, (0, 1))
+        most(2)
+        state(0, (0,))
+        blend(2)
+        state(0, (1,))
+        layer(1, (2,))
+        state(0, (2, 3))
+        state(1, four)
+        quant(q2, s2, 0, C0, T.xt, r=x0, w=[qm + ".0"])
+        if t < R - 1:
+            send(t + 1)
+        ts(T.xt[:, 4 * C0:4 * C], T.x32[:, 4 * C0:4 * C], 0.03125, None, A.mult, r=xs[1], w=["xt.1"])
+        if t < R - 1:
+            mm(bank(T.pb, 0, 0, C0), T.qa, T.sa, 0, q2, s2, 0, C0, r=["qa", "sa", qm + ".0"], w=["pb0"])
+            signs(".a", 0, C0, 0, 0)
+        quant(q2, s2, C0, C, T.xt, r=["xt.1"], w=[qm + ".1"])
+        if t < R - 1:
+            vn = T["vh%d" % (t + 1)]
+            act(vn[:, 0:4 * C], T.x32[:], F.Copy, scale=0.015625, r=xs[0] + xs[1], w=["vh%d.0" % (t + 1), "vh%d.1" % (t + 1)])
+        if t == 0:
+            for k in (5, 6):
+                lo = 48 if k == 5 else 0
+                act(T.tb[:, 4 * (TOFF[k] + lo):4 * (TOFF[k] + 128)], T.zr[:, 0:4 * (128 - lo)], F.Copy, r=["zr"], w=["tb%d.%d" % (k, j) for j in four])
+    q, s = T.q3, T.s3
+    for h, (a, b) in enumerate(CH):
+        mm(bank(T.pa, h, 0, b - a), T.qv, T.sv, 0, q, s, a, b, r=["qv", "q3.%d" % h], w=["pa%d" % h])
+        dma("sp", T.oc[:, 4 * a:4 * b], q[:, a:b].bitcast(dt.uint8), r=["q3.%d" % h])
+        act(T.ys[:, a:b], bank(T.pa, h, 0, b - a), F.Copy, w=["pa%d" % h, "ys%d" % h])
+        dma("act", T.y[:, a:b], T.ys[:, a:b], r=["ys%d" % h])
+    for k in four:
+        dma("sp", T.osc[4 * k:4 * k + 4, :], s[32 * k:32 * k + 4, 0:C], r=["q3.0", "q3.1"])
+    tt(T.dk[:, 1:E], T.ks[:, 1:E], T.ks[:, 0:E - 1], A.subtract, r=["ks"], w=["dk"])
+    scan(T.ls[:], T.dk[:], T.i4[:, 0:E], A.add, A.min, r=["dk", "dk0", "i4"], w=["ls"])
+    ts(T.lr[:], T.ls[:, 0:E].indirect(T.pos[:, 0:NB]), 0.25, None, A.mult, r=["ls", "pos"], w=["lr"])
+    dma("sp", T.lv[:], T.lr[0:128:16, :], r=["lr"])
+    for sname, v in cnt.items():
+        g.wait_ge(T.sem[sname], v)

@@ -4,18 +4,21 @@ A = AluOpType
 F = ActivationFunctionType
 C, H, E, R = 320, 96, 416, 3
 C0 = 192
-NB, AB, EB = 26, 11, 18
-PARTS = (".a", ".b", ".l")
-MUL = (5.0, 41.0, 3281.0)
-WC = 1640.0
-CEN = (0.0, 0.0, 5380000.0 - 3282.0 * WC)
-NT = 496
+PIECES = ((0, 64), (64, 128), (128, C0), (C0, C))
+G3 = 288
+EP = C + 128
+NB, AB, EB = 26, 11, 19
+RADIX, HIGH = 36.0, 4096.0
+STEP = (0.0, 1.0, 0.5)
+NONE1, NONE2 = -34.0, -1200.0
 BIG = 11010048.0
-BIGV = 2048.0
-TILES = (((0, 23, 24, 25), 416), ((7, 8, 9, 10), 160), ((11, 12, 13, 14), 224), ((15, 16, 17, 18), 288),
-         ((19, 20, 21, 22), 352), ((3, 4, 5, 6), 128), ((1, 2), 128))
+BIGV = 512.0
+SPLIT = 402653184.0
+MID = E // 2
+TILES = (((0, 25, 24, 23), 416), ((1, 2), 128), ((11, 12, 13, 14), 224), ((15, 16, 17, 18), 288),
+         ((19, 20, 21, 22), 352), ((3, 4, 5, 6), 128), ((7, 8, 9, 10), 160))
 TD, DC = 0, 23
-LATE = (None, (3, 18, 19, 20, 21, 22, 4, 5, 6, 1, 2), (3, 4, 23, 18, 19, 20, 21, 22, 5, 6, 1, 2))
+TF = 6
 TOFF = [sum(w for _, w in TILES[:k]) for k in range(len(TILES) + 1)]
 Q4, U8, BF, F16, F32, I32, U16 = "float8_e4m3fn_x4", "uint8", "bfloat16", "float16", "float32", "int32", "uint16"
 
@@ -28,20 +31,22 @@ SCRATCH = {
     "xt": _sb(4 * C, BF), "x32": _sb(4 * C, BF), "ut": _sb(512, BF), "vt": _sb(512, BF),
     "qw": _sb(512, Q4), "sw": _sb(512, U8), "qu": _sb(128, Q4), "su": _sb(128, U8),
     "qa": _sb(128, Q4), "sa": _sb(128, U8), "qb": _sb(128, Q4), "sb": _sb(128, U8), "qv": _sb(128, Q4), "sv": _sb(128, U8),
-    "et": _sb(2048, BF), "qe": _sb(512, Q4), "se": _sb(512, U8), "ct": _sb(1536, BF), "qc": _sb(384, Q4), "sc": _sb(384, U8),
-    "tr": _sb(512, BF), "qr": _sb(128, Q4), "sr": _sb(128, U8),
-    "i4": _sb(528, F32), "jm": _sb(E, BF), "pi": _sb(8, I32), "ci": _sb(8, I32), "cf": _sb(8, F32),
-    "cj": _sb(32, F32), "cv": _sb(32, F32), "cw": _sb(32, I32), "ob": _sb(32, U16),
-    "col": _sb(8, F32), "vv": _sb(16, F32), "d0a": _sb(E, BF), "d0b": _sb(E, BF), "d0k": _sb(E, BF), "d0v": _sb(C, BF),
-    "tie": _sb(E, BF), "zr": _sb(512, BF), "oab": _sb(16, U16), "od": _sb(32, U16),
-    "xo": _sb(4 * NT, BF), "qo": _sb(NT, Q4), "so": _sb(NT, U8), "oi": _sb(32, U16), "tab": _sb(NT, F32), "gt": _sb(E, F32),
-    "ab": _sb(E, BF), "k2b": _sb(E, BF), "k2f": _sb(E, F16), "wb": _sb(E + 16, BF), "wf": _sb(E + 16, F16),
-    "mb": _sb(E, BF), "mh": _sb(E, F16), "mf": _sb(E, F32), "kb": _sb(E, BF), "kh": _sb(E, F16), "kf": _sb(E, F32),
-    "kth": _sb(E, F16), "ktf": _sb(E, F32), "jk": _sb(3 * E, F16),
+    "one": _sb(516, BF), "et": _sb(516, BF), "qe": _sb(512, Q4), "se": _sb(512, U8),
+    "ct": _sb(1024, BF), "qc": _sb(256, Q4), "sc": _sb(256, U8), "tp": _sb(512, BF), "qp": _sb(128, Q4), "sp": _sb(128, U8),
+    "kt": _sb(2048, BF), "qk": _sb(512, Q4), "sk8": _sb(512, U8),
+    "pi": _sb(8, I32), "ci": _sb(8, I32), "cf": _sb(8, F32), "jm": _sb(80, BF), "df": _sb(48, BF), "ta": _sb(48, BF),
+    "tc": _sb(48, BF), "tab": _sb(64, BF), "col": _sb(12, F32), "ic": _sb(E, BF), "zr": _sb(512, BF),
+    "oab": _sb(16, U16), "orr": _sb(32, U16), "od": _sb(32, U16), "og": _sb(32, U16), "op": _sb(32, U16), "o2": _sb(32, U16),
+    "d0k": _sb(E, BF), "d0h": _sb(MID, BF), "d0v": _sb(C, BF), "tie1": _sb(E, BF), "tie2": _sb(E, F32),
+    "ab": _sb(E, BF), "a2": _sb(E, BF), "wb": _sb(E + 16, BF), "mb": _sb(E, BF), "dg": _sb(4 * EP, BF),
+    "qd1": _sb(EP, Q4), "sd1": _sb(EP, U8), "qd2": _sb(EP, Q4), "sd2": _sb(EP, U8),
+    "oh": _sb(E, BF), "pre": _sb(E, F16), "sel": _sb(E, F16), "hl": _sb(2 * E, BF), "qh": _sb(MID, Q4), "sh": _sb(MID, U8),
+    "junk": _sb(E, BF), "acc": _sb(8, F32), "a8": _sb(H, BF), "b4": _sb(H, BF), "d1k": _sb(E, F32),
+    "kt1": _sb(E, F16), "kt2": _sb(E, F32), "jk": _sb(3 * E, F16),
     "sk": _sb(E, F32), "kw": _sb(32, F32), "rw": _sb(32, F32), "rc": _sb(32, F32), "dd": _sb(32, F32),
-    "tb": _sb(4 * TOFF[-1], BF), "qt": _sb(TOFF[-1], Q4), "st": _sb(TOFF[-1], U8),
-    "pos": _sb(32, U16), "onm": _sb(40, U16), "ordr": _sb(E, F32), "gn": _sb(C, F32), "gm": _sb(C, F16),
-    "sn": _sb(C, F32), "sm": _sb(C, F16), "ov": _sb(160, U16),
+    "tb": _sb(4 * TOFF[-1], BF), "qt": _sb(TOFF[-1] + 256, Q4), "st": _sb(TOFF[-1] + 256, U8),
+    "pos": _sb(32, U16), "onm": _sb(40, U16), "ordr": _sb(E, BF), "gn": _sb(C, BF), "gm": _sb(C, BF),
+    "sn": _sb(C, F16), "sm": _sb(C, F16), "ov": _sb(160, U16),
     "g1": _sb(4 * C, BF), "g3": _sb(4 * C, BF), "g2": _sb(4 * C, BF), "zt": _sb(4 * C, BF), "qz": _sb(C, Q4), "sz": _sb(C, U8),
     "ow": _sb(32, U16), "ks": _sb(E, F32), "dk": _sb(E, F32), "ls": _sb(E, F32), "lr": _sb(E, F32), "ys": _sb(C, F32),
     "pa": ("psum", [128, 2048], F32), "pb": ("psum", [128, 2048], F32),
@@ -51,7 +56,7 @@ for _t in range(R):
 for _t in range(R + 1):
     SCRATCH["q%d" % _t] = _sb(E, Q4)
     SCRATCH["s%d" % _t] = _sb(E, U8)
-SEMAPHORES = ["pe", "dve", "act", "gp", "snd", "arr0", "arr1", "arr2"] + ["d%d" % k for k in range(20)]
+SEMAPHORES = ["pe", "dve", "act", "gp", "snd", "arr0", "arr1", "arr2"] + ["d%d" % k for k in range(30)]
 
 
 def rank_program(g, core, T, topo):
@@ -124,20 +129,22 @@ def rank_program(g, core, T, topo):
     def ms(out, c, w=()):
         op("dve", lambda: V.memset(out, c), (), w)
 
-    def scan(out, d0, d1, o0, o1, r=(), w=()):
-        op("dve", lambda: V.tensor_tensor_scan(out, d0, d1, 0.0, o0, o1), r, w)
+    def scan(out, d0, d1, o0, o1, r=(), w=(), first=0.0):
+        op("dve", lambda: V.tensor_tensor_scan(out, d0, d1, first, o0, o1), r, w)
 
-    def quant(q, s, a, b, tile, r=(), w=()):
-        op("dve", lambda: V.quantize_mx(q[:, a:b], s[:, a:b], tile[:, 4 * a:4 * b]), r, w)
+    def quant(q, s, a, b, tile, r=(), w=(), at=None):
+        lo = 4 * a if at is None else at
+        op("dve", lambda: V.quantize_mx(q[:, a:b], s[:, a:b], tile[:, lo:lo + 4 * (b - a)]), r, w)
 
     def act(out, in_, func, r=(), w=(), **kw):
         op("act", lambda: S.activation(out, in_, func, **kw), r, w)
 
-    def mm(out, q, s, a, q2, s2, b0, b1, r=(), w=(), start=True, stop=True):
-        op("pe", lambda: P.matmul_mx(out, q[:, a:a + 128], s[:, a:a + 128], q2[:, b0:b1], s2[:, b0:b1], start, stop), r, w)
+    def bank(k, a, b):
+        return (T.pa, T.pb)[k // 4][:, 512 * (k % 4) + a:512 * (k % 4) + b]
 
-    def bank(p, k, a, b):
-        return p[:, 512 * k + a:512 * k + b]
+    def mm(k, q, s, a, q2, s2, b0, b1, r=(), start=True, stop=True):
+        op("pe", lambda: P.matmul_mx(bank(k, 0, b1 - b0), q[:, a:a + 128], s[:, a:a + 128], q2[:, b0:b1], s2[:, b0:b1], start, stop),
+           r, ["p%d" % k])
 
     def iota(out, pat, base, cm, w, small=True):
         if small:
@@ -156,270 +163,325 @@ def rank_program(g, core, T, topo):
         cnt["snd"] = cnt.get("snd", 0) + 2 * neng
         lastw["q%d.h" % t] = ("arr%d" % t, 2 * neng)
 
-    def weave(*lists):
-        for k in range(max(len(x) for x in lists)):
-            for x in lists:
-                if k < len(x):
-                    x[k]()
+    def spread(out, n, k, scale, w):
+        act(out[:, 0:n], T.tab[:, 16 * k:16 * k + 16].indirect(T.orr[:, 0:n // 16]), F.Copy, scale=scale, r=["tab%d" % (k // 3), "orr"], w=w)
+
+    def block(k, lst):
+        act(T.ct[:, 512 * k:512 * k + 512], T.jm[:, 0:16].indirect(T[lst][:]), F.Copy, r=["jm0", lst], w=["ct%d" % k])
+
+    def ties(t):
+        tie = T["tie%d" % t]
+        spread(tie, E, 3, STEP[t], ["tie%d" % t])
+        for a, c in (((E - 2, NONE1),), ((E - 6, NONE1), (E - 4, NONE2), (E - 2, NONE2 + HIGH * NONE1)))[t - 1]:
+            act(tie[:, a:a + 2], tie[:, a:a + 2], F.Identity, bias=c, w=["tie%d" % t])
+
+    def zeros(k):
+        quant(T.qt, T.st, TOFF[-1] + 128 * k, TOFF[-1] + 128 * k + 128, T.zr, r=["zr"], w=["qt.z%d" % k], at=0)
 
     CH = ((0, C0), (C0, C))
-    cf, col = T.cf, T.col
+    PART = {"a": (0, C0), "b": (C0, C), "l": (C, E)}
+    cf, col, jm, dg = T.cf, T.col, T.jm, T.dg
     four = range(4)
-    x0 = ["xt.0.%d" % b for b in four]
+    x0, x1 = (["xt.%d.%d" % (h, b) for b in four] for h in range(2))
+    xs = [["x32.%d.%d" % (h, j) for j in four] for h in range(2)]
+    sks = ["sk.a", "sk.b", "sk.l"]
+    tieds = ["tied.a", "tied.b", "tied.l"]
     dma("sp", T.xt[:, 0:512], T.x[:, 0:512], w=x0)
     dma("act", T.ut[:], T.u[:], w=["ut"])
-    dma("sp", T.xt[:, 512:4 * C], T.x[:, 512:4 * C], w=["xt.1"])
-    dma("sp", T.qw[:].bitcast(dt.uint8), T.wc[:], r=["xt.1"], w=["qw"])
+    dma("sp", T.xt[:, 512:4 * C], T.x[:, 512:4 * C], w=x1)
+    dma("sp", T.qw[:].bitcast(dt.uint8), T.wc[:], r=x1, w=["qw"])
     dma("sp", T.sw[:], T.ws[:], w=["sw"])
     dma("sp", T.vt[:], T.v[:], w=["vt"])
-    iota(T.pi[:, 0:4], [[0, 2], [1, 2]], 0, 1, ["pi"], False)
-    iota(T.jm[:], [[0, NB], [1, 16]], 0, 0, ["jm"])
-    iota(T.i4[:], [[4, 528]], 0, 0, ["i4"])
-    ms(T.xo[:], 0.0, w=["xo0", "xo1"])
-    ts(T.ci[:, 0:2], T.pi[:, 0:2], 15, None, A.bitwise_and, r=["pi"], w=["ci0"])
-    ts(T.ci[:, 2:3], T.pi[:, 0:1], 2, 3, A.arith_shift_right, A.bitwise_and, r=["pi"], w=["ci1"])
-    ts(T.ci[:, 3:4], T.pi[:, 0:1], 3, None, A.bitwise_and, r=["pi"], w=["ci2"])
+    iota(T.pi[:, 0:2], [[2, 2]], 0, 1, ["pi"], False)
+    iota(jm[:, 0:16], [[1, 16]], 0, 0, ["jm0"])
+    iota(jm[:, 48:80], [[1, 8], [0, 4]], 0, 0, ["jm3"])
+    iota(jm[:, 16:32], [[0, 2], [1, 8]], 0, 0, ["jm1"])
+    iota(jm[:, 32:48], [[0, 4], [1, 4]], 0, 0, ["jm2"])
+    iota(T.ic[:], [[1, E]], -MID, 0, ["ic"])
     ms(T.zr[:], 0.0, w=["zr"])
-    cp(cf[:, 0:4], T.ci[:, 0:4], r=["ci0", "ci1", "ci2"], w=["cf"])
-    ts(T.oab[:, 0:8], T.jm[:, 0:8], 16.0, None, A.mult, r=["jm"], w=["oa"])
-    ts(T.oab[:, 8:16], T.jm[:, 0:8], 16.0, 1.0, A.mult, A.add, r=["jm"], w=["ob"])
-    ts(T.d0a[:], T.jm[:], cf[:, 0:1], -2.0 * BIG, A.is_equal, A.mult, r=["jm", "cf"], w=["d0a"])
-    ts(T.d0b[:], T.jm[:], cf[:, 1:2], BIG, A.is_equal, A.mult, r=["jm", "cf"], w=["d0b"])
-    act(T.tr[:], T.zr[:], F.Copy, r=["zr"], w=["tr0", "tr1"])
-    act(T.ct[:, 0:512], T.zr[:], F.Identity, bias=1.0, r=["zr"], w=["ct0"])
+    for k, (sh, m) in enumerate(((0, 15), (1, 7), (2, 3), (0, 3), (4, 7))):
+        ts(T.ci[:, k:k + 1], T.pi[:, 0:1], sh, m, A.arith_shift_right, A.bitwise_and, r=["pi"], w=["ci%d" % k])
+    ts(T.ci[:, 5:6], T.pi[:, 1:2], 2, 1, A.arith_shift_right, A.bitwise_and, r=["pi"], w=["ci5"])
+    ts(T.oab[:, 0:8], jm[:, 0:8], 16.0, None, A.mult, r=["jm0"], w=["oa"])
+    cp(cf[:, 0:6], T.ci[:, 0:6], r=["ci%d" % k for k in range(6)], w=["cf"])
+    ts(T.oab[:, 8:16], jm[:, 0:8], 16.0, 1.0, A.mult, A.add, r=["jm0"], w=["ob"])
+    ms(T.wb[:, E:E + 16], 0.0, w=["wb.p"])
+    ts(T.og[:], jm[:, 48:80], cf[:, 4:5], None, A.is_equal, r=["jm3", "cf"], w=["og"])
+    ts(col[:, 7:8], cf[:, 0:1], -7.5, None, A.add, r=["cf"], w=["col7"])
+    ts(T.orr[:], T.zr[:, 0:32], cf[:, 0:1], None, A.add, r=["zr", "cf"], w=["orr"])
+    ts(T.op[:], T.og[:], cf[:, 5:6], None, A.subtract, r=["og", "cf"], w=["op"])
+    ts(col[:, 4:7], jm[:, 0:3], -0.25, col[:, 7:8], A.mult, A.add, r=["jm0", "col7"], w=["col4"])
+    for k in range(3):
+        ts(T.df[:, 16 * k:16 * k + 16], jm[:, 16 * k:16 * k + 16], cf[:, k:k + 1], None, A.subtract, r=["jm%d" % k, "cf"], w=["df%d" % k])
+    dfs = ["df%d" % k for k in range(3)]
+    ms(T.one[:], 1.0, w=["one"])
+    ts(T.ta[:], T.df[:], 0.0, -2.0, A.is_equal, A.mult, r=dfs, w=["ta"])
+    ts(T.tc[:], T.df[:], 1.0, None, A.is_equal, r=dfs, w=["tc"])
+    ts(col[:, 9:10], cf[:, 3:4], NB - DC + 0.5, 1.0, A.is_lt, A.add, r=["cf"], w=["col9"])
+    tt(T.tab[:, 0:48], T.ta[:], T.tc[:], A.add, r=["ta", "tc"], w=["tab0"])
+    ts(T.o2[:], T.og[:], col[:, 9:10], None, A.mult, r=["og", "col9"], w=["o2"])
+    act(T.tp[:], jm[:, 0:16].indirect(T.op[:]), F.Copy, r=["jm0", "op"], w=["tp"])
     quant(T.q0, T.s0, 0, 128, T.xt, r=x0, w=["q0.0"])
     send(0)
-    keep(T.ct[:, 0:512], T.ct[:, 0:512], [[-16, 8], [0, 64]], A.is_ge, 0, 1, [], ["ct0"])
-    keep(T.ct[:, 0:512], T.ct[:, 0:512], [[16, 8], [0, 64]], A.is_ge, 15, -1, [], ["ct0"])
-    keep(T.tr[:, 0:512:4], T.ct[:, 0:512:4], [[1, 128]], A.is_gt, 0, -1, ["ct0"], ["tr0"])
-    keep(T.tr[:, 1:512:4], T.ct[:, 0:512:4], [[-1, 128]], A.is_ge, 0, 1, ["ct0"], ["tr1"])
     quant(T.qu, T.su, 0, 128, T.ut, r=["ut"], w=["qu"])
-    tt(T.d0k[:], T.d0a[:], T.d0b[:], A.add, r=["d0a", "d0b"], w=["d0k"])
+    quant(T.q0, T.s0, 128, C, T.xt, r=x1, w=["q0.1"])
     for q, s, lo, tok in ((T.qa, T.sa, 0, "a"), (T.qb, T.sb, 8, "b")):
         cp(q[:, 0:128].bitcast(dt.uint32), T.qu[:, 0:128].bitcast(dt.uint32).indirect(T.oab[:, lo:lo + 8]), r=["qu", "o" + tok], w=["q" + tok])
         act(s[:, 0:128], T.su[:, 0:128].indirect(T.oab[:, lo:lo + 8]), F.Copy, r=["qu", "o" + tok], w=["s" + tok])
-    quant(T.q0, T.s0, 128, C, T.xt, r=["xt.1"], w=["q0.1"])
-    for b in four:
-        act(T.et[:, 512 * b:512 * (b + 1)], T.zr[:], F.Copy, r=["zr"], w=["et%d" % b])
-        keep(T.et[:, 512 * b + b:512 * (b + 1):4], T.ct[:, 0:512:4], [[1, 128]], A.is_equal, 0, -1, ["ct0"], ["et%d" % b])
-    act(T.vh0[:, 0:4 * C], T.xt[:], F.Copy, scale=0.5, r=x0 + ["xt.1"], w=["vh0.0", "vh0.1"])
-    act(T.x32[:], T.xt[:], F.Copy, scale=32.0, r=x0 + ["xt.1"], w=["x32.%d.%d" % (h, b) for h in range(2) for b in four])
-
-    def hold_pattern():
-        tt(T.vv[:, 4:8], T.vv[:, 8:12], T.vv[:, 12:16], A.add, r=["vv1", "vv2"], w=["vv0"])
-        for b in four:
-            act(T.d0v[:, b:C:4], T.jm[:, 0:C // 4], F.Identity, scale=0.0, bias=T.vv[:, 4 + b:5 + b], r=["jm", "vv0"], w=["d0v%d" % b])
+    keep(T.et[:], T.one[:], [[1, 516]], A.is_equal, -3, -4, ["one"], ["et"])
+    for k, wt in ((0, RADIX), (1, 1.0), (3, HIGH)):
+        x = T.kt[:, 512 * k:512 * k + 512]
+        iota(x, [[0, 128], [-2 * int(wt), 4]], 4 * int(wt), 0, ["kt%d" % k])
+        keep(x, x, [[1, 128], [0, 4]], A.is_equal, 0, -1, [], ["kt%d" % k])
+        if k == 0:
+            keep(T.kt[:, 2:512:4], T.one[:, 0:128], [[1, 128]], A.is_equal, 0, -1, ["one"], ["kt0"])
+    iota(dg[:, 2:4 * E:4], [[0, E]], 0, 0, ["dg2a", "dg2b", "dg2l"])
+    iota(dg[:, 4 * E:4 * EP], [[0, 4 * (EP - E)]], 0, 0, ["dgp"])
+    spread(T.d0h, MID, 1, BIG, ["d0h"])
+    act(T.vh0[:, 0:4 * C], T.xt[:], F.Copy, scale=0.5, r=x0 + x1, w=["vh0.0", "vh0.1"])
+    for k, (cs, wd) in enumerate(TILES):
+        lo = 0 if len(cs) < 4 else 16 * min(c for c in cs if c)
+        dma("sp", T.tb[:, 4 * (TOFF[k] + lo):4 * (TOFF[k] + wd)], T.zr[:, 0:4 * (wd - lo)], r=["zr", "vt"],
+            w=["tb%d.%d" % (k, j) for j in four] + ["in.a", "in.b"] * (k == TD))
+    block(0, "og")
 
     spare.extend([
-        lambda: ts(col[:, 0:1], cf[:, 0:1], 15.0, BIG, A.is_lt, A.mult, r=["cf"], w=["col0"]),
-        lambda: ts(T.cj[:, 0:31], T.i4[:, 0:31], 4.0, cf[:, 0:1], A.mult, A.add, r=["i4", "cf"], w=["cj"]),
-        lambda: ms(T.wb[:, E:E + 16], -1.0, w=["wb.p"]),
-        lambda: ts(T.cv[:, 0:31], T.cj[:, 0:31], 12.5, 1.0 / NB, A.add, A.mult, r=["cj"], w=["cv"]),
-        lambda: cp(T.cw[:, 0:31], T.cv[:, 0:31], r=["cv"], w=["cw"]),
-        lambda: ts(T.cv[:, 0:31], T.cw[:, 0:31], -1.0 * NB, NB - 1.0, A.mult, A.add, r=["cw"], w=["cv"]),
-        lambda: tt(T.cj[:, 0:31], T.cj[:, 0:31], T.cv[:, 0:31], A.add, r=["cv"], w=["cj"]),
-        lambda: cp(T.ob[:, 0:31], T.cj[:, 0:31], r=["cj"], w=["obk"]),
-        lambda: ts(T.vv[:, 0:4], T.jm[:, 0:4], cf[:, 2:3], None, A.subtract, r=["cf", "jm"], w=["vv0"]),
-        lambda: ts(T.vv[:, 8:12], T.vv[:, 0:4], 0.0, -2.0 * BIGV, A.is_equal, A.mult, r=["vv0"], w=["vv1"]),
-        lambda: ts(T.vv[:, 12:16], T.vv[:, 0:4], 1.0, BIGV, A.is_equal, A.mult, r=["vv0"], w=["vv2"]),
-        hold_pattern,
-        lambda: ts(col[:, 2:3], cf[:, 2:3], 3.0, -BIGV, A.is_lt, A.mult, r=["cf"], w=["col2"]),
-        lambda: tt(col[:, 3:4], col[:, 2:3], cf[:, 3:4], A.add, r=["col2", "cf"], w=["col3"]),
-        lambda: ts(T.od[:, 0:NB], T.i4[:, 0:NB], 0.25, None, A.mult, r=["i4"], w=["od"]),
-        lambda: ms(T.wf[:, E:E + 16], -1.0 - WC, w=["wf.p"]),
+        lambda: ts(col[:, 0:2], T.df[:, 15:32:16], 0.0, BIG, A.is_gt, A.mult, r=dfs, w=["col0"]),
+        lambda: ts(col[:, 2:3], T.df[:, 47:48], 0.0, -4.0 * BIGV, A.is_gt, A.mult, r=dfs, w=["col2"]),
+        lambda: ts(T.tab[:, 48:64], T.df[:, 0:16], 0.0, None, A.is_gt, r=dfs, w=["tab1"]),
+        lambda: ts(col[:, 3:4], col[:, 2:3], cf[:, 3:4], 4.0 * MID, A.add, A.add, r=["col2", "cf"], w=["col3"]),
+        lambda: ts(T.od[:, 0:NB], T.ic[:, 0:NB], 1.0 * MID, None, A.add, r=["ic"], w=["od"]),
         lambda: ms(T.rw[:, 0:1], 0.0, w=["rw0"]),
         lambda: ms(T.dk[:, 0:1], 0.0, w=["dk0"]),
-        lambda: ts(col[:, 1:2], col[:, 0:1], 432.0, None, A.add, r=["col0"], w=["col1"]),
+        lambda: ts(col[:, 8:9], T.ta[:, 0:1], BIG, -16.0 - E, A.mult, A.add, r=["ta"], w=["col8"]),
+        lambda: ts(col[:, 10:12], jm[:, 0:3:2], -1.0, col[:, 0:1], A.mult, A.add, r=["jm0", "col0"], w=["col10"]),
+        lambda: ts(col[:, 10:12], col[:, 10:12], col[:, 8:9], 16.0 + E, A.add, A.add, r=["col8"], w=["col10"]),
     ])
 
-    for t in range(R):
-        d = 2 ** t
-        dc = DC + (t == 2)
-        q, s, vh = T["q%d" % t], T["s%d" % t], T["vh%d" % t]
-        qn = "q%d" % t
-        k2, k2n = (T.k2f, "k2f") if t == 2 else (T.k2b, "k2b")
-        wv, wn = (T.wf, "wf") if t == 2 else (T.wb, "wb")
-        kn = "bhf"[t]
-        mw, kk = T["m" + kn], T["k" + kn]
-        ka, kan = (T.kb, "kb") if t == 0 else (T.kf, "kf")
-
-        def signs(part, a, b, pk, o):
-            ts(T.ab[:, a:b], bank(T.pb, pk, o, o + b - a), 0.0, None, A.is_gt, w=["pb%d" % pk, "ab" + part])
-
-        def chain(part, wa, wb, c0, c1, ws):
-            a, b = 16 * c0, 16 * c1
-            ws = [wn + p for p in ws]
-            steps = [
-                lambda: tt(wv[:, wa:wb], k2[:, wa:wb], T.ab[:, wa:wb], A.add, r=[k2n + part, "ab" + part], w=[wn + part]),
-                lambda: ts(mw[:, a:b], wv[:, a:b], MUL[t], 1.0 - CEN[t], A.mult, A.add, r=ws, w=["m" + kn + part]),
-                lambda: tt(kk[:, a:b], mw[:, a:b], wv[:, a + d:b + d], A.add, r=ws + ["m" + kn + part], w=["k" + kn + part]),
-                lambda: scan(T.sk[:, a:b], T.d0k[:, a:b], kk[:, a:b], A.add, A.max, r=["d0k", "k" + kn + part], w=["sk" + part])]
-            if t == 1:
-                steps.append(lambda: cp(ka[:, a:b], kk[:, a:b], r=["k" + kn + part], w=[kan + part]))
-            if t:
-                steps.append(lambda: ts(T.kw[:, c0:c1], T.sk[:, a + 15:b:16], col[:, 0:1], 0.5, A.subtract, A.add, r=["sk" + part, "col0"], w=["kw" + part]))
-            return steps
-
-        def compare(c):
-            k = [c in cs for cs, _ in TILES].index(True)
-            j = TILES[k][0].index(c)
-            o = 4 * TOFF[k] + j
-            row, rn = (kk, "k" + kn) if c >= dc else (ka, kan)
-            rs = [rn + p for p, lo in zip(PARTS, (0, AB, EB)) if c > lo] + ["kw.l" if c >= EB else "kw.b" if c >= AB else "kw.a"]
-            out = T.tb[:, o:o + 64 * c - j:4]
-            if c >= dc:
-                ts(out, row[:, 0:16 * c], T.kw[:, c:c + 1], 0.5, A.is_lt, A.subtract, r=rs, w=["tb%d.%d" % (k, j)])
-            else:
-                act(out, row[:, 0:16 * c], F.Sign, scale=-1.0, bias=T.kw[:, c:c + 1], accum_out=T.rw[:, c:c + 1],
-                    r=rs, w=["tb%d.%d" % (k, j), "rw%d" % c])
-
-        def rowsum(c):
-            j = c - DC + 1
-            o = 4 * TOFF[TD] + j
-            scan(T.jk[:, E * j - 16 * c:E * j], T.tb[:, o:o + 64 * c - j:4], T.zr[:, 0:16 * c], A.add, A.add,
-                 r=["tb%d.%d" % (TD, j), "zr"], w=["jk%d" % j])
-
-        def tied(part, c0, c1):
-            a, b = 16 * c0, 16 * c1
-            tt(T["kt" + kn][:, a:b], kk[:, a:b], T.tie[:, a:b], A.add,
-               r=["k" + kn + p for p in (PARTS[:2] if part == ".e" else PARTS[2:])] + ["tie"], w=["kt" + kn + part])
-
-        def inside(part, c0, c1, w0, tok):
-            a, b = 16 * c0, 16 * c1
-            o = 4 * TOFF[TD]
-            tt(T.tb[:, o + 4 * a:o + 4 * b:4], T.kw[:, w0:c1].indirect(T.od[:, c0 - w0:c1 - w0]), T["kt" + kn][:, a:b], A.is_gt,
-               r=["kw.a", "kw.b", "od", "kt" + kn + part] + ["kw.l"] * (part == ".l"), w=[tok])
-
-        def fold(k):
-            wd = TILES[k][1]
-            quant(T.qt, T.st, TOFF[k], TOFF[k] + wd, T.tb, r=["tb%d.%d" % (k, j) for j in four] + (["tbe"] if k == TD else []), w=["qt%d" % k])
-
-        def total(k):
-            wd = TILES[k][1]
-            mm(bank(T.pb, 0, 0, wd), T.qc, T.sc, 128 * t if k == TD else 0, T.qt, T.st, TOFF[k], TOFF[k] + wd,
-               r=["qc", "qt%d" % k], w=["pb0"], start=k == 0, stop=k == len(TILES) - 1)
-
-        sks = ["sk" + p for p in PARTS]
-        late = chain(".l", C, E, EB, NB, [".b", ".l", ".p"])
-        if t == 0:
-            mm(bank(T.pb, 0, 0, C), T.qa, T.sa, 0, q, s, 0, C, r=["qa", "sa", qn + ".0", qn + ".1"], w=["pb0"])
-            mm(bank(T.pb, 1, 0, C), T.qb, T.sb, 0, q, s, 0, C, r=["qb", "sb", qn + ".0", qn + ".1"], w=["pb1"])
-            gap(3)
-            ts(k2[:, 0:C], bank(T.pb, 0, 0, C), 0.0, 2.0, A.is_gt, A.mult, w=["pb0", k2n + ".a", k2n + ".b"])
-            signs(".b", 0, C, 1, 0)
-            weave([gap] * 4, chain(".b", 0, C, 0, EB, [".b"]))
-            mm(bank(T.pb, 2, 0, 128), T.qa, T.sa, 0, q, s, E - 128, E, r=["qa", "sa", qn + ".1", qn + ".h"], w=["pb2"])
-            mm(bank(T.pb, 3, 0, 128), T.qb, T.sb, 0, q, s, E - 128, E, r=["qb", "sb", qn + ".1", qn + ".h"], w=["pb3"])
-            ts(T.tie[:], T.jm[:], cf[:, 0:1], None, A.is_gt, r=["jm", "cf"], w=["tie"])
-            ts(k2[:, C:E], bank(T.pb, 2, 128 - H, 128), 0.0, 2.0, A.is_gt, A.mult, w=["pb2", k2n + ".l"])
-            signs(".l", C, E, 3, 128 - H)
-            weave([gap] * 4, late)
-            for n in ("kb", "sk"):
-                lastw[n + ".a"] = lastw[n + ".b"]
-            gap()
-            ts(T.dd[:, 0:NB], T.sk[:, 15:E:16], col[:, 0:1], 4.0 * NB, A.subtract, A.mult, r=sks + ["col0"], w=["dd"])
-            gap()
-            tt(T.kw[:, 0:NB], T.dd[:, 0:NB], T.i4[:, 0:NB], A.add, r=["dd", "i4"], w=["kw" + p for p in PARTS])
-            gap()
-            tt(T.xo[:, 0:4 * NT:4], T.kw[:, 0:NB].indirect(T.ob[:, 0:31]), T.i4[:, NB - 1:NB - 1 + NT], A.is_equal,
-               r=["kw.a", "obk", "i4"], w=["xo0"])
-            ts(T.oi[:, 0:NB], T.kw[:, 0:NB], 0.25, NB - 1.0, A.mult, A.subtract, r=["kw.a"], w=["oi"])
-            cp(T.xo[:, 5:4 * NT:4], T.xo[:, 0:4 * NT - 4:4], r=["xo0"], w=["xo1"])
-            quant(T.qr, T.sr, 0, 128, T.tr, r=["tr0", "tr1"], w=["qr"])
-            quant(T.qo, T.so, 0, NT, T.xo, r=["xo0", "xo1"], w=["qo"])
-            mm(bank(T.pb, 0, 0, NT), T.qr, T.sr, 0, T.qo, T.so, 0, NT, r=["qr", "qo"], w=["pb0"])
-            act(T.ct[:, 512:1024], T.ct[:, 0:512], F.Copy, scale=2.0, r=["ct0"], w=["ct1"])
-            for b in four:
-                act(T.ct[:, 1024 + b:1536:4], T.ct[:, 0:512:4], F.Copy, scale=1.0 if b == 1 else 2.0, r=["ct0"], w=["ct2%d" % b])
-            quant(T.qv, T.sv, 0, 128, T.vt, r=["vt"], w=["qv"])
-            gap(2)
-            scan(T.tab[:], bank(T.pb, 0, 0, NT), T.zr[:, 0:NT], A.add, A.add, r=["zr"], w=["pb0", "tab"])
-            act(T.gt[:], T.tab[:, 0:NT].indirect(T.oi[:, 0:NB]), F.Copy, r=["tab", "oi"], w=["gt"])
-            quant(T.qe, T.se, 0, 512, T.et, r=["et%d" % b for b in four], w=["qe"])
-            gap(9)
-            scan(T.sk[:], T.d0k[:], T.gt[:], A.add, A.max, r=["d0k", "gt"], w=sks)
-            ts(T.pos[:, 0:NB], T.sk[:, 15:E:16], col[:, 0:1], None, A.subtract, r=["sk.a", "col0"], w=["pos"])
-            ts(T.onm[:, 0:20], T.sk[:, 15:C:16], col[:, 0:1], 1.0, A.subtract, A.subtract, r=["sk.a", "col0"], w=["on"])
+    def classes(part, a, b, k, o, lo, hi):
+        sa, sb = bank(k, o, o + b - a), bank(k + 1, o, o + b - a)
+        ts(T.a2[:, a:b], sa, 0.0, 2.0, A.is_gt, A.mult, r=["p%d" % k], w=["a2" + part])
+        ts(T.ab[:, a:b], sb, 0.0, 0.5, A.is_gt, A.add, r=["p%d" % (k + 1)], w=["ab" + part])
+        if part == "l":
+            ts(T.a8[:], sa, 0.0, -8.0, A.is_le, A.mult, r=["p%d" % k], w=["a8"])
+            ts(T.b4[:], sb, 0.0, 4.0, A.is_gt, A.mult, r=["p%d" % (k + 1)], w=["b4"])
+        gap()
+        tt(T.wb[:, a:b], T.a2[:, a:b], T.ab[:, a:b], A.add, r=["a2" + part, "ab" + part], w=["wb" + part])
+        if part == "l":
+            tt(T.mb[:, a:b], T.a8[:], T.b4[:], A.add, r=["a8", "b4"], w=["mbl"])
         else:
-            mm(bank(T.pb, 1, 0, C - C0), T.qa, T.sa, 0, q, s, C0, C, r=["qa", "sa", qn + ".1"], w=["pb1"])
-            second = chain(".b", C0, C, AB, EB, [".a", ".b"])
-            weave(chain(".a", 0, C0, 0, AB, [".a"]), [lambda: None, lambda: signs(".b", C0, C, 1, 0)] + second[:3])
-            for c in range(7, AB):
-                compare(c)
-            weave(second[3:])
-            for c in range(AB, EB):
-                compare(c)
-            mm(bank(T.pb, 2, 0, 128), T.qa, T.sa, 0, q, s, E - 128, E, r=["qa", "sa", qn + ".1", qn + ".h"], w=["pb2"])
-            tied(".e", 0, EB)
-            signs(".l", C, E, 2, 128 - H)
-            weave([lambda: inside(".e", 0, EB, 0, "tbe"), lambda: fold(1)], late)
-            for c in LATE[t]:
-                compare(c)
-            tied(".l", EB, NB)
-            compare(dc)
-            inside(".l", EB, NB, 16, "tb%d.0" % TD)
-            for c in range(dc + 1, NB):
-                compare(c)
-            if t == 2:
-                fold(2)
-            fold(TD)
-            total(TD)
-            total(1)
-            for k in (2, 3):
-                if k == 3 or t == 1:
-                    fold(k)
-                total(k)
-            for c in range(dc, NB):
-                rowsum(c)
-            fold(4)
-            total(4)
-            ts(T.rc[:, dc:NB], T.jk[:, E * (dc - DC + 1) - 1:3 * E:E], 2.0, col[:, 1:2], A.mult, A.add, r=["jk1", "jk2", "jk3", "col1"], w=["rc1"])
-            for k in (5, 6):
-                fold(k)
-                total(k)
-            ts(T.rc[:, 0:dc], T.rw[:, 0:dc], col[:, 1:2], None, A.add, r=["rw%d" % c for c in range(dc)] + ["col1"], w=["rc0"])
-            scan(T.sk[:], T.d0k[:], bank(T.pb, 0, 0, E), A.add, A.max, r=["d0k"], w=["pb0"] + sks)
-            tt(T.dd[:, 0:NB], T.rc[:, 0:NB], T.sk[:, 15:E:16], A.subtract, r=["rc0", "rc1"] + sks, w=["dd"])
-            ts(T.pos[:, 0:NB], T.dd[:, 0:NB], 0.5, None, A.mult, r=["dd"], w=["pos"])
-            ts(T.onm[:, 0:20], T.dd[:, 0:20], 0.5, 1.0, A.mult, A.subtract, r=["dd"], w=["on"])
-        for b in four:
-            mm(bank(T.pa, b, 0, 128), T.qe, T.se, 128 * b, q, s, E - 128, E, r=["qe", qn + ".1", qn + ".h"], w=["pa%d" % b])
-            act(vh[:, 4 * C + b:4 * E:4], bank(T.pa, b, 128 - H, 128), F.Copy, scale=0.5, w=["pa%d" % b, "vh%d.h%d" % (t, b)])
-        if t == 0:
-            act(T.k2b[:], ka[:], F.Copy, scale=2.0, r=["kb" + p for p in PARTS], w=["k2b" + p for p in PARTS])
-            for k, (cs, wd) in enumerate(TILES):
-                lo = 0 if len(cs) < 4 else 16 * min(c for c in cs if c)
-                if k < 5:
-                    act(T.tb[:, 4 * (TOFF[k] + lo):4 * (TOFF[k] + wd)], T.zr[:, 0:4 * (wd - lo)], F.Copy, r=["zr"],
-                        w=["tb%d.%d" % (k, j) for j in four] + (["tbe"] if k == TD else []))
-        cp(T.ordr[:, 0:E].indirect(T.pos[:, 0:NB]), T.i4[:, 0:E], r=["pos", "i4"], w=["ordr"])
-        act(T.gn[:], T.ordr[:, 0:E].indirect(T.onm[:, 0:20]), F.Copy, r=["ordr", "on"], w=["gn"])
+            gap(2)
+            ts(T.mb[:, a:b], T.wb[:, a:b], 4.0, -10.0, A.mult, A.add, r=["wbo"], w=["mbo"])
+        gap(2)
+        more = ["wbl", "mbl", "wb.p"] * (part == "l")
+        tt(dg[:, 4 * lo:4 * hi:4], T.mb[:, lo:hi], T.wb[:, lo + 1:hi + 1], A.add, r=["wbo", "mbo"] + more, w=["dg0" + part])
+        n = int(part == "l")
+        act(T.junk[:, lo:hi], dg[:, 4 * lo:4 * hi:4], F.Sign, scale=-1.0, bias=col[:, 5:6], accum_out=T.acc[:, n:n + 1],
+            r=["dg0" + part, "col4"], w=["junk" + part, "acc" + part])
+        gap(2)
+        ts(T.oh[:, lo:hi], dg[:, 4 * lo:4 * hi:4], col[:, 4:5], None, A.is_equal, r=["dg0" + part, "col4"], w=["oh" + part])
+
+    mm(0, T.qa, T.sa, 0, T.q0, T.s0, 0, C, r=["qa", "sa", "q0.0", "q0.1"])
+    mm(1, T.qb, T.sb, 0, T.q0, T.s0, 0, C, r=["qb", "sb", "q0.0", "q0.1"])
+    quant(T.qp, T.sp, 0, 128, T.tp, r=["tp"], w=["qp"])
+    classes("o", 0, C, 0, 0, 0, C - 2)
+    mm(2, T.qa, T.sa, 0, T.q0, T.s0, E - 128, E, r=["qa", "sa", "q0.1", "q0.h"])
+    mm(3, T.qb, T.sb, 0, T.q0, T.s0, E - 128, E, r=["qb", "sb", "q0.1", "q0.h"])
+    for b in four:
+        quant(T.qe, T.se, 128 * b, 128 * (b + 1), T.et, r=["et"], w=["qe%d" % b], at=3 - b)
+    ts(T.acc[:, 2:3], T.acc[:, 0:1], 1.0 * E, None, A.add, r=["acco"], w=["acc2"])
+    block(1, "o2")
+    spread(T.d0v, C, 2, BIGV, ["d0v"])
+    classes("l", C, E, 2, 128 - H, C - 2, E)
+    zeros(0)
+    ts(T.acc[:, 3:4], T.acc[:, 1:2], T.acc[:, 2:3], 0.5, A.add, A.mult, r=["accl", "acc2"], w=["acc3"])
+    zeros(1)
+    scan(T.pre[:], T.oh[:], T.oh[:], A.add, A.max, r=["oho", "ohl", "acc3"], w=["pre"], first=T.acc[:, 3:4])
+    ts(T.sel[:, E - 1:E], dg[:, 4 * E - 4:4 * E - 3], col[:, 6:7], T.acc[:, 3:4], A.is_equal, A.mult, r=["dg0l", "col4", "acc3"], w=["sel2"])
+    gap(9)
+    halves = ((0, MID), (MID, E))
+    for h, (a, b) in enumerate(halves):
+        b = min(b, E - 1)
+        tt(T.sel[:, a:b], T.pre[:, a:b], T.oh[:, a:b], A.mult, r=["pre", "oho", "ohl"], w=["sel%d" % h])
+    for h, (a, b) in enumerate(halves):
+        ts(T.hl[:, 2 * a:2 * b:2], T.sel[:, a:b], SPLIT, SPLIT, A.add, A.subtract, r=["sel%d" % h, "sel2"], w=["hi%d" % h])
+    for h, (a, b) in enumerate(halves):
+        tt(T.hl[:, 2 * a + 1:2 * b:2], T.sel[:, a:b], T.hl[:, 2 * a:2 * b:2], A.subtract, r=["hi%d" % h], w=["lo%d" % h])
+    quant(T.qv, T.sv, 0, 128, T.vt, r=["vt"], w=["qv"])
+    quant(T.qh, T.sh, 0, MID, T.hl, r=["lo0", "lo1"], w=["qh"])
+    mm(4, T.qp, T.sp, 0, T.qh, T.sh, 0, MID, r=["qp", "qh"])
+    spread(T.d0k, E, 0, BIG, ["d0k"])
+    act(T.d1k[:, 0:E - 1], T.d0k[:, 1:E], F.Copy, r=["d0k"], w=["d1k"])
+    act(dg[:, 3:4 * E:4], dg[:, 0:4 * E:4], F.Sign, scale=-1.0, bias=dg[:, 4 * E - 4:4 * E - 3], r=["dg0o", "dg0l"], w=["dg3"])
+    ties(1)
+    quant(T.qc, T.sc, 0, 256, T.ct, r=["ct0", "ct1"], w=["qc"])
+    scan(T.sk[:, 0:MID], T.d0h[:], bank(4, 0, MID), A.add, A.max, r=["d0h"], w=["p4"] + sks)
+
+    def unpack(t, banks, products):
+        q, s = T["q%d" % t], T["s%d" % t]
+        for b, k in enumerate(banks):
+            if products:
+                mm(k, T.qe, T.se, 128 * b, q, s, E - 128, E, r=["qe%d" % b, "q%d.1" % t, "q%d.h" % t])
+            else:
+                act(T["vh%d" % t][:, 4 * C + b:4 * E:4], bank(k, 128 - H, 128), F.Copy, scale=0.5, w=["p%d" % k, "vh%d.h%d" % (t, b)])
+
+    OWN = {"a": (0, AB), "b": (AB, EB), "l": (EB, NB)}
+    KEYS = {"a": (1, 0, 16 * AB), "b": (6, 16 * EB - 128, 16 * EB), "l": (7, E - 128, E),
+            "ab": (2, 0, 16 * EB), "abl": (3, 0, 16 * (DC - 1))}
+    SCORE = {"a": 0, "b": 4, "l": 5}
+
+    def score(t, part):
+        a, b = PART[part]
+        rs = {"a": [".0"], "b": [".1"], "l": [".1", ".h"]}[part]
+        mm(SCORE[part], T.qa, T.sa, 0, T["q%d" % t], T["s%d" % t], min(a, b - 128), b, r=["qa", "sa"] + ["q%d%s" % (t, n) for n in rs])
+
+    def signs(t, part):
+        a, b = PART[part]
+        k = SCORE[part]
+        o = max(0, 128 - (b - a))
+        ts(dg[:, 4 * a + t:4 * b:4], bank(k, o, o + b - a), 0.0, None, A.is_gt, w=["p%d" % k, "dg%d%s" % (t, part)])
+
+    def digits(t, part):
+        a, b = PART[part]
+        quant(T["qd%d" % t], T["sd%d" % t], a, max(b, a + 128), dg,
+              r=["dg0o", "dg0l", "dg3", "dgp", "dg1" + part, "dg2" + part], w=["qd%d%s" % (t, part)])
+
+    def keys(t, row, old):
+        k, lo, hi = KEYS[row]
+        terms = {(1, False): ((0, 0), (1, 2)), (2, True): ((3, 2), (1, 6)), (2, False): ((2, 0), (0, 4))}.get((t, old), ())
+        u = t - old
+        have = "abl" if old else {"b": "ab", "l": "bl"}.get(row, row)
+        for i, (c, d) in enumerate(terms):
+            mm(k, T.qk, T.sk8, 128 * c, T["qd%d" % u], T["sd%d" % u], lo + d, hi + d,
+               r=["qk%d" % c] + ["qd%d%s" % (u, p) for p in have], start=i == 0 and (old or t == 1), stop=i == 1 and not old)
+
+    def tied(t, part):
+        a, b = (16 * c for c in OWN[part])
+        k, lo, _ = KEYS[part]
+        tt(T["kt%d" % t][:, a:b], bank(k, a - lo, b - lo), T["tie%d" % t][:, a:b], A.add, r=["p%d" % k, "tie%d" % t], w=["tied." + part])
+
+    def hold(t, part):
+        a, b = (16 * c for c in OWN[part])
+        k, lo, _ = KEYS[part]
+        if part == "l":
+            scan(T.sk[:, a:b], T.d0k[:, a:b], T["kt%d" % t][:, a:b], A.add, A.max, r=["d0k", "tied.l"], w=["sk.l"])
+        else:
+            scan(T.sk[:, a:b], T.d0k[:, a:b], bank(k, a - lo, b - lo), A.add, A.max, r=["d0k", "p%d" % k], w=["sk." + part])
+
+    def owned(t, part):
+        c0, c1 = OWN[part]
+        ts(T.kw[:, c0:c1], T.sk[:, 16 * c0 + 15:16 * c1:16], col[:, 0:1], STEP[t], A.subtract, A.add, r=["sk." + part, "col0"], w=["kw." + part])
+
+    def inside(t, parts):
+        c0, c1 = OWN[parts[0]][0] // 2 * 2, OWN[parts[-1]][1]
+        o = 4 * TOFF[TD]
+        tt(T.tb[:, o + 64 * c0:o + 64 * c1:4], T.kw[:, 0:c1].indirect(T.od[:, c0:c1]), T["kt%d" % t][:, 16 * c0:16 * c1], A.is_gt,
+           r=["kw." + p for p in "abl" if OWN[p][0] < c1] + ["tied." + p for p in "abl" if OWN[p][0] < c1] + ["od"],
+           w=["in.a", "in.b"] if parts[0] != "a" else ["in.a"])
+
+    def compare(t, c):
+        k = [c in cs for cs, _ in TILES].index(True)
+        j = TILES[k][0].index(c)
+        o = 4 * TOFF[k] + j
+        part = "l" if c >= EB else "b" if c >= AB else "a"
+        out = T.tb[:, o:o + 64 * c - j:4]
+        if c >= DC:
+            ts(out, T["kt%d" % t][:, 0:16 * c], T.kw[:, c:c + 1], 0.5, A.is_le, A.subtract, r=tieds + ["kw.l"], w=["tb%d.%d" % (k, j)])
+        else:
+            kb = KEYS["a" if c <= AB else "ab" if c <= EB else "abl"][0]
+            act(out, bank(kb, 0, 16 * c), F.Sign, scale=-1.0, bias=T.kw[:, c:c + 1], accum_out=T.rw[:, c:c + 1],
+                r=["p%d" % kb, "kw." + part, "tied.a"], w=["tb%d.%d" % (k, j), "rw%d" % c])
+
+    def rowsum(c):
+        j, i = TILES[TD][0].index(c), c - DC + 1
+        o = 4 * TOFF[TD] + j
+        scan(T.jk[:, E * i - 16 * c:E * i], T.tb[:, o:o + 64 * c - j:4], T.zr[:, 0:16 * c], A.add, A.add,
+             r=["tb%d.%d" % (TD, j), "zr"], w=["jk%d" % i])
+
+    def fold(k, start=False, stop=False):
+        wd = TILES[k][1]
+        quant(T.qt, T.st, TOFF[k], TOFF[k] + wd, T.tb, r=["tb%d.%d" % (k, j) for j in four] + ["in.a", "in.b"] * (k == TD), w=["qt%d" % k])
+        mm(6, T.qc, T.sc, 128 if k == TD else 0, T.qt, T.st, TOFF[k], TOFF[k] + (E if start else wd),
+           r=["qc", "qt%d" % k, "qt.z0", "qt.z1"], start=start, stop=stop)
+
+    def order(t):
+        for c in range(AB, EB):
+            compare(t, c)
+        inside(t, "ab")
+        signs(t, "l")
+        digits(t, "l")
+        keys(t, "l", False)
+        keys(t, "abl", False)
+        fold(TF, start=True)
+        tied(t, "l")
+        hold(t, "l")
+        unpack(t, (4, 5, 0, 7), True)
+        owned(t, "l")
+        fold(2)
+        for c in list(range(DC - 1, EB - 1, -1)) + [6, 5, 4, 3, 2, 1]:
+            compare(t, c)
+        for c in range(DC, NB):
+            compare(t, c)
+        inside(t, "l")
+        fold(3)
+        for c in range(DC, NB):
+            rowsum(c)
+        fold(TD)
+        fold(4)
+        ts(T.d1k[:, 16 * DC + 15:E:16], T.jk[:, E - 1:(NB - DC) * E:E], -2.0, col[:, 8:9], A.mult, A.add,
+           r=["jk%d" % i for i in range(1, NB - DC + 1)] + ["col8", "d1k"], w=["rc1"])
+        fold(5)
+        fold(1, stop=True)
+        unpack(t, (4, 5, 0, 7), False)
+        act(T["vh%d" % t][:, 0:4 * C], T.x32[:], F.Copy, scale=0.015625, r=xs[0] + xs[1], w=["vh%d.0" % t, "vh%d.1" % t])
+        ts(T.d1k[:, 15:16 * DC:16], T.rw[:, 0:DC], -1.0, col[:, 8:9], A.mult, A.add, r=["rw%d" % c for c in range(DC)] + ["col8", "d1k"], w=["rc0"])
+        scan(T.sk[:], bank(6, 0, E), T.d1k[:], A.max, A.add, r=["d1k", "rc0", "rc1"], w=["p6"] + sks, first=-BIG)
+
+    for t in range(R):
+        vh = T["vh%d" % t]
+        last = t == R - 1
+        if t:
+            order(t)
+            ts(T.pos[:, 0:NB], T.sk[:, 15:E:16], col[:, 10:11], -0.5, A.subtract, A.mult, r=sks + ["col10"], w=["pos"])
+            ts(T.onm[:, 0:20], T.sk[:, 15:C:16], col[:, 11:12], -0.5, A.subtract, A.mult, r=sks + ["col10"], w=["on"])
+        else:
+            unpack(0, (5, 6, 7, 0), True)
+            unpack(0, (5, 6, 7, 0), False)
+            act(T.x32[:], T.xt[:], F.Copy, scale=32.0, r=x0 + x1, w=xs[0] + xs[1])
+            ts(T.pos[:, 0:NB], T.sk[:, 7:MID:8], col[:, 1:2], 1.0, A.subtract, A.subtract, r=sks + ["col0"], w=["pos"])
+            ts(T.onm[:, 0:20], T.sk[:, 7:C // 2:8], col[:, 1:2], 2.0, A.subtract, A.subtract, r=sks + ["col0"], w=["on"])
+        cp(T.ordr[:, 0:E].indirect(T.pos[:, 0:NB]), T.ic[:], r=["pos", "ic"], w=["ordr"])
         ts(T.onm[:, 20:40], T.pos[:, 0:20], 1.0, E - 1.0, A.add, A.min, r=["pos"], w=["om"])
+        act(T.gn[:], T.ordr[:, 0:E].indirect(T.onm[:, 0:20]), F.Copy, r=["ordr", "on"], w=["gn"])
         cp(T.gm[:], T.ordr[:, 0:E].indirect(T.onm[:, 20:40]), r=["ordr", "om"], w=["gm"])
-        dv = ["d0v%d" % b for b in four]
-        scan(T.sn[:], T.d0v[:], T.gn[:], A.add, A.max, r=["gn"] + dv, w=["sn"])
-        ts(T.ov[:, 0:80], T.sn[:, 3:C:4], col[:, 3:4], None, A.add, r=["sn", "col3"], w=["ovn"])
-        scan(T.sm[:], T.d0v[:], T.gm[:], A.add, A.max, r=["gm"] + dv, w=["sm"])
-        if t == 0:
-            quant(T.qc, T.sc, 0, 384, T.ct, r=["ct0", "ct1"] + ["ct2%d" % b for b in four], w=["qc"])
-        if t == 1:
-            ts(T.k2f[:], kk[:], 2.0, -WC, A.mult, A.add, r=["kh" + p for p in PARTS], w=["k2f" + p for p in PARTS])
-        if t == R - 1:
+        if last:
             scan(T.sk[:], T.d0k[:], T.ordr[:], A.add, A.max, r=["d0k", "ordr"], w=sks)
-        ts(T.ov[:, 80:160], T.sm[:, 3:C:4], col[:, 3:4], None, A.add, r=["sm", "col3"], w=["ovm"])
+        else:
+            quant(T.qk, T.sk8, 256 * t, 256 * t + 128, T.kt, r=["kt%d" % (2 * t)], w=["qk%d" % (2 * t)])
+        scan(T.sm[:], T.d0v[:], T.gm[:], A.add, A.max, r=["gm", "d0v"], w=["sm"])
+        scan(T.sn[:], T.d0v[:], T.gn[:], A.add, A.max, r=["gn", "d0v"], w=["sn"])
+        ts(T.ov[:, 80:160], T.sm[:, 3:C:4], 4.0, col[:, 3:4], A.mult, A.add, r=["sm", "col3"], w=["ovm"])
+        if last:
+            ts(T.ow[:, 0:NB], T.sk[:, 15:E:16], col[:, 0:1], 1.0 * MID, A.subtract, A.add, r=sks + ["col0"], w=["ow"])
+        ts(T.ov[:, 0:80], T.sn[:, 3:C:4], 4.0, col[:, 3:4], A.mult, A.add, r=["sn", "col3"], w=["ovn"])
+        if not last:
+            quant(T.qk, T.sk8, 256 * t + 128, 256 * t + 256, T.kt, r=["kt%d" % (2 * t + 1)], w=["qk%d" % (2 * t + 1)])
         vr = ["vh%d.0" % t, "vh%d.1" % t] + ["vh%d.h%d" % (t, b) for b in four]
-        pieces = ((0, 64), (64, C0), (C0, C))
+        pieces = PIECES
         for k, (a, b) in enumerate(pieces):
-            act(T.g1[:, 4 * a:4 * b], vh[:, 0:4 * E].indirect(T.ov[:, a // 4:b // 4]), F.Copy, r=vr + ["ovn"], w=["g1.%d" % k])
-        act(T.g3[:, 4 * C0:4 * C], vh[:, 0:4 * E].indirect(T.ov[:, 80 + C0 // 4:160]), F.Copy, r=vr + ["ovm"], w=["g3"])
+            act(T.g1[:, 4 * a:4 * b], vh[:, 0:4 * E].indirect(T.ov[:, 80 + a // 4:80 + b // 4]), F.Copy, r=vr + ["ovm"], w=["g1.%d" % k])
+        act(T.g3[:, 4 * G3:4 * C], vh[:, 0:4 * E].indirect(T.ov[:, G3 // 4:80]), F.Copy, r=vr + ["ovn"], w=["g3b"])
+        if last:
+            act(T.ks[:], T.kt2[:, 0:E].indirect(T.ow[:, 0:NB]), F.Copy, scale=512.0, r=tieds + ["ow"], w=["ks"])
+        cp(T.g3[:, 4 * C0:4 * G3], vh[:, 0:4 * E].indirect(T.ov[:, C0 // 4:G3 // 4]), r=vr + ["ovn"], w=["g3a"])
 
         def most(k):
             a, b = pieces[k]
-            if k < 2:
-                tt(T.g2[:, 4 * a:4 * b], vh[:, 0:4 * E].indirect(T.ov[:, 80 + a // 4:80 + b // 4]), T.g1[:, 4 * a:4 * b], A.max,
-                   r=vr + ["ovm", "g1.%d" % k], w=["g2.%d" % k])
+            if a < C0:
+                tt(T.g2[:, 4 * a:4 * b], vh[:, 0:4 * E].indirect(T.ov[:, a // 4:b // 4]), T.g1[:, 4 * a:4 * b], A.max,
+                   r=vr + ["ovn", "g1.%d" % k], w=["g2.%d" % k])
             else:
-                tt(T.g2[:, 4 * a:4 * b], T.g3[:, 4 * a:4 * b], T.g1[:, 4 * a:4 * b], A.max, r=["g3", "g1.%d" % k], w=["g2.%d" % k])
+                tt(T.g2[:, 4 * a:4 * b], T.g3[:, 4 * a:4 * b], T.g1[:, 4 * a:4 * b], A.max, r=["g3a", "g3b", "g1.%d" % k], w=["g2.%d" % k])
 
         def blend(k):
             a, b = pieces[k]
@@ -428,62 +490,90 @@ def rank_program(g, core, T, topo):
         def layer(h, ks):
             a, b = CH[h]
             quant(T.qz, T.sz, a, b, T.zt, r=["zt%d" % k for k in ks], w=["qz%d" % h])
-            p, pn = ((T.pa, "pa"), (T.pb, "pb"))[h]
             for j in four:
-                mm(bank(p, j, 0, b - a), T.qw, T.sw, 128 * j, T.qz, T.sz, a, b, r=["qw", "sw", "qz%d" % h], w=["%s%d" % (pn, j)])
+                mm(4 * h + j, T.qw, T.sw, 128 * j, T.qz, T.sz, a, b, r=["qw", "sw", "qz%d" % h])
 
         def state(h, js):
             a, b = CH[h]
-            p, pn = ((T.pa, "pa"), (T.pb, "pb"))[h]
             for j in js:
                 x = T.x32[:, 4 * a + j:4 * b:4]
-                tt(x, bank(p, j, 0, b - a), x, A.add, w=["%s%d" % (pn, j), "x32.%d.%d" % (h, j)])
-                if h == 0:
-                    act(T.xt[:, j:4 * C0:4], x, F.Copy, scale=0.03125, r=["x32.0.%d" % j], w=["xt.0.%d" % j])
+                tt(x, bank(4 * h + j, 0, b - a), x, A.add, w=["p%d" % (4 * h + j), "x32.%d.%d" % (h, j)])
+                if j < 2:
+                    act(T.xt[:, 4 * a + j:4 * b:4], x, F.Copy, scale=0.03125, r=["x32.%d.%d" % (h, j)], w=["xt.%d.%d" % (h, j)])
 
-        xs = [["x32.%d.%d" % (h, j) for j in four] for h in range(2)]
-        q2, s2, qm = T["q%d" % (t + 1)], T["s%d" % (t + 1)], "q%d" % (t + 1)
+        def shrink(h):
+            a, b = CH[h]
+            for j in (2, 3):
+                ts(T.xt[:, 4 * a + j:4 * b:4], T.x32[:, 4 * a + j:4 * b:4], 0.03125, None, A.mult, r=["x32.%d.%d" % (h, j)], w=["xt.%d.%d" % (h, j)])
+
+        u = t + 1
+        q2, s2, qm = T["q%d" % u], T["s%d" % u], "q%d" % u
         most(0)
-        if t == R - 1:
-            ts(T.ow[:, 0:NB], T.sk[:, 15:E:16], col[:, 0:1], 0.25, A.subtract, A.mult, r=sks + ["col0"], w=["ow"])
-            act(T.ks[:], ka[:, 0:E].indirect(T.ow[:, 0:NB]), F.Copy, scale=2048.0, r=["kf" + p for p in PARTS] + ["ow"], w=["ks"])
-        blend(0)
         most(1)
-        blend(1)
-        layer(0, (0, 1))
+        blend(0)
         most(2)
-        state(0, (0,))
+        blend(1)
         blend(2)
-        state(0, (1,))
-        layer(1, (2,))
-        state(0, (2, 3))
-        state(1, four)
-        quant(q2, s2, 0, C0, T.xt, r=x0, w=[qm + ".0"])
-        if t < R - 1:
-            send(t + 1)
-        ts(T.xt[:, 4 * C0:4 * C], T.x32[:, 4 * C0:4 * C], 0.03125, None, A.mult, r=xs[1], w=["xt.1"])
-        if t < R - 1:
-            mm(bank(T.pb, 0, 0, C0), T.qa, T.sa, 0, q2, s2, 0, C0, r=["qa", "sa", qm + ".0"], w=["pb0"])
-            signs(".a", 0, C0, 0, 0)
-        quant(q2, s2, C0, C, T.xt, r=["xt.1"], w=[qm + ".1"])
-        if t < R - 1:
-            vn = T["vh%d" % (t + 1)]
-            act(vn[:, 0:4 * C], T.x32[:], F.Copy, scale=0.015625, r=xs[0] + xs[1], w=["vh%d.0" % (t + 1), "vh%d.1" % (t + 1)])
+        most(3)
+        layer(0, (0, 1, 2))
+        blend(3)
+        state(0, (0,))
+        layer(1, (3,))
+        state(0, (1, 2, 3))
+        state(1, (0, 1))
+        shrink(0)
+        state(1, (2, 3))
+        if last:
+            break
         if t == 0:
-            for k in (5, 6):
-                lo = 48 if k == 5 else 0
-                act(T.tb[:, 4 * (TOFF[k] + lo):4 * (TOFF[k] + 128)], T.zr[:, 0:4 * (128 - lo)], F.Copy, r=["zr"], w=["tb%d.%d" % (k, j) for j in four])
+            ties(2)
+            act(T.kt[:, 1024:1536], T.kt[:, 0:512], F.Copy, scale=HIGH, r=["kt0"], w=["kt2"])
+        keys(u, "a", True)
+        keys(u, "abl", True)
+        quant(q2, s2, 0, C0, T.xt, r=x0, w=[qm + ".0"])
+        send(u)
+        score(u, "a")
+        shrink(1)
+        keys(u, "b", True)
+        quant(q2, s2, C0, C, T.xt, r=x1, w=[qm + ".1"])
+        score(u, "b")
+        keys(u, "ab", True)
+        signs(u, "a")
+        digits(u, "a")
+        keys(u, "a", False)
+        signs(u, "b")
+        digits(u, "b")
+        keys(u, "b", False)
+        keys(u, "l", True)
+        keys(u, "ab", False)
+        score(u, "l")
+        hold(u, "a")
+        tied(u, "a")
+        owned(u, "a")
+        for c in (10, 9, 8, 7):
+            compare(u, c)
+        hold(u, "b")
+        tied(u, "b")
+        owned(u, "b")
     q, s = T.q3, T.s3
-    for h, (a, b) in enumerate(CH):
-        mm(bank(T.pa, h, 0, b - a), T.qv, T.sv, 0, q, s, a, b, r=["qv", "q3.%d" % h], w=["pa%d" % h])
+
+    def leave(h):
+        a, b = CH[h]
+        quant(q, s, a, b, T.xt, r=(x0, x1)[h], w=["q3.%d" % h])
+        mm(h, T.qv, T.sv, 0, q, s, a, b, r=["qv", "q3.%d" % h])
         dma("sp", T.oc[:, 4 * a:4 * b], q[:, a:b].bitcast(dt.uint8), r=["q3.%d" % h])
-        act(T.ys[:, a:b], bank(T.pa, h, 0, b - a), F.Copy, w=["pa%d" % h, "ys%d" % h])
-        dma("act", T.y[:, a:b], T.ys[:, a:b], r=["ys%d" % h])
+
+    leave(0)
+    shrink(1)
+    tt(T.dk[:, 1:E], T.ks[:, 1:E], T.ks[:, 0:E - 1], A.subtract, r=["ks"], w=["dk"])
+    leave(1)
+    scan(T.ls[:], T.dk[:], T.ic[:], A.add, A.min, r=["dk", "dk0", "ic"], w=["ls"])
     for k in four:
         dma("sp", T.osc[4 * k:4 * k + 4, :], s[32 * k:32 * k + 4, 0:C], r=["q3.0", "q3.1"])
-    tt(T.dk[:, 1:E], T.ks[:, 1:E], T.ks[:, 0:E - 1], A.subtract, r=["ks"], w=["dk"])
-    scan(T.ls[:], T.dk[:], T.i4[:, 0:E], A.add, A.min, r=["dk", "dk0", "i4"], w=["ls"])
-    ts(T.lr[:], T.ls[:, 0:E].indirect(T.pos[:, 0:NB]), 0.25, None, A.mult, r=["ls", "pos"], w=["lr"])
-    dma("sp", T.lv[:], T.lr[0:128:16, :], r=["lr"])
+    ts(T.lr[:], T.ls[:, 0:E].indirect(T.pos[:, 0:NB]), 1.0 * MID, None, A.add, r=["ls", "pos"], w=["lr"])
+    for h, (a, b) in enumerate(CH):
+        act(T.ys[:, a:b], bank(h, 0, b - a), F.Copy, w=["p%d" % h, "ys%d" % h])
+        dma("act", T.y[:, a:b], T.ys[:, a:b], r=["ys%d" % h])
+    dma("sp", T.lv[:], T.lr[15:128:16, :], r=["lr"])
     for sname, v in cnt.items():
         g.wait_ge(T.sem[sname], v)

@@ -4,21 +4,19 @@ A = AluOpType
 F = ActivationFunctionType
 C, H, E, R = 320, 96, 416, 3
 C0 = 192
-PIECES = ((0, 64), (64, 128), (128, C0), (C0, C))
-G3 = 288
+PIECES, MODE = ((0, 32), (32, 80), (80, 144), (144, C0), (C0, 256), (256, C)), "FDFFFA"
 EP = C + 128
 NB, AB, EB = 26, 11, 19
 RADIX, HIGH = 36.0, 4096.0
 STEP = (0.0, 1.0, 0.5)
 NONE1, NONE2 = -34.0, -1200.0
-BIG = 11010048.0
-BIGV = 512.0
-SPLIT = 402653184.0
+BIG, BIGP, BIGV = 11010048.0, 4096.0, 512.0
+SPLIT = 805306368.0
 MID = E // 2
-TILES = (((0, 25, 24, 23), 416), ((1, 2), 128), ((11, 12, 13, 14), 224), ((15, 16, 17, 18), 288),
-         ((19, 20, 21, 22), 352), ((3, 4, 5, 6), 128), ((7, 8, 9, 10), 160))
-TD, DC = 0, 23
-TF = 6
+TILES = (((0, 25, 24, 23), 416), ((1, 2), 128), ((3, 4, 5, 6), 128), ((11, 12, 13, 14), 224), ((7, 8, 9, 10), 160),
+         ((19, 20, 21, 22), 352), ((15, 16, 17, 18), 288))
+TD, TF = 0, 6
+DVS = ((), (3, 4, 5, 6, 22, 23, 24, 25), (3, 4, 5, 6, 23, 24, 25))
 TOFF = [sum(w for _, w in TILES[:k]) for k in range(len(TILES) + 1)]
 Q4, U8, BF, F16, F32, I32, U16 = "float8_e4m3fn_x4", "uint8", "bfloat16", "float16", "float32", "int32", "uint16"
 
@@ -35,16 +33,17 @@ SCRATCH = {
     "ct": _sb(1024, BF), "qc": _sb(256, Q4), "sc": _sb(256, U8), "tp": _sb(512, BF), "qp": _sb(128, Q4), "sp": _sb(128, U8),
     "kt": _sb(2048, BF), "qk": _sb(512, Q4), "sk8": _sb(512, U8),
     "pi": _sb(8, I32), "ci": _sb(8, I32), "cf": _sb(8, F32), "jm": _sb(80, BF), "df": _sb(48, BF), "ta": _sb(48, BF),
-    "tc": _sb(48, BF), "tab": _sb(64, BF), "col": _sb(12, F32), "ic": _sb(E, BF), "zr": _sb(512, BF),
+    "tc": _sb(48, BF), "tab": _sb(64, BF), "col": _sb(16, F32), "off": _sb(16, F32), "cc": _sb(36, F32),
+    "ic": _sb(E, BF), "zr": _sb(512, BF),
     "oab": _sb(16, U16), "orr": _sb(32, U16), "od": _sb(32, U16), "og": _sb(32, U16), "op": _sb(32, U16), "o2": _sb(32, U16),
-    "d0k": _sb(E, BF), "d0h": _sb(MID, BF), "d0v": _sb(C, BF), "tie1": _sb(E, BF), "tie2": _sb(E, F32),
-    "ab": _sb(E, BF), "a2": _sb(E, BF), "wb": _sb(E + 16, BF), "mb": _sb(E, BF), "dg": _sb(4 * EP, BF),
-    "qd1": _sb(EP, Q4), "sd1": _sb(EP, U8), "qd2": _sb(EP, Q4), "sd2": _sb(EP, U8),
-    "oh": _sb(E, BF), "pre": _sb(E, F16), "sel": _sb(E, F16), "hl": _sb(2 * E, BF), "qh": _sb(MID, Q4), "sh": _sb(MID, U8),
-    "junk": _sb(E, BF), "acc": _sb(8, F32), "a8": _sb(H, BF), "b4": _sb(H, BF), "d1k": _sb(E, F32),
-    "kt1": _sb(E, F16), "kt2": _sb(E, F32), "jk": _sb(3 * E, F16),
-    "sk": _sb(E, F32), "kw": _sb(32, F32), "rw": _sb(32, F32), "rc": _sb(32, F32), "dd": _sb(32, F32),
-    "tb": _sb(4 * TOFF[-1], BF), "qt": _sb(TOFF[-1] + 256, Q4), "st": _sb(TOFF[-1] + 256, U8),
+    "d0k": _sb(E, BF), "d0h": _sb(MID, BF), "d0v": _sb(C, BF), "d1k": _sb(E + 16, F32), "tie1": _sb(E, BF), "tie2": _sb(E, F32),
+    "ab": _sb(E, BF), "a2": _sb(E, BF), "a8": _sb(H, BF), "b4": _sb(H, BF), "wb": _sb(E + 16, BF), "mb": _sb(E, BF),
+    "dg": _sb(4 * EP, BF), "qd1": _sb(EP, Q4), "sd1": _sb(EP, U8), "qd2": _sb(EP, Q4), "sd2": _sb(EP, U8),
+    "oh": _sb(E, BF), "oh2": _sb(E, F16), "pre": _sb(E, F16), "sel": _sb(E, F16), "hl": _sb(2 * E, BF),
+    "qh": _sb(MID, Q4), "sh": _sb(MID, U8), "junk": _sb(E, BF), "acc": _sb(8, F32),
+    "kt1": _sb(E, F16), "kt2": _sb(E, F32), "jk": _sb(8 * E, F16),
+    "sk": _sb(E, F32), "ps": _sb(E, F32), "kw": _sb(32, F32), "rw": _sb(32, F32),
+    "tb": _sb(4 * TOFF[-1], BF), "qt": _sb(TOFF[-1] + 128, Q4), "st": _sb(TOFF[-1] + 128, U8),
     "pos": _sb(32, U16), "onm": _sb(40, U16), "ordr": _sb(E, BF), "gn": _sb(C, BF), "gm": _sb(C, BF),
     "sn": _sb(C, F16), "sm": _sb(C, F16), "ov": _sb(160, U16),
     "g1": _sb(4 * C, BF), "g3": _sb(4 * C, BF), "g2": _sb(4 * C, BF), "zt": _sb(4 * C, BF), "qz": _sb(C, Q4), "sz": _sb(C, U8),
@@ -166,17 +165,28 @@ def rank_program(g, core, T, topo):
     def spread(out, n, k, scale, w):
         act(out[:, 0:n], T.tab[:, 16 * k:16 * k + 16].indirect(T.orr[:, 0:n // 16]), F.Copy, scale=scale, r=["tab%d" % (k // 3), "orr"], w=w)
 
-    def block(k, lst):
-        act(T.ct[:, 512 * k:512 * k + 512], T.jm[:, 0:16].indirect(T[lst][:]), F.Copy, r=["jm0", lst], w=["ct%d" % k])
+    def block(out, lst, scale, w):
+        act(out, T.jm[:, 0:16].indirect(T[lst][:]), F.Copy, scale=scale, r=["jm0", lst], w=w)
 
-    def ties(t):
+    def ties(t, step):
         tie = T["tie%d" % t]
-        spread(tie, E, 3, STEP[t], ["tie%d" % t])
-        for a, c in (((E - 2, NONE1),), ((E - 6, NONE1), (E - 4, NONE2), (E - 2, NONE2 + HIGH * NONE1)))[t - 1]:
-            act(tie[:, a:a + 2], tie[:, a:a + 2], F.Identity, bias=c, w=["tie%d" % t])
+        if step == 0:
+            spread(tie, E, 3, STEP[t], tie_of[t])
+            return
+        for k, (a, c) in enumerate((((E - 2, NONE1),), ((E - 6, NONE1), (E - 4, NONE2), (E - 2, NONE2 + HIGH * NONE1)))[t - 1]):
+            act(tie[:, a:a + 2], tie[:, a:a + 2], F.Identity, bias=c, w=["tie%d.%d" % (t, k)])
 
-    def zeros(k):
-        quant(T.qt, T.st, TOFF[-1] + 128 * k, TOFF[-1] + 128 * k + 128, T.zr, r=["zr"], w=["qt.z%d" % k], at=0)
+    def missing(t, step):
+        if step == 0:
+            scan(T.cc[:, 16 * t - 16:16 * t], T.d0k[:, 0:16], T["tie%d" % t][:, E - 16:E], A.add, A.max, r=["d0k"] + tie_of[t], w=["cd%d" % t])
+        else:
+            ts(T.cc[:, 31 + t:32 + t], T.col[:, 0:1], -2.0, T.cc[:, 16 * t - 1:16 * t], A.mult, A.add, r=["col0", "cd%d" % t], w=["cc%d" % t])
+
+    def unit(b):
+        quant(T.qe, T.se, 128 * b, 128 * (b + 1), T.et, r=["et"], w=["qe%d" % b], at=3 - b)
+
+    def weights(k):
+        quant(T.qk, T.sk8, 128 * k, 128 * k + 128, T.kt, r=["kt%d" % k], w=["qk%d" % k])
 
     CH = ((0, C0), (C0, C))
     PART = {"a": (0, C0), "b": (C0, C), "l": (C, E)}
@@ -186,149 +196,164 @@ def rank_program(g, core, T, topo):
     xs = [["x32.%d.%d" % (h, j) for j in four] for h in range(2)]
     sks = ["sk.a", "sk.b", "sk.l"]
     tieds = ["tied.a", "tied.b", "tied.l"]
+    tie_of = [["tie%d.%d" % (t, k) for k in range(3)] for t in range(R)]
+    dfs = ["df%d" % k for k in range(3)]
     dma("sp", T.xt[:, 0:512], T.x[:, 0:512], w=x0)
     dma("act", T.ut[:], T.u[:], w=["ut"])
     dma("sp", T.xt[:, 512:4 * C], T.x[:, 512:4 * C], w=x1)
-    dma("sp", T.qw[:].bitcast(dt.uint8), T.wc[:], r=x1, w=["qw"])
-    dma("sp", T.sw[:], T.ws[:], w=["sw"])
-    dma("sp", T.vt[:], T.v[:], w=["vt"])
     iota(T.pi[:, 0:2], [[2, 2]], 0, 1, ["pi"], False)
     iota(jm[:, 0:16], [[1, 16]], 0, 0, ["jm0"])
     iota(jm[:, 48:80], [[1, 8], [0, 4]], 0, 0, ["jm3"])
     iota(jm[:, 16:32], [[0, 2], [1, 8]], 0, 0, ["jm1"])
     iota(jm[:, 32:48], [[0, 4], [1, 4]], 0, 0, ["jm2"])
-    iota(T.ic[:], [[1, E]], -MID, 0, ["ic"])
-    ms(T.zr[:], 0.0, w=["zr"])
+    ms(T.one[:], 1.0, w=["one"])
+    keep(T.et[:], T.one[:], [[1, 516]], A.is_equal, -3, -4, ["one"], ["et"])
     for k, (sh, m) in enumerate(((0, 15), (1, 7), (2, 3), (0, 3), (4, 7))):
         ts(T.ci[:, k:k + 1], T.pi[:, 0:1], sh, m, A.arith_shift_right, A.bitwise_and, r=["pi"], w=["ci%d" % k])
     ts(T.ci[:, 5:6], T.pi[:, 1:2], 2, 1, A.arith_shift_right, A.bitwise_and, r=["pi"], w=["ci5"])
-    ts(T.oab[:, 0:8], jm[:, 0:8], 16.0, None, A.mult, r=["jm0"], w=["oa"])
+    ms(T.zr[:], 0.0, w=["zr"])
     cp(cf[:, 0:6], T.ci[:, 0:6], r=["ci%d" % k for k in range(6)], w=["cf"])
+    ts(T.oab[:, 0:8], jm[:, 0:8], 16.0, None, A.mult, r=["jm0"], w=["oa"])
     ts(T.oab[:, 8:16], jm[:, 0:8], 16.0, 1.0, A.mult, A.add, r=["jm0"], w=["ob"])
     ms(T.wb[:, E:E + 16], 0.0, w=["wb.p"])
     ts(T.og[:], jm[:, 48:80], cf[:, 4:5], None, A.is_equal, r=["jm3", "cf"], w=["og"])
     ts(col[:, 7:8], cf[:, 0:1], -7.5, None, A.add, r=["cf"], w=["col7"])
-    ts(T.orr[:], T.zr[:, 0:32], cf[:, 0:1], None, A.add, r=["zr", "cf"], w=["orr"])
-    ts(T.op[:], T.og[:], cf[:, 5:6], None, A.subtract, r=["og", "cf"], w=["op"])
-    ts(col[:, 4:7], jm[:, 0:3], -0.25, col[:, 7:8], A.mult, A.add, r=["jm0", "col7"], w=["col4"])
     for k in range(3):
         ts(T.df[:, 16 * k:16 * k + 16], jm[:, 16 * k:16 * k + 16], cf[:, k:k + 1], None, A.subtract, r=["jm%d" % k, "cf"], w=["df%d" % k])
-    dfs = ["df%d" % k for k in range(3)]
-    ms(T.one[:], 1.0, w=["one"])
+    ts(T.op[:], T.og[:], cf[:, 5:6], None, A.subtract, r=["og", "cf"], w=["op"])
+    ts(col[:, 4:7], jm[:, 0:3], -0.25, col[:, 7:8], A.mult, A.add, r=["jm0", "col7"], w=["col4"])
     ts(T.ta[:], T.df[:], 0.0, -2.0, A.is_equal, A.mult, r=dfs, w=["ta"])
     ts(T.tc[:], T.df[:], 1.0, None, A.is_equal, r=dfs, w=["tc"])
-    ts(col[:, 9:10], cf[:, 3:4], NB - DC + 0.5, 1.0, A.is_lt, A.add, r=["cf"], w=["col9"])
-    tt(T.tab[:, 0:48], T.ta[:], T.tc[:], A.add, r=["ta", "tc"], w=["tab0"])
-    ts(T.o2[:], T.og[:], col[:, 9:10], None, A.mult, r=["og", "col9"], w=["o2"])
-    act(T.tp[:], jm[:, 0:16].indirect(T.op[:]), F.Copy, r=["jm0", "op"], w=["tp"])
+    quant(T.qt, T.st, TOFF[-1], TOFF[-1] + 128, T.zr, r=["zr"], w=["qt.z"], at=0)
+    block(T.tp[:], "op", 0.5, ["tp"])
+    spare.extend([
+        lambda: ts(T.orr[:], T.zr[:, 0:32], cf[:, 0:1], None, A.add, r=["zr", "cf"], w=["orr"]),
+        lambda: ts(col[:, 9:10], cf[:, 3:4], 0.5, 1.0, A.is_lt, A.add, r=["cf"], w=["col9"]),
+        lambda: tt(T.tab[:, 0:48], T.ta[:], T.tc[:], A.add, r=["ta", "tc"], w=["tab0"]),
+        lambda: ts(T.tab[:, 48:64], T.df[:, 0:16], 0.0, None, A.is_gt, r=dfs, w=["tab1"]),
+        lambda: ts(T.o2[:], T.og[:], col[:, 9:10], None, A.mult, r=["og", "col9"], w=["o2"]),
+        lambda: ts(col[:, 0:2], T.df[:, 15:32:16], 0.0, BIG, A.is_gt, A.mult, r=dfs, w=["col0"]),
+        lambda: ts(col[:, 2:3], T.df[:, 47:48], 0.0, -4.0 * BIGV, A.is_gt, A.mult, r=dfs, w=["col2"]),
+        lambda: ts(col[:, 13:14], T.df[:, 15:16], 0.0, T.ta[:, 0:1], A.is_gt, A.add, r=dfs + ["ta"], w=["col13"]),
+        lambda: ts(col[:, 3:4], col[:, 2:3], cf[:, 3:4], 4.0 * MID, A.add, A.add, r=["col2", "cf"], w=["col3"]),
+        lambda: ts(col[:, 8:9], T.ta[:, 0:1], BIGP, MID + 8.0, A.mult, A.add, r=["ta"], w=["col8"]),
+        lambda: ts(col[:, 10:11], col[:, 13:14], BIGP, None, A.mult, r=["col13"], w=["col10"]),
+        lambda: ts(col[:, 11:12], col[:, 13:14], BIGP, -1.0, A.mult, A.add, r=["col13"], w=["col11"]),
+        lambda: ts(T.od[:, 0:NB], T.ic[:, 0:NB], 1.0 * MID, None, A.add, r=["ic"], w=["od"]),
+    ])
     quant(T.q0, T.s0, 0, 128, T.xt, r=x0, w=["q0.0"])
     send(0)
+    dma("sp", T.vt[:], T.v[:], r=["q0.h"], w=["vt"])
+    dma("sp", T.qw[:].bitcast(dt.uint8), T.wc[:], w=["qw"])
+    dma("sp", T.sw[:], T.ws[:], w=["sw"])
     quant(T.qu, T.su, 0, 128, T.ut, r=["ut"], w=["qu"])
+    gap()
     quant(T.q0, T.s0, 128, C, T.xt, r=x1, w=["q0.1"])
     for q, s, lo, tok in ((T.qa, T.sa, 0, "a"), (T.qb, T.sb, 8, "b")):
         cp(q[:, 0:128].bitcast(dt.uint32), T.qu[:, 0:128].bitcast(dt.uint32).indirect(T.oab[:, lo:lo + 8]), r=["qu", "o" + tok], w=["q" + tok])
         act(s[:, 0:128], T.su[:, 0:128].indirect(T.oab[:, lo:lo + 8]), F.Copy, r=["qu", "o" + tok], w=["s" + tok])
-    keep(T.et[:], T.one[:], [[1, 516]], A.is_equal, -3, -4, ["one"], ["et"])
-    for k, wt in ((0, RADIX), (1, 1.0), (3, HIGH)):
-        x = T.kt[:, 512 * k:512 * k + 512]
-        iota(x, [[0, 128], [-2 * int(wt), 4]], 4 * int(wt), 0, ["kt%d" % k])
-        keep(x, x, [[1, 128], [0, 4]], A.is_equal, 0, -1, [], ["kt%d" % k])
-        if k == 0:
+    iota(T.ic[:], [[1, E]], -MID, 0, ["ic"])
+    for ks in (((0, RADIX), (1, 1.0)), ((3, HIGH),)):
+        for k, wt in ks:
+            iota(T.kt[:, 512 * k:512 * k + 512], [[0, 128], [-2 * int(wt), 4]], 4 * int(wt), 0, ["kt%d" % k])
+        if len(ks) == 1:
             keep(T.kt[:, 2:512:4], T.one[:, 0:128], [[1, 128]], A.is_equal, 0, -1, ["one"], ["kt0"])
+        for k, wt in ks:
+            x = T.kt[:, 512 * k:512 * k + 512]
+            keep(x, x, [[1, 128], [0, 4]], A.is_equal, 0, -1, [], ["kt%d" % k])
     iota(dg[:, 2:4 * E:4], [[0, E]], 0, 0, ["dg2a", "dg2b", "dg2l"])
     iota(dg[:, 4 * E:4 * EP], [[0, 4 * (EP - E)]], 0, 0, ["dgp"])
-    spread(T.d0h, MID, 1, BIG, ["d0h"])
-    act(T.vh0[:, 0:4 * C], T.xt[:], F.Copy, scale=0.5, r=x0 + x1, w=["vh0.0", "vh0.1"])
+    for x, tok in ((T.rw[:, 0:2], "rw0"), (T.dk[:, 0:2], "dk0")):
+        iota(x, [[0, 2]], 0, 0, [tok])
+    act(T.vh0[:, 0:4 * C], T.xt[:], F.Copy, scale=0.5, r=x0 + x1, w=["vh0"])
+    block(T.ct[:, 0:512], "og", -0.5, ["ct0"])
     for k, (cs, wd) in enumerate(TILES):
         lo = 0 if len(cs) < 4 else 16 * min(c for c in cs if c)
-        dma("sp", T.tb[:, 4 * (TOFF[k] + lo):4 * (TOFF[k] + wd)], T.zr[:, 0:4 * (wd - lo)], r=["zr", "vt"],
+        dma("sp", T.tb[:, 4 * (TOFF[k] + lo):4 * (TOFF[k] + wd)], T.zr[:, 0:4 * (wd - lo)], r=["zr"],
             w=["tb%d.%d" % (k, j) for j in four] + ["in.a", "in.b"] * (k == TD))
-    block(0, "og")
-
-    spare.extend([
-        lambda: ts(col[:, 0:2], T.df[:, 15:32:16], 0.0, BIG, A.is_gt, A.mult, r=dfs, w=["col0"]),
-        lambda: ts(col[:, 2:3], T.df[:, 47:48], 0.0, -4.0 * BIGV, A.is_gt, A.mult, r=dfs, w=["col2"]),
-        lambda: ts(T.tab[:, 48:64], T.df[:, 0:16], 0.0, None, A.is_gt, r=dfs, w=["tab1"]),
-        lambda: ts(col[:, 3:4], col[:, 2:3], cf[:, 3:4], 4.0 * MID, A.add, A.add, r=["col2", "cf"], w=["col3"]),
-        lambda: ts(T.od[:, 0:NB], T.ic[:, 0:NB], 1.0 * MID, None, A.add, r=["ic"], w=["od"]),
-        lambda: ms(T.rw[:, 0:1], 0.0, w=["rw0"]),
-        lambda: ms(T.dk[:, 0:1], 0.0, w=["dk0"]),
-        lambda: ts(col[:, 8:9], T.ta[:, 0:1], BIG, -16.0 - E, A.mult, A.add, r=["ta"], w=["col8"]),
-        lambda: ts(col[:, 10:12], jm[:, 0:3:2], -1.0, col[:, 0:1], A.mult, A.add, r=["jm0", "col0"], w=["col10"]),
-        lambda: ts(col[:, 10:12], col[:, 10:12], col[:, 8:9], 16.0 + E, A.add, A.add, r=["col8"], w=["col10"]),
-    ])
-
-    def classes(part, a, b, k, o, lo, hi):
-        sa, sb = bank(k, o, o + b - a), bank(k + 1, o, o + b - a)
-        ts(T.a2[:, a:b], sa, 0.0, 2.0, A.is_gt, A.mult, r=["p%d" % k], w=["a2" + part])
-        ts(T.ab[:, a:b], sb, 0.0, 0.5, A.is_gt, A.add, r=["p%d" % (k + 1)], w=["ab" + part])
-        if part == "l":
-            ts(T.a8[:], sa, 0.0, -8.0, A.is_le, A.mult, r=["p%d" % k], w=["a8"])
-            ts(T.b4[:], sb, 0.0, 4.0, A.is_gt, A.mult, r=["p%d" % (k + 1)], w=["b4"])
-        gap()
-        tt(T.wb[:, a:b], T.a2[:, a:b], T.ab[:, a:b], A.add, r=["a2" + part, "ab" + part], w=["wb" + part])
-        if part == "l":
-            tt(T.mb[:, a:b], T.a8[:], T.b4[:], A.add, r=["a8", "b4"], w=["mbl"])
-        else:
-            gap(2)
-            ts(T.mb[:, a:b], T.wb[:, a:b], 4.0, -10.0, A.mult, A.add, r=["wbo"], w=["mbo"])
-        gap(2)
-        more = ["wbl", "mbl", "wb.p"] * (part == "l")
-        tt(dg[:, 4 * lo:4 * hi:4], T.mb[:, lo:hi], T.wb[:, lo + 1:hi + 1], A.add, r=["wbo", "mbo"] + more, w=["dg0" + part])
-        n = int(part == "l")
-        act(T.junk[:, lo:hi], dg[:, 4 * lo:4 * hi:4], F.Sign, scale=-1.0, bias=col[:, 5:6], accum_out=T.acc[:, n:n + 1],
-            r=["dg0" + part, "col4"], w=["junk" + part, "acc" + part])
-        gap(2)
-        ts(T.oh[:, lo:hi], dg[:, 4 * lo:4 * hi:4], col[:, 4:5], None, A.is_equal, r=["dg0" + part, "col4"], w=["oh" + part])
-
-    mm(0, T.qa, T.sa, 0, T.q0, T.s0, 0, C, r=["qa", "sa", "q0.0", "q0.1"])
-    mm(1, T.qb, T.sb, 0, T.q0, T.s0, 0, C, r=["qb", "sb", "q0.0", "q0.1"])
-    quant(T.qp, T.sp, 0, 128, T.tp, r=["tp"], w=["qp"])
-    classes("o", 0, C, 0, 0, 0, C - 2)
-    mm(2, T.qa, T.sa, 0, T.q0, T.s0, E - 128, E, r=["qa", "sa", "q0.1", "q0.h"])
-    mm(3, T.qb, T.sb, 0, T.q0, T.s0, E - 128, E, r=["qb", "sb", "q0.1", "q0.h"])
-    for b in four:
-        quant(T.qe, T.se, 128 * b, 128 * (b + 1), T.et, r=["et"], w=["qe%d" % b], at=3 - b)
-    ts(T.acc[:, 2:3], T.acc[:, 0:1], 1.0 * E, None, A.add, r=["acco"], w=["acc2"])
-    block(1, "o2")
-    spread(T.d0v, C, 2, BIGV, ["d0v"])
-    classes("l", C, E, 2, 128 - H, C - 2, E)
-    zeros(0)
-    ts(T.acc[:, 3:4], T.acc[:, 1:2], T.acc[:, 2:3], 0.5, A.add, A.mult, r=["accl", "acc2"], w=["acc3"])
-    zeros(1)
-    scan(T.pre[:], T.oh[:], T.oh[:], A.add, A.max, r=["oho", "ohl", "acc3"], w=["pre"], first=T.acc[:, 3:4])
-    ts(T.sel[:, E - 1:E], dg[:, 4 * E - 4:4 * E - 3], col[:, 6:7], T.acc[:, 3:4], A.is_equal, A.mult, r=["dg0l", "col4", "acc3"], w=["sel2"])
-    gap(9)
-    halves = ((0, MID), (MID, E))
-    for h, (a, b) in enumerate(halves):
-        b = min(b, E - 1)
-        tt(T.sel[:, a:b], T.pre[:, a:b], T.oh[:, a:b], A.mult, r=["pre", "oho", "ohl"], w=["sel%d" % h])
-    for h, (a, b) in enumerate(halves):
-        ts(T.hl[:, 2 * a:2 * b:2], T.sel[:, a:b], SPLIT, SPLIT, A.add, A.subtract, r=["sel%d" % h, "sel2"], w=["hi%d" % h])
-    for h, (a, b) in enumerate(halves):
-        tt(T.hl[:, 2 * a + 1:2 * b:2], T.sel[:, a:b], T.hl[:, 2 * a:2 * b:2], A.subtract, r=["hi%d" % h], w=["lo%d" % h])
-    quant(T.qv, T.sv, 0, 128, T.vt, r=["vt"], w=["qv"])
-    quant(T.qh, T.sh, 0, MID, T.hl, r=["lo0", "lo1"], w=["qh"])
-    mm(4, T.qp, T.sp, 0, T.qh, T.sh, 0, MID, r=["qp", "qh"])
-    spread(T.d0k, E, 0, BIG, ["d0k"])
-    act(T.d1k[:, 0:E - 1], T.d0k[:, 1:E], F.Copy, r=["d0k"], w=["d1k"])
-    act(dg[:, 3:4 * E:4], dg[:, 0:4 * E:4], F.Sign, scale=-1.0, bias=dg[:, 4 * E - 4:4 * E - 3], r=["dg0o", "dg0l"], w=["dg3"])
-    ties(1)
-    quant(T.qc, T.sc, 0, 256, T.ct, r=["ct0", "ct1"], w=["qc"])
-    scan(T.sk[:, 0:MID], T.d0h[:], bank(4, 0, MID), A.add, A.max, r=["d0h"], w=["p4"] + sks)
 
     def unpack(t, banks, products):
         q, s = T["q%d" % t], T["s%d" % t]
-        for b, k in enumerate(banks):
+        for b, k in banks:
             if products:
                 mm(k, T.qe, T.se, 128 * b, q, s, E - 128, E, r=["qe%d" % b, "q%d.1" % t, "q%d.h" % t])
             else:
                 act(T["vh%d" % t][:, 4 * C + b:4 * E:4], bank(k, 128 - H, 128), F.Copy, scale=0.5, w=["p%d" % k, "vh%d.h%d" % (t, b)])
 
+    def classes(part, lo, hi, more):
+        tt(dg[:, 4 * lo:4 * hi:4], T.mb[:, lo:hi], T.wb[:, lo + 1:hi + 1], A.add, r=["wbo", "mbo"] + more, w=["dg0" + part])
+        n = int(part == "l")
+        act(T.junk[:, lo:hi], dg[:, 4 * lo:4 * hi:4], F.Sign, scale=-1.0, bias=col[:, 5:6], accum_out=T.acc[:, n:n + 1],
+            r=["dg0" + part, "col4"], w=["junk" + part, "acc" + part])
+
+    def members(part, lo, hi):
+        ts(T.oh2[:, lo:hi], dg[:, 4 * lo:4 * hi:4], col[:, 4:5], 2.0, A.is_equal, A.mult, r=["dg0" + part, "col4"], w=["oh2" + part])
+        ts(T.oh[:, lo:hi], dg[:, 4 * lo:4 * hi:4], col[:, 4:5], None, A.is_equal, r=["dg0" + part, "col4"], w=["oh" + part])
+
+    mm(0, T.qa, T.sa, 0, T.q0, T.s0, 0, C, r=["qa", "sa", "q0.0", "q0.1"])
+    mm(1, T.qb, T.sb, 0, T.q0, T.s0, 0, C, r=["qb", "sb", "q0.0", "q0.1"])
+    mm(2, T.qa, T.sa, 0, T.q0, T.s0, E - 128, E, r=["qa", "sa", "q0.1", "q0.h"])
+    mm(3, T.qb, T.sb, 0, T.q0, T.s0, E - 128, E, r=["qb", "sb", "q0.1", "q0.h"])
+    unit(0)
+    gap(3)
+    quant(T.qp, T.sp, 0, 128, T.tp, r=["tp"], w=["qp"])
+    ts(T.a2[:, 0:C], bank(0, 0, C), 0.0, 2.0, A.is_gt, A.mult, r=["p0"], w=["a2o"])
+    ts(T.ab[:, 0:C], bank(1, 0, C), 0.0, 0.5, A.is_gt, A.add, r=["p1"], w=["abo"])
+    gap(3)
+    spread(T.d0h, MID, 1, BIG, ["d0h"])
+    tt(T.wb[:, 0:C], T.a2[:, 0:C], T.ab[:, 0:C], A.add, r=["a2o", "abo"], w=["wbo"])
+    unit(1)
+    gap()
+    ts(T.mb[:, 0:C], T.wb[:, 0:C], 4.0, -10.0, A.mult, A.add, r=["wbo"], w=["mbo"])
+    unit(2)
+    gap()
+    classes("o", 0, C - 2, [])
+    spread(T.d0v, C, 2, BIGV, ["d0v"])
+    sa, sb = bank(2, 128 - H, 128), bank(3, 128 - H, 128)
+    ts(T.a2[:, C:E], sa, 0.0, 2.0, A.is_gt, A.mult, r=["p2"], w=["a2l"])
+    ts(T.ab[:, C:E], sb, 0.0, 0.5, A.is_gt, A.add, r=["p3"], w=["abl"])
+    ts(T.a8[:], sa, 0.0, -8.0, A.is_le, A.mult, r=["p2"], w=["a8"])
+    ts(T.b4[:], sb, 0.0, 4.0, A.is_gt, A.mult, r=["p3"], w=["b4"])
+    tt(T.wb[:, C:E], T.a2[:, C:E], T.ab[:, C:E], A.add, r=["a2l", "abl"], w=["wbl"])
+    tt(T.mb[:, C:E], T.a8[:], T.b4[:], A.add, r=["a8", "b4"], w=["mbl"])
+    members("o", 0, C - 2)
+    classes("l", C - 2, E, ["wbl", "mbl", "wb.p"])
+    ts(T.acc[:, 2:3], T.acc[:, 0:1], 1.0 * E, None, A.add, r=["acco"], w=["acc2"])
+    unit(3)
+    members("l", C - 2, E)
+    ts(T.oh2[:, 0:1], T.oh2[:, 0:1], T.acc[:, 2:3], None, A.add, r=["acc2"], w=["oh2o"])
+    HALO0 = ((0, 5), (1, 6), (2, 7), (3, 0))
+    unpack(0, HALO0, True)
+    act(T.x32[:], T.xt[:], F.Copy, scale=32.0, r=x0 + x1, w=xs[0] + xs[1])
+    scan(T.pre[:], T.oh2[:], T.oh[:], A.add, A.max, r=["oho", "ohl", "oh2o", "oh2l", "accl"], w=["pre"], first=T.acc[:, 1:2])
+    ts(T.acc[:, 3:4], T.acc[:, 1:2], T.acc[:, 2:3], None, A.add, r=["accl", "acc2"], w=["acc3"])
+    gap()
+    halves = ((0, MID), (MID, E))
+    for h, (a, b) in enumerate(halves):
+        b = min(b, E - 1)
+        tt(T.sel[:, a:b], T.pre[:, a:b], T.oh[:, a:b], A.mult, r=["pre", "oho", "ohl"], w=["sel%d" % h])
+        if h == 0:
+            ts(T.sel[:, E - 1:E], dg[:, 4 * E - 4:4 * E - 3], col[:, 6:7], T.acc[:, 3:4], A.is_equal, A.mult, r=["dg0l", "col4", "acc3"], w=["sel2"])
+    for h, (a, b) in enumerate(halves):
+        ts(T.hl[:, 2 * a:2 * b:2], T.sel[:, a:b], SPLIT, SPLIT, A.add, A.subtract, r=["sel%d" % h] + ["sel2"] * h, w=["hi%d" % h])
+    for h, (a, b) in enumerate(halves):
+        tt(T.hl[:, 2 * a + 1:2 * b:2], T.sel[:, a:b], T.hl[:, 2 * a:2 * b:2], A.subtract, r=["hi%d" % h], w=["lo%d" % h])
+    block(T.ct[:, 512:1024], "o2", -0.5, ["ct1"])
+    gap(2)
+    quant(T.qh, T.sh, 0, MID, T.hl, r=["lo0", "lo1"], w=["qh"])
+    mm(4, T.qp, T.sp, 0, T.qh, T.sh, 0, MID, r=["qp", "qh"])
+    spread(T.d0k, E, 0, BIG, ["d0k"])
+    unpack(0, HALO0, False)
+    quant(T.qc, T.sc, 0, 256, T.ct, r=["ct0", "ct1"], w=["qc"])
+    scan(T.sk[:, 0:MID], T.d0h[:], bank(4, 0, MID), A.add, A.max, r=["d0h"], w=["p4"] + sks)
+
     OWN = {"a": (0, AB), "b": (AB, EB), "l": (EB, NB)}
-    KEYS = {"a": (1, 0, 16 * AB), "b": (6, 16 * EB - 128, 16 * EB), "l": (7, E - 128, E),
-            "ab": (2, 0, 16 * EB), "abl": (3, 0, 16 * (DC - 1))}
-    SCORE = {"a": 0, "b": 4, "l": 5}
+    SCORE = {"a": 7, "b": 0, "l": 1}
+    SUM, HALO = 2, ((0, 3), (1, 0), (2, 1), (3, 7))
+
+    def row(t, part):
+        top = max(c for c in range(NB) if c not in DVS[t])
+        return {"a": (4, 0, 16 * AB), "b": (5, 0, 16 * EB), "l": (7, E - 128, E), "all": (6, 0, 16 * top)}[part]
 
     def score(t, part):
         a, b = PART[part]
@@ -346,212 +371,291 @@ def rank_program(g, core, T, topo):
         quant(T["qd%d" % t], T["sd%d" % t], a, max(b, a + 128), dg,
               r=["dg0o", "dg0l", "dg3", "dgp", "dg1" + part, "dg2" + part], w=["qd%d%s" % (t, part)])
 
-    def keys(t, row, old):
-        k, lo, hi = KEYS[row]
+    def keys(t, part, old):
         terms = {(1, False): ((0, 0), (1, 2)), (2, True): ((3, 2), (1, 6)), (2, False): ((2, 0), (0, 4))}.get((t, old), ())
         u = t - old
-        have = "abl" if old else {"b": "ab", "l": "bl"}.get(row, row)
+        have = "abl" if old else {"a": "a", "b": "ab", "l": "bl", "all": "abl"}[part]
         for i, (c, d) in enumerate(terms):
+            k, lo, hi = row(t, part)
             mm(k, T.qk, T.sk8, 128 * c, T["qd%d" % u], T["sd%d" % u], lo + d, hi + d,
                r=["qk%d" % c] + ["qd%d%s" % (u, p) for p in have], start=i == 0 and (old or t == 1), stop=i == 1 and not old)
 
-    def tied(t, part):
-        a, b = (16 * c for c in OWN[part])
-        k, lo, _ = KEYS[part]
-        tt(T["kt%d" % t][:, a:b], bank(k, a - lo, b - lo), T["tie%d" % t][:, a:b], A.add, r=["p%d" % k, "tie%d" % t], w=["tied." + part])
-
     def hold(t, part):
         a, b = (16 * c for c in OWN[part])
-        k, lo, _ = KEYS[part]
-        if part == "l":
-            scan(T.sk[:, a:b], T.d0k[:, a:b], T["kt%d" % t][:, a:b], A.add, A.max, r=["d0k", "tied.l"], w=["sk.l"])
-        else:
-            scan(T.sk[:, a:b], T.d0k[:, a:b], bank(k, a - lo, b - lo), A.add, A.max, r=["d0k", "p%d" % k], w=["sk." + part])
+        k, lo, _ = row(t, part)
+        scan(T.sk[:, a:b], T.d0k[:, a:b], bank(k, a - lo, b - lo), A.add, A.max, r=["d0k", "p%d" % k], w=["sk." + part])
+
+    def tied(t, part):
+        a, b = (16 * c for c in OWN[part])
+        k, lo, _ = row(t, part)
+        tt(T["kt%d" % t][:, a:b], bank(k, a - lo, b - lo), T["tie%d" % t][:, a:b], A.add, r=["p%d" % k] + tie_of[t], w=["tied." + part])
 
     def owned(t, part):
         c0, c1 = OWN[part]
+        c1 = min(c1, NB - 1)
         ts(T.kw[:, c0:c1], T.sk[:, 16 * c0 + 15:16 * c1:16], col[:, 0:1], STEP[t], A.subtract, A.add, r=["sk." + part, "col0"], w=["kw." + part])
+        if part == "l":
+            ts(T.kw[:, c1:NB], T.sk[:, E - 1:E], T.cc[:, 31 + t:32 + t], STEP[t], A.add, A.add, r=["sk.l", "cc%d" % t], w=["kw.z"])
 
-    def inside(t, parts):
-        c0, c1 = OWN[parts[0]][0] // 2 * 2, OWN[parts[-1]][1]
+    def inside(t, part):
+        c0, c1 = (0, EB) if part == "ab" else (EB - 1, NB)
         o = 4 * TOFF[TD]
         tt(T.tb[:, o + 64 * c0:o + 64 * c1:4], T.kw[:, 0:c1].indirect(T.od[:, c0:c1]), T["kt%d" % t][:, 16 * c0:16 * c1], A.is_gt,
-           r=["kw." + p for p in "abl" if OWN[p][0] < c1] + ["tied." + p for p in "abl" if OWN[p][0] < c1] + ["od"],
-           w=["in.a", "in.b"] if parts[0] != "a" else ["in.a"])
+           r=["kw.a", "kw.b", "tied.a", "tied.b", "od"] + ["kw.l", "kw.z", "tied.l"] * (part == "l"), w=["in.a", "in.b"][:1 + (part == "l")])
 
-    def compare(t, c):
+    def lane(c):
         k = [c in cs for cs, _ in TILES].index(True)
         j = TILES[k][0].index(c)
         o = 4 * TOFF[k] + j
-        part = "l" if c >= EB else "b" if c >= AB else "a"
-        out = T.tb[:, o:o + 64 * c - j:4]
-        if c >= DC:
-            ts(out, T["kt%d" % t][:, 0:16 * c], T.kw[:, c:c + 1], 0.5, A.is_le, A.subtract, r=tieds + ["kw.l"], w=["tb%d.%d" % (k, j)])
+        return k, T.tb[:, o:o + 64 * c - j:4], "tb%d.%d" % (k, j)
+
+    def compare(t, cs, mine):
+        for c in cs:
+            if (c in DVS[t]) != mine:
+                continue
+            _, out, tok = lane(c)
+            own = "kw.z" if c == NB - 1 else "kw.l" if c >= EB else "kw.b" if c >= AB else "kw.a"
+            if mine:
+                ts(out, T["kt%d" % t][:, 0:16 * c], T.kw[:, c:c + 1], 2.0, A.is_le, A.mult,
+                   r=["tied." + p for p in "abl" if OWN[p][0] < c] + [own], w=[tok])
+            else:
+                kb = row(t, "a" if c <= AB else "b" if c <= EB else "all")[0]
+                act(out, bank(kb, 0, 16 * c), F.Sign, scale=-1.0, bias=T.kw[:, c:c + 1], accum_out=T.rw[:, c:c + 1],
+                    r=["p%d" % kb, own, "tied.a"] + ["tied.b"] * (c > AB), w=[tok, "rw%d" % c] + ["rw0"] * (c == 1))
+
+    def above(t, c):
+        return len([x for x in DVS[t] if x > c])
+
+    def rowsum(t, cs):
+        for c in cs:
+            if c in DVS[t]:
+                _, x, tok = lane(c)
+                i = DVS[t].index(c) + 1
+                scan(T.jk[:, E * i - 16 * c:E * i], x, T.zr[:, 0:16 * c], A.add, A.add, r=[tok, "zr"], w=["rw%d" % c],
+                     first=16.0 * (above(t, c) - c))
+
+    def fold(c, sums, stop=False):
+        k = lane(c)[0]
+        quant(T.qt, T.st, TOFF[k], TOFF[k] + TILES[k][1], T.tb, r=["tb%d.%d" % (k, j) for j in four] + ["in.a", "in.b"] * (k == TD), w=["qt%d" % k])
+        for x in sums:
+            k = lane(x)[0]
+            mm(SUM, T.qc, T.sc, 128 if k == TD else 0, T.qt, T.st, TOFF[k], TOFF[k] + (E if k == TF else TILES[k][1]),
+               r=["qc", "qt%d" % k, "qt.z"], start=k == TF, stop=stop)
+
+    def rows(t, c0):
+        c1 = min(c for c in range(c0, NB + 1) if c == NB or (c in DVS[t]) != (c0 in DVS[t]))
+        out = T.d1k[:, 16 * c0 + 16:16 * c1 + 1:16]
+        rs = ["rw%d" % c for c in range(c0, c1)] + ["off", "d1k"]
+        if c0 in DVS[t]:
+            i = DVS[t].index(c0)
+            ts(out, T.jk[:, E * i + E - 1:E * (i + c1 - c0):E], 0.5, T.off[:, 0:1], A.mult, A.add, r=rs, w=["rc%d" % c0])
         else:
-            kb = KEYS["a" if c <= AB else "ab" if c <= EB else "abl"][0]
-            act(out, bank(kb, 0, 16 * c), F.Sign, scale=-1.0, bias=T.kw[:, c:c + 1], accum_out=T.rw[:, c:c + 1],
-                r=["p%d" % kb, "kw." + part, "tied.a"], w=["tb%d.%d" % (k, j), "rw%d" % c])
-
-    def rowsum(c):
-        j, i = TILES[TD][0].index(c), c - DC + 1
-        o = 4 * TOFF[TD] + j
-        scan(T.jk[:, E * i - 16 * c:E * i], T.tb[:, o:o + 64 * c - j:4], T.zr[:, 0:16 * c], A.add, A.add,
-             r=["tb%d.%d" % (TD, j), "zr"], w=["jk%d" % i])
-
-    def fold(k, start=False, stop=False):
-        wd = TILES[k][1]
-        quant(T.qt, T.st, TOFF[k], TOFF[k] + wd, T.tb, r=["tb%d.%d" % (k, j) for j in four] + ["in.a", "in.b"] * (k == TD), w=["qt%d" % k])
-        mm(6, T.qc, T.sc, 128 if k == TD else 0, T.qt, T.st, TOFF[k], TOFF[k] + (E if start else wd),
-           r=["qc", "qt%d" % k, "qt.z0", "qt.z1"], start=start, stop=stop)
+            n = above(t, c0)
+            ts(out, T.rw[:, c0:c1], 0.5, T.off[:, n:n + 1], A.mult, A.add, r=rs, w=["rc%d" % c0])
+        return "rc%d" % c0
 
     def order(t):
-        for c in range(AB, EB):
-            compare(t, c)
-        inside(t, "ab")
+        top = min(c for c in DVS[t] if c >= EB)
+        compare(t, (15, 16, 17, 18, 11, 12, 13, 14), False)
+        rowsum(t, (3,))
         signs(t, "l")
+        fold(3, ())
+        rowsum(t, (4,))
         digits(t, "l")
         keys(t, "l", False)
-        keys(t, "abl", False)
-        fold(TF, start=True)
-        tied(t, "l")
+        keys(t, "all", False)
+        inside(t, "ab")
+        fold(7, ())
+        rowsum(t, (5,))
         hold(t, "l")
-        unpack(t, (4, 5, 0, 7), True)
+        tied(t, "l")
+        rowsum(t, (6,))
         owned(t, "l")
-        fold(2)
-        for c in list(range(DC - 1, EB - 1, -1)) + [6, 5, 4, 3, 2, 1]:
-            compare(t, c)
-        for c in range(DC, NB):
-            compare(t, c)
+        compare(t, range(NB - 1, EB - 1, -1), False)
+        compare(t, (2, 1), False)
+        fold(15, (15, 7, 3))
+        unpack(t, HALO, True)
+        act(T["vh%d" % t][:, 0:4 * C], T.x32[:], F.Copy, scale=0.015625, r=xs[0] + xs[1], w=["vh%d" % t])
+        unpack(t, HALO, False)
+        compare(t, (25, 24, 23, 22), True)
         inside(t, "l")
-        fold(3)
-        for c in range(DC, NB):
-            rowsum(c)
-        fold(TD)
-        fold(4)
-        ts(T.d1k[:, 16 * DC + 15:E:16], T.jk[:, E - 1:(NB - DC) * E:E], -2.0, col[:, 8:9], A.mult, A.add,
-           r=["jk%d" % i for i in range(1, NB - DC + 1)] + ["col8", "d1k"], w=["rc1"])
-        fold(5)
-        fold(1, stop=True)
-        unpack(t, (4, 5, 0, 7), False)
-        act(T["vh%d" % t][:, 0:4 * C], T.x32[:], F.Copy, scale=0.015625, r=xs[0] + xs[1], w=["vh%d.0" % t, "vh%d.1" % t])
-        ts(T.d1k[:, 15:16 * DC:16], T.rw[:, 0:DC], -1.0, col[:, 8:9], A.mult, A.add, r=["rw%d" % c for c in range(DC)] + ["col8", "d1k"], w=["rc0"])
-        scan(T.sk[:], bank(6, 0, E), T.d1k[:], A.max, A.add, r=["d1k", "rc0", "rc1"], w=["p6"] + sks, first=-BIG)
+        fold(11, (11,))
+        rowsum(t, (25,))
+        fold(25, (25,))
+        rowsum(t, (24,))
+        fold(19, (19,))
+        fold(1, (1,), stop=True)
+        rowsum(t, (23, 22))
+        rcs = [rows(t, c) for c in (3, 0, 7, top)]
+        scan(T.ps[:], bank(SUM, 0, E), T.d1k[:, 1:E + 1], A.max, A.add, r=["d1k"] + rcs, w=["ps", "p%d" % SUM], first=-BIGP)
 
     for t in range(R):
         vh = T["vh%d" % t]
         last = t == R - 1
+        u = t + 1
         if t:
             order(t)
-            ts(T.pos[:, 0:NB], T.sk[:, 15:E:16], col[:, 10:11], -0.5, A.subtract, A.mult, r=sks + ["col10"], w=["pos"])
-            ts(T.onm[:, 0:20], T.sk[:, 15:C:16], col[:, 11:12], -0.5, A.subtract, A.mult, r=sks + ["col10"], w=["on"])
+            x, y, c0, c1, rs = T.ps[:, 15:E:16], T.ps[:, 15:C:16], col[:, 10:11], col[:, 11:12], ["ps", "col10", "col11"]
         else:
-            unpack(0, (5, 6, 7, 0), True)
-            unpack(0, (5, 6, 7, 0), False)
-            act(T.x32[:], T.xt[:], F.Copy, scale=32.0, r=x0 + x1, w=xs[0] + xs[1])
-            ts(T.pos[:, 0:NB], T.sk[:, 7:MID:8], col[:, 1:2], 1.0, A.subtract, A.subtract, r=sks + ["col0"], w=["pos"])
-            ts(T.onm[:, 0:20], T.sk[:, 7:C // 2:8], col[:, 1:2], 2.0, A.subtract, A.subtract, r=sks + ["col0"], w=["on"])
+            x, y, c0, c1, rs = T.sk[:, 7:MID:8], T.sk[:, 7:C // 2:8], col[:, 1:2], col[:, 1:2], sks + ["col0"]
+        z = float(t == 0)
+        ts(T.pos[:, 0:NB], x, c0, z, A.subtract, A.subtract, r=rs, w=["pos"])
+        ts(T.onm[:, 20:40], y, c1, E - 1.0, A.subtract, A.min, r=rs, w=["om"])
+        ts(T.onm[:, 0:20], y, c0, z + 1.0, A.subtract, A.subtract, r=rs, w=["on"])
         cp(T.ordr[:, 0:E].indirect(T.pos[:, 0:NB]), T.ic[:], r=["pos", "ic"], w=["ordr"])
-        ts(T.onm[:, 20:40], T.pos[:, 0:20], 1.0, E - 1.0, A.add, A.min, r=["pos"], w=["om"])
-        act(T.gn[:], T.ordr[:, 0:E].indirect(T.onm[:, 0:20]), F.Copy, r=["ordr", "on"], w=["gn"])
-        cp(T.gm[:], T.ordr[:, 0:E].indirect(T.onm[:, 20:40]), r=["ordr", "om"], w=["gm"])
-        if last:
-            scan(T.sk[:], T.d0k[:], T.ordr[:], A.add, A.max, r=["d0k", "ordr"], w=sks)
-        else:
-            quant(T.qk, T.sk8, 256 * t, 256 * t + 128, T.kt, r=["kt%d" % (2 * t)], w=["qk%d" % (2 * t)])
-        scan(T.sm[:], T.d0v[:], T.gm[:], A.add, A.max, r=["gm", "d0v"], w=["sm"])
-        scan(T.sn[:], T.d0v[:], T.gn[:], A.add, A.max, r=["gn", "d0v"], w=["sn"])
-        ts(T.ov[:, 80:160], T.sm[:, 3:C:4], 4.0, col[:, 3:4], A.mult, A.add, r=["sm", "col3"], w=["ovm"])
-        if last:
-            ts(T.ow[:, 0:NB], T.sk[:, 15:E:16], col[:, 0:1], 1.0 * MID, A.subtract, A.add, r=sks + ["col0"], w=["ow"])
-        ts(T.ov[:, 0:80], T.sn[:, 3:C:4], 4.0, col[:, 3:4], A.mult, A.add, r=["sn", "col3"], w=["ovn"])
         if not last:
-            quant(T.qk, T.sk8, 256 * t + 128, 256 * t + 256, T.kt, r=["kt%d" % (2 * t + 1)], w=["qk%d" % (2 * t + 1)])
-        vr = ["vh%d.0" % t, "vh%d.1" % t] + ["vh%d.h%d" % (t, b) for b in four]
-        pieces = PIECES
-        for k, (a, b) in enumerate(pieces):
-            act(T.g1[:, 4 * a:4 * b], vh[:, 0:4 * E].indirect(T.ov[:, 80 + a // 4:80 + b // 4]), F.Copy, r=vr + ["ovm"], w=["g1.%d" % k])
-        act(T.g3[:, 4 * G3:4 * C], vh[:, 0:4 * E].indirect(T.ov[:, G3 // 4:80]), F.Copy, r=vr + ["ovn"], w=["g3b"])
-        if last:
-            act(T.ks[:], T.kt2[:, 0:E].indirect(T.ow[:, 0:NB]), F.Copy, scale=512.0, r=tieds + ["ow"], w=["ks"])
-        cp(T.g3[:, 4 * C0:4 * G3], vh[:, 0:4 * E].indirect(T.ov[:, C0 // 4:G3 // 4]), r=vr + ["ovn"], w=["g3a"])
+            ties(u, 0)
+            if t == 0:
+                act(dg[:, 3:4 * E:4], dg[:, 0:4 * E:4], F.Sign, scale=-1.0, bias=dg[:, 4 * E - 4:4 * E - 3], r=["dg0o", "dg0l"], w=["dg3"])
+                gap(3)
+            else:
+                weights(2)
+            ties(u, 1)
+        for h, (a, b) in enumerate(CH):
+            act(T.gn[:, a:b], T.ordr[:, 0:E].indirect(T.onm[:, a // 16:b // 16]), F.Copy, r=["ordr", "on"], w=["gn%d" % h])
+            cp(T.gm[:, a:b], T.ordr[:, 0:E].indirect(T.onm[:, 20 + a // 16:20 + b // 16]), r=["ordr", "om"], w=["gm%d" % h])
+
+        def near(h, n):
+            a, b = CH[h]
+            scan(T["s" + n][:, a:b], T.d0v[:, a:b], T["g" + n][:, a:b], A.add, A.max, r=["g%s%d" % (n, h), "d0v"], w=["s%s%d" % (n, h)])
+
+        def offs(h, n):
+            a, b = CH[h]
+            o = 80 * (n == "m")
+            ts(T.ov[:, o + a // 4:o + b // 4], T["s" + n][:, a + 3:b:4], 4.0, col[:, 3:4], A.mult, A.add, r=["s%s%d" % (n, h), "col3"], w=["ov%s%d" % (n, h)])
+
+        vr = ["vh%d" % t] + ["vh%d.h%d" % (t, b) for b in four]
+
+        def pick(k, n):
+            a, b = PIECES[k]
+            o = 80 * (n == "m")
+            return vh[:, 0:4 * E].indirect(T.ov[:, o + a // 4:o + b // 4]), vr + ["ov%s%d" % (n, a >= C0)]
+
+        def gather(k, n):
+            a, b = PIECES[k]
+            x, rs = pick(k, n)
+            if n == "m":
+                act(T.g1[:, 4 * a:4 * b], x, F.Copy, r=rs, w=["g1.%d" % k])
+            elif MODE[k] == "A":
+                act(T.g3[:, 4 * a:4 * b], x, F.Copy, r=rs, w=["g3.%d" % k])
+            else:
+                cp(T.g3[:, 4 * a:4 * b], x, r=rs, w=["g3.%d" % k])
 
         def most(k):
-            a, b = pieces[k]
-            if a < C0:
-                tt(T.g2[:, 4 * a:4 * b], vh[:, 0:4 * E].indirect(T.ov[:, a // 4:b // 4]), T.g1[:, 4 * a:4 * b], A.max,
-                   r=vr + ["ovn", "g1.%d" % k], w=["g2.%d" % k])
-            else:
-                tt(T.g2[:, 4 * a:4 * b], T.g3[:, 4 * a:4 * b], T.g1[:, 4 * a:4 * b], A.max, r=["g3a", "g3b", "g1.%d" % k], w=["g2.%d" % k])
+            a, b = PIECES[k]
+            x, rs = pick(k, "n") if MODE[k] == "F" else (T.g3[:, 4 * a:4 * b], ["g3.%d" % k])
+            tt(T.g2[:, 4 * a:4 * b], x, T.g1[:, 4 * a:4 * b], A.max, r=rs + ["g1.%d" % k], w=["g2.%d" % k])
 
         def blend(k):
-            a, b = pieces[k]
+            a, b = PIECES[k]
             tt(T.zt[:, 4 * a:4 * b], T.g2[:, 4 * a:4 * b], vh[:, 4 * a:4 * b], A.add, r=["g2.%d" % k] + vr, w=["zt%d" % k])
 
-        def layer(h, ks):
+        def pack(h):
             a, b = CH[h]
-            quant(T.qz, T.sz, a, b, T.zt, r=["zt%d" % k for k in ks], w=["qz%d" % h])
-            for j in four:
-                mm(4 * h + j, T.qw, T.sw, 128 * j, T.qz, T.sz, a, b, r=["qw", "sw", "qz%d" % h])
+            quant(T.qz, T.sz, a, b, T.zt, r=["zt%d" % k for k, p in enumerate(PIECES) if a <= p[0] < b], w=["qz%d" % h])
+
+        def layer(h, js):
+            a, b = CH[h]
+            for j in js:
+                mm(j, T.qw, T.sw, 128 * j, T.qz, T.sz, a, b, r=["qw", "sw", "qz%d" % h])
 
         def state(h, js):
             a, b = CH[h]
             for j in js:
                 x = T.x32[:, 4 * a + j:4 * b:4]
-                tt(x, bank(4 * h + j, 0, b - a), x, A.add, w=["p%d" % (4 * h + j), "x32.%d.%d" % (h, j)])
+                tt(x, bank(j, 0, b - a), x, A.add, w=["p%d" % j, "x32.%d.%d" % (h, j)])
                 if j < 2:
                     act(T.xt[:, 4 * a + j:4 * b:4], x, F.Copy, scale=0.03125, r=["x32.%d.%d" % (h, j)], w=["xt.%d.%d" % (h, j)])
 
-        def shrink(h):
+        def shrink(h, j):
             a, b = CH[h]
-            for j in (2, 3):
-                ts(T.xt[:, 4 * a + j:4 * b:4], T.x32[:, 4 * a + j:4 * b:4], 0.03125, None, A.mult, r=["x32.%d.%d" % (h, j)], w=["xt.%d.%d" % (h, j)])
+            ts(T.xt[:, 4 * a + j:4 * b:4], T.x32[:, 4 * a + j:4 * b:4], 0.03125, None, A.mult, r=["x32.%d.%d" % (h, j)], w=["xt.%d.%d" % (h, j)])
 
-        u = t + 1
-        q2, s2, qm = T["q%d" % u], T["s%d" % u], "q%d" % u
+        def fresh(h):
+            a, b = CH[h]
+            quant(T["q%d" % u], T["s%d" % u], a, b, T.xt, r=(x0, x1)[h], w=["q%d.%d" % (u, h)])
+
+        near(0, "m")
+        near(0, "n")
+        near(1, "m")
+        offs(0, "m")
+        for k in (0, 2, 1, 3):
+            gather(k, "m")
+        near(1, "n")
+        offs(0, "n")
+        if last:
+            scan(T.sk[:], T.d0k[:], T.ordr[:], A.add, A.max, r=["d0k", "ordr"], w=sks)
+        elif t == 1:
+            weights(3)
+        else:
+            quant(T.qv, T.sv, 0, 128, T.vt, r=["vt"], w=["qv"])
+        for part in ("a", "b", "all"):
+            keys(u, part, True)
+        offs(1, "m")
+        offs(1, "n")
+        gather(1, "n")
+        gather(4, "m")
+        gather(5, "n")
+        gather(5, "m")
         most(0)
-        most(1)
-        blend(0)
+        if last:
+            ts(T.ow[:, 0:NB], T.sk[:, 15:E:16], col[:, 0:1], 1.0 * MID, A.subtract, A.add, r=sks + ["col0"], w=["ow"])
+            act(T.ks[:], T.kt2[:, 0:E].indirect(T.ow[:, 0:NB]), F.Copy, scale=512.0, r=tieds + ["ow"], w=["ks"])
         most(2)
-        blend(1)
-        blend(2)
+        blend(0)
+        most(1)
         most(3)
-        layer(0, (0, 1, 2))
+        blend(2)
+        blend(1)
         blend(3)
-        state(0, (0,))
-        layer(1, (3,))
-        state(0, (1, 2, 3))
-        state(1, (0, 1))
-        shrink(0)
-        state(1, (2, 3))
+        most(4)
+        pack(0)
+        layer(0, four)
+        most(5)
+        blend(4)
+        blend(5)
+        state(0, (0, 1))
+        pack(1)
+        layer(1, (0, 1))
+        state(0, (2, 3))
+        layer(1, (2, 3))
+        shrink(0, 2)
+        if t == 0:
+            weights(0)
+        state(1, (0,))
+        shrink(0, 3)
+        state(1, (1,))
+        if not last:
+            missing(u, 0)
+        fresh(0)
         if last:
             break
-        if t == 0:
-            ties(2)
-            act(T.kt[:, 1024:1536], T.kt[:, 0:512], F.Copy, scale=HIGH, r=["kt0"], w=["kt2"])
-        keys(u, "a", True)
-        keys(u, "abl", True)
-        quant(q2, s2, 0, C0, T.xt, r=x0, w=[qm + ".0"])
         send(u)
         score(u, "a")
-        shrink(1)
-        keys(u, "b", True)
-        quant(q2, s2, C0, C, T.xt, r=x1, w=[qm + ".1"])
-        score(u, "b")
-        keys(u, "ab", True)
+        state(1, (2, 3))
+        if t == 0:
+            act(T.kt[:, 1024:1536], T.kt[:, 0:512], F.Copy, scale=HIGH, r=["kt0"], w=["kt2"])
+            spread(T.d1k, E + 16, 0, BIGP, ["d1k"])
+            act(T.off[:], jm[:, 0:16], F.Identity, scale=8.0, bias=col[:, 8:9], r=["jm0", "col8"], w=["off"])
+            weights(1)
+        shrink(1, 2)
+        shrink(1, 3)
         signs(u, "a")
+        fresh(1)
+        score(u, "b")
+        missing(u, 1)
         digits(u, "a")
         keys(u, "a", False)
         signs(u, "b")
         digits(u, "b")
         keys(u, "b", False)
         keys(u, "l", True)
-        keys(u, "ab", False)
         score(u, "l")
         hold(u, "a")
         tied(u, "a")
         owned(u, "a")
-        for c in (10, 9, 8, 7):
-            compare(u, c)
+        compare(u, (10, 9, 8, 7), False)
+        compare(u, (3, 4, 5, 6), True)
         hold(u, "b")
         tied(u, "b")
         owned(u, "b")
@@ -559,21 +663,29 @@ def rank_program(g, core, T, topo):
 
     def leave(h):
         a, b = CH[h]
-        quant(q, s, a, b, T.xt, r=(x0, x1)[h], w=["q3.%d" % h])
-        mm(h, T.qv, T.sv, 0, q, s, a, b, r=["qv", "q3.%d" % h])
+        mm(4 + h, T.qv, T.sv, 0, q, s, a, b, r=["qv", "q3.%d" % h])
         dma("sp", T.oc[:, 4 * a:4 * b], q[:, a:b].bitcast(dt.uint8), r=["q3.%d" % h])
 
+    def result(h):
+        a, b = CH[h]
+        act(T.ys[:, a:b], bank(4 + h, 0, b - a), F.Copy, w=["p%d" % (4 + h), "ys%d" % h])
+
     leave(0)
-    shrink(1)
-    tt(T.dk[:, 1:E], T.ks[:, 1:E], T.ks[:, 0:E - 1], A.subtract, r=["ks"], w=["dk"])
+    state(1, (2, 3))
+    result(0)
+    dma("act", T.y[:, 0:C0], T.ys[:, 0:C0], r=["ys0"])
+    shrink(1, 2)
+    tt(T.dk[:, 1:MID], T.ks[:, 1:MID], T.ks[:, 0:MID - 1], A.subtract, r=["ks"], w=["dk0", "dk1"])
+    shrink(1, 3)
+    tt(T.dk[:, MID:E], T.ks[:, MID:E], T.ks[:, MID - 1:E - 1], A.subtract, r=["ks"], w=["dk2"])
+    fresh(1)
     leave(1)
-    scan(T.ls[:], T.dk[:], T.ic[:], A.add, A.min, r=["dk", "dk0", "ic"], w=["ls"])
+    scan(T.ls[:], T.dk[:], T.ic[:], A.add, A.min, r=["dk1", "dk2", "ic"], w=["ls"])
     for k in four:
-        dma("sp", T.osc[4 * k:4 * k + 4, :], s[32 * k:32 * k + 4, 0:C], r=["q3.0", "q3.1"])
+        dma(("sp", "act")[k // 2], T.osc[4 * k:4 * k + 4, :], s[32 * k:32 * k + 4, 0:C], r=["q3.0", "q3.1"])
+    result(1)
     ts(T.lr[:], T.ls[:, 0:E].indirect(T.pos[:, 0:NB]), 1.0 * MID, None, A.add, r=["ls", "pos"], w=["lr"])
-    for h, (a, b) in enumerate(CH):
-        act(T.ys[:, a:b], bank(h, 0, b - a), F.Copy, w=["p%d" % h, "ys%d" % h])
-        dma("act", T.y[:, a:b], T.ys[:, a:b], r=["ys%d" % h])
+    dma("act", T.y[:, C0:C], T.ys[:, C0:C], r=["ys1"])
     dma("sp", T.lv[:], T.lr[15:128:16, :], r=["lr"])
     for sname, v in cnt.items():
         g.wait_ge(T.sem[sname], v)

@@ -4,15 +4,17 @@ A = AluOpType
 F = ActivationFunctionType
 C, H, E, R = 320, 96, 416, 3
 C0 = 192
-PIECES, MODE = ((0, 32), (32, 80), (80, 144), (144, C0), (C0, 256), (256, C)), "FDFFFA"
+PIECES, MODE = ((0, 48), (48, 88), (88, 136), (136, C0), (C0, 248), (248, C)), "FDFFFA"
 EP = C + 128
 NB, AB, EB = 26, 11, 19
 RADIX, HIGH = 36.0, 4096.0
 STEP = (0.0, 1.0, 0.5)
 NONE1, NONE2 = -34.0, -1200.0
 BIG, BIGP, BIGV = 11010048.0, 4096.0, 512.0
-SPLIT = 805306368.0
+MEM, LIFT = 1024.0, 2048.0
+TINY, LOW = 1e-37, 2.0 ** -13
 MID = E // 2
+LV = 256
 TILES = (((0, 25, 24, 23), 416), ((1, 2), 128), ((3, 4, 5, 6), 128), ((11, 12, 13, 14), 224), ((7, 8, 9, 10), 160),
          ((19, 20, 21, 22), 352), ((15, 16, 17, 18), 288))
 TD, TF = 0, 6
@@ -28,26 +30,26 @@ def _sb(n, d):
 SCRATCH = {
     "xt": _sb(4 * C, BF), "x32": _sb(4 * C, BF), "ut": _sb(512, BF), "vt": _sb(512, BF),
     "qw": _sb(512, Q4), "sw": _sb(512, U8), "qu": _sb(128, Q4), "su": _sb(128, U8),
-    "qa": _sb(128, Q4), "sa": _sb(128, U8), "qb": _sb(128, Q4), "sb": _sb(128, U8), "qv": _sb(128, Q4), "sv": _sb(128, U8),
-    "one": _sb(516, BF), "et": _sb(516, BF), "qe": _sb(512, Q4), "se": _sb(512, U8),
-    "ct": _sb(1024, BF), "qc": _sb(256, Q4), "sc": _sb(256, U8), "tp": _sb(512, BF), "qp": _sb(128, Q4), "sp": _sb(128, U8),
+    "qa": _sb(256, Q4), "sa": _sb(256, U8), "qv": _sb(128, Q4), "sv": _sb(128, U8),
+    "et": _sb(516, BF), "qe": _sb(512, Q4), "se": _sb(512, U8),
+    "ct": _sb(1024, BF), "qc": _sb(256, Q4), "sc": _sb(256, U8),
     "kt": _sb(2048, BF), "qk": _sb(512, Q4), "sk8": _sb(512, U8),
-    "pi": _sb(8, I32), "ci": _sb(8, I32), "cf": _sb(8, F32), "jm": _sb(80, BF), "df": _sb(48, BF), "ta": _sb(48, BF),
-    "tc": _sb(48, BF), "tab": _sb(64, BF), "col": _sb(16, F32), "off": _sb(16, F32), "cc": _sb(36, F32),
+    "pi": _sb(8, I32), "ci": _sb(8, I32), "cf": _sb(8, F32), "jm": _sb(196, BF), "df": _sb(32, BF), "ta": _sb(32, BF),
+    "tc": _sb(32, BF), "tab": _sb(48, BF), "t64": _sb(64, BF), "col": _sb(16, F32), "off": _sb(16, F32), "cc": _sb(36, F32),
     "ic": _sb(E, BF), "zr": _sb(512, BF),
-    "oab": _sb(16, U16), "orr": _sb(32, U16), "od": _sb(32, U16), "og": _sb(32, U16), "op": _sb(32, U16), "o2": _sb(32, U16),
-    "d0k": _sb(E, BF), "d0h": _sb(MID, BF), "d0v": _sb(C, BF), "d1k": _sb(E + 16, F32), "tie1": _sb(E, BF), "tie2": _sb(E, F32),
+    "oab": _sb(16, U16), "orr": _sb(32, U16), "od": _sb(32, U16), "o64": _sb(52, U16),
+    "d0k": _sb(E, BF), "d0t": _sb(2 * E, BF), "d0p": _sb(E, BF), "d0v": _sb(C, BF), "d1k": _sb(E + 16, F32),
+    "tie1": _sb(E, BF), "tie2": _sb(E, F32),
     "ab": _sb(E, BF), "a2": _sb(E, BF), "a8": _sb(H, BF), "b4": _sb(H, BF), "wb": _sb(E + 16, BF), "mb": _sb(E, BF),
     "dg": _sb(4 * EP, BF), "qd1": _sb(EP, Q4), "sd1": _sb(EP, U8), "qd2": _sb(EP, Q4), "sd2": _sb(EP, U8),
-    "oh": _sb(E, BF), "oh2": _sb(E, F16), "pre": _sb(E, F16), "sel": _sb(E, F16), "hl": _sb(2 * E, BF),
-    "qh": _sb(MID, Q4), "sh": _sb(MID, U8), "junk": _sb(E, BF), "acc": _sb(8, F32),
+    "zf": _sb(3 * E, F16), "tz": _sb(2 * E + 66, F16), "th": _sb(2 * E, F16), "junk": _sb(E, BF), "acc": _sb(8, F32),
     "kt1": _sb(E, F16), "kt2": _sb(E, F32), "jk": _sb(8 * E, F16),
     "sk": _sb(E, F32), "ps": _sb(E, F32), "kw": _sb(32, F32), "rw": _sb(32, F32),
     "tb": _sb(4 * TOFF[-1], BF), "qt": _sb(TOFF[-1] + 128, Q4), "st": _sb(TOFF[-1] + 128, U8),
     "pos": _sb(32, U16), "onm": _sb(40, U16), "ordr": _sb(E, BF), "gn": _sb(C, BF), "gm": _sb(C, BF),
     "sn": _sb(C, F16), "sm": _sb(C, F16), "ov": _sb(160, U16),
     "g1": _sb(4 * C, BF), "g3": _sb(4 * C, BF), "g2": _sb(4 * C, BF), "zt": _sb(4 * C, BF), "qz": _sb(C, Q4), "sz": _sb(C, U8),
-    "ow": _sb(32, U16), "ks": _sb(E, F32), "dk": _sb(E, F32), "ls": _sb(E, F32), "lr": _sb(E, F32), "ys": _sb(C, F32),
+    "ow": _sb(32, U16), "ks": _sb(E, F32), "dk": _sb(E, BF), "ls": _sb(E, BF), "lr": _sb(E, F32), "ys": _sb(C, F32),
     "pa": ("psum", [128, 2048], F32), "pb": ("psum", [128, 2048], F32),
 }
 for _t in range(R):
@@ -131,12 +133,18 @@ def rank_program(g, core, T, topo):
     def scan(out, d0, d1, o0, o1, r=(), w=(), first=0.0):
         op("dve", lambda: V.tensor_tensor_scan(out, d0, d1, first, o0, o1), r, w)
 
+    def turn(out, in_, r, w):
+        op("dve", lambda: V.transpose(out, in_), r, w)
+
     def quant(q, s, a, b, tile, r=(), w=(), at=None):
         lo = 4 * a if at is None else at
         op("dve", lambda: V.quantize_mx(q[:, a:b], s[:, a:b], tile[:, lo:lo + 4 * (b - a)]), r, w)
 
     def act(out, in_, func, r=(), w=(), **kw):
         op("act", lambda: S.activation(out, in_, func, **kw), r, w)
+
+    def lin(out, in_, scale, bias, r, w):
+        act(out, in_, F.Identity, r, w, scale=scale, bias=bias)
 
     def bank(k, a, b):
         return (T.pa, T.pb)[k // 4][:, 512 * (k % 4) + a:512 * (k % 4) + b]
@@ -151,8 +159,8 @@ def rank_program(g, core, T, topo):
         else:
             op("gp", lambda: g.iota(out, pat, base, cm), (), w)
 
-    def keep(out, in_, pat, cmp, base, cm, r, w):
-        op("gp", lambda: g.affine_select(out, in_, pat, cmp, 0.0, base, cm), r, w)
+    def keep(out, in_, n, base, fill, r, w):
+        op("gp", lambda: g.affine_select(out, in_, [[16, 8], [0, n // 8]], A.is_ge, fill, base, -1), r, w)
 
     def send(t):
         q, s = T["q%d" % t], T["s%d" % t]
@@ -163,15 +171,12 @@ def rank_program(g, core, T, topo):
         lastw["q%d.h" % t] = ("arr%d" % t, 2 * neng)
 
     def spread(out, n, k, scale, w):
-        act(out[:, 0:n], T.tab[:, 16 * k:16 * k + 16].indirect(T.orr[:, 0:n // 16]), F.Copy, scale=scale, r=["tab%d" % (k // 3), "orr"], w=w)
-
-    def block(out, lst, scale, w):
-        act(out, T.jm[:, 0:16].indirect(T[lst][:]), F.Copy, scale=scale, r=["jm0", lst], w=w)
+        act(out[:, 0:n], T.tab[:, 16 * k:16 * k + 16].indirect(T.orr[:, 0:n // 16]), F.Copy, scale=scale, r=["tab%d" % (k // 2), "orr"], w=w)
 
     def ties(t, step):
         tie = T["tie%d" % t]
         if step == 0:
-            spread(tie, E, 3, STEP[t], tie_of[t])
+            spread(tie, E, 2, STEP[t], tie_of[t])
             return
         for k, (a, c) in enumerate((((E - 2, NONE1),), ((E - 6, NONE1), (E - 4, NONE2), (E - 2, NONE2 + HIGH * NONE1)))[t - 1]):
             act(tie[:, a:a + 2], tie[:, a:a + 2], F.Identity, bias=c, w=["tie%d.%d" % (t, k)])
@@ -182,95 +187,102 @@ def rank_program(g, core, T, topo):
         else:
             ts(T.cc[:, 31 + t:32 + t], T.col[:, 0:1], -2.0, T.cc[:, 16 * t - 1:16 * t], A.mult, A.add, r=["col0", "cd%d" % t], w=["cc%d" % t])
 
+    def weave(h):
+        act(T.d0t[:, E * h:E * h + E], T.t64[:].indirect(T.o64[:, NB * h:NB * h + NB]), F.Copy, r=["t64.1", "t64.33", "o64"], w=["d0t%d" % h])
+
+    def diagonal(out, c, r, w):
+        op("gp", lambda: g.affine_select(out, T.zr[:, 0:128], [[1, 128]], A.not_equal, c, 0, -1), ["zr"] + r, w)
+
+    def diagonals(h):
+        for k, wt in enumerate((4 * RADIX, 2 * RADIX, 1.0, -2 * RADIX, 4.0, 2.0, 0.0, -2.0)):
+            o = 1024 * h + 512 * (k // 4)
+            diagonal(T.kt[:, o + k % 4:o + 512:4], wt * HIGH ** h, [], ["kt%d.%d" % (h, k)])
+
+    def weights(h):
+        quant(T.qk, T.sk8, 256 * h, 256 * h + 256, T.kt, r=["kt%d.%d" % (h, k) for k in range(8)], w=["qk%d" % h])
+
     def unit(b):
         quant(T.qe, T.se, 128 * b, 128 * (b + 1), T.et, r=["et"], w=["qe%d" % b], at=3 - b)
 
-    def weights(k):
-        quant(T.qk, T.sk8, 128 * k, 128 * k + 128, T.kt, r=["kt%d" % k], w=["qk%d" % k])
-
     CH = ((0, C0), (C0, C))
     PART = {"a": (0, C0), "b": (C0, C), "l": (C, E)}
-    cf, col, jm, dg = T.cf, T.col, T.jm, T.dg
+    cf, col, jm, dg, zf = T.cf, T.col, T.jm, T.dg, T.zf
     four = range(4)
     x0, x1 = (["xt.%d.%d" % (h, b) for b in four] for h in range(2))
     xs = [["x32.%d.%d" % (h, j) for j in four] for h in range(2)]
-    sks = ["sk.a", "sk.b", "sk.l"]
     tieds = ["tied.a", "tied.b", "tied.l"]
+    ins = ["in.a", "in.b", "in.l"]
     tie_of = [["tie%d.%d" % (t, k) for k in range(3)] for t in range(R)]
-    dfs = ["df%d" % k for k in range(3)]
+    dfs, poss = ["df0", "df1"], ["pos0", "pos1"]
     dma("sp", T.xt[:, 0:512], T.x[:, 0:512], w=x0)
-    dma("act", T.ut[:], T.u[:], w=["ut"])
+    dma("sp", T.ut[:], T.u[:], w=["ut"])
     dma("sp", T.xt[:, 512:4 * C], T.x[:, 512:4 * C], w=x1)
     iota(T.pi[:, 0:2], [[2, 2]], 0, 1, ["pi"], False)
+    iota(jm[:, 64:80], [[1, 2], [16, 8]], 0, 0, ["jm4"])
+    iota(jm[:, 80:144:2], [[2, 2], [0, 16]], -1, 0, ["jm5"])
+    iota(jm[:, 81:144:2], [[-2, 2], [0, 16]], 1, 0, ["jm6"])
+    iota(jm[:, 144:196], [[0, 13], [16, 4]], 0, 0, ["jm7"])
     iota(jm[:, 0:16], [[1, 16]], 0, 0, ["jm0"])
-    iota(jm[:, 48:80], [[1, 8], [0, 4]], 0, 0, ["jm3"])
-    iota(jm[:, 16:32], [[0, 2], [1, 8]], 0, 0, ["jm1"])
-    iota(jm[:, 32:48], [[0, 4], [1, 4]], 0, 0, ["jm2"])
-    ms(T.one[:], 1.0, w=["one"])
-    keep(T.et[:], T.one[:], [[1, 516]], A.is_equal, -3, -4, ["one"], ["et"])
-    for k, (sh, m) in enumerate(((0, 15), (1, 7), (2, 3), (0, 3), (4, 7))):
-        ts(T.ci[:, k:k + 1], T.pi[:, 0:1], sh, m, A.arith_shift_right, A.bitwise_and, r=["pi"], w=["ci%d" % k])
-    ts(T.ci[:, 5:6], T.pi[:, 1:2], 2, 1, A.arith_shift_right, A.bitwise_and, r=["pi"], w=["ci5"])
+    iota(jm[:, 16:32], [[0, 4], [1, 4]], 0, 0, ["jm1"])
     ms(T.zr[:], 0.0, w=["zr"])
-    cp(cf[:, 0:6], T.ci[:, 0:6], r=["ci%d" % k for k in range(6)], w=["cf"])
-    ts(T.oab[:, 0:8], jm[:, 0:8], 16.0, None, A.mult, r=["jm0"], w=["oa"])
-    ts(T.oab[:, 8:16], jm[:, 0:8], 16.0, 1.0, A.mult, A.add, r=["jm0"], w=["ob"])
+    for k, (sh, m) in enumerate(((0, 15), (2, 3), (0, 3), (4, 1))):
+        ts(T.ci[:, k:k + 1], T.pi[:, 0:1], sh, m, A.arith_shift_right, A.bitwise_and, r=["pi"], w=["ci%d" % k])
     ms(T.wb[:, E:E + 16], 0.0, w=["wb.p"])
-    ts(T.og[:], jm[:, 48:80], cf[:, 4:5], None, A.is_equal, r=["jm3", "cf"], w=["og"])
-    ts(col[:, 7:8], cf[:, 0:1], -7.5, None, A.add, r=["cf"], w=["col7"])
-    for k in range(3):
-        ts(T.df[:, 16 * k:16 * k + 16], jm[:, 16 * k:16 * k + 16], cf[:, k:k + 1], None, A.subtract, r=["jm%d" % k, "cf"], w=["df%d" % k])
-    ts(T.op[:], T.og[:], cf[:, 5:6], None, A.subtract, r=["og", "cf"], w=["op"])
-    ts(col[:, 4:7], jm[:, 0:3], -0.25, col[:, 7:8], A.mult, A.add, r=["jm0", "col7"], w=["col4"])
-    ts(T.ta[:], T.df[:], 0.0, -2.0, A.is_equal, A.mult, r=dfs, w=["ta"])
-    ts(T.tc[:], T.df[:], 1.0, None, A.is_equal, r=dfs, w=["tc"])
-    quant(T.qt, T.st, TOFF[-1], TOFF[-1] + 128, T.zr, r=["zr"], w=["qt.z"], at=0)
-    block(T.tp[:], "op", 0.5, ["tp"])
+    cp(T.oab[:], jm[:, 64:80], r=["jm4"], w=["oab"])
+    cp(cf[:, 0:4], T.ci[:, 0:4], r=["ci%d" % k for k in four], w=["cf"])
+    ms(T.et[:], 0.0, w=["et0"])
+    lin(col[:, 1:2], cf[:, 3:4], -2.0 * LIFT, LIFT, ["cf"], ["col1"])
+    lin(col[:, 7:8], cf[:, 0:1], 1.0, -7.5, ["cf"], ["col7"])
+    lin(col[:, 14:15], cf[:, 3:4], -LIFT, LIFT + 2.0, ["cf"], ["col14"])
+    lin(T.t64[:], jm[:, 80:144], col[:, 1:2], 0.0, ["jm5", "jm6", "col1"], ["t64"])
+    lin(col[:, 15:16], cf[:, 3:4], LIFT, 2.0, ["cf"], ["col15"])
+    lin(col[:, 4:7], jm[:, 0:3], -0.25, col[:, 7:8], ["jm0", "col7"], ["col4"])
+    for q, sg in ((1, 2.0), (33, -2.0)):
+        lin(T.t64[:, q:q + 1], col[:, 1:2], sg, -LIFT, ["col1", "t64"], ["t64.%d" % q])
     spare.extend([
+        lambda: ts(T.o64[:], jm[:, 144:196], cf[:, 0:1], None, A.add, r=["jm7", "cf"], w=["o64"]),
+        lambda: ts(T.df[:, 0:16], jm[:, 0:16], cf[:, 0:1], None, A.subtract, r=["jm0", "cf"], w=["df0"]),
+        lambda: ts(T.df[:, 16:32], jm[:, 16:32], cf[:, 1:2], None, A.subtract, r=["jm1", "cf"], w=["df1"]),
         lambda: ts(T.orr[:], T.zr[:, 0:32], cf[:, 0:1], None, A.add, r=["zr", "cf"], w=["orr"]),
-        lambda: ts(col[:, 9:10], cf[:, 3:4], 0.5, 1.0, A.is_lt, A.add, r=["cf"], w=["col9"]),
-        lambda: tt(T.tab[:, 0:48], T.ta[:], T.tc[:], A.add, r=["ta", "tc"], w=["tab0"]),
-        lambda: ts(T.tab[:, 48:64], T.df[:, 0:16], 0.0, None, A.is_gt, r=dfs, w=["tab1"]),
-        lambda: ts(T.o2[:], T.og[:], col[:, 9:10], None, A.mult, r=["og", "col9"], w=["o2"]),
-        lambda: ts(col[:, 0:2], T.df[:, 15:32:16], 0.0, BIG, A.is_gt, A.mult, r=dfs, w=["col0"]),
-        lambda: ts(col[:, 2:3], T.df[:, 47:48], 0.0, -4.0 * BIGV, A.is_gt, A.mult, r=dfs, w=["col2"]),
+        lambda: ts(T.ta[:], T.df[:], 0.0, -2.0, A.is_equal, A.mult, r=dfs, w=["ta"]),
+        lambda: ts(T.tc[:], T.df[:], 1.0, None, A.is_equal, r=dfs, w=["tc"]),
+        lambda: quant(T.qt, T.st, TOFF[-1], TOFF[-1] + 128, T.zr, r=["zr"], w=["qt.z"], at=0),
+        lambda: ts(col[:, 2:3], T.df[:, 31:32], 0.0, -4.0 * BIGV, A.is_gt, A.mult, r=dfs, w=["col2"]),
+        lambda: tt(T.tab[:, 0:32], T.ta[:], T.tc[:], A.add, r=["ta", "tc"], w=["tab0"]),
+        lambda: ts(T.tab[:, 32:48], T.df[:, 0:16], 0.0, None, A.is_gt, r=dfs, w=["tab1"]),
+        lambda: ts(col[:, 3:4], col[:, 2:3], cf[:, 2:3], 4.0 * MID, A.add, A.add, r=["col2", "cf"], w=["col3"]),
+        lambda: ts(col[:, 0:1], T.df[:, 15:16], 0.0, BIG, A.is_gt, A.mult, r=dfs, w=["col0"]),
         lambda: ts(col[:, 13:14], T.df[:, 15:16], 0.0, T.ta[:, 0:1], A.is_gt, A.add, r=dfs + ["ta"], w=["col13"]),
-        lambda: ts(col[:, 3:4], col[:, 2:3], cf[:, 3:4], 4.0 * MID, A.add, A.add, r=["col2", "cf"], w=["col3"]),
-        lambda: ts(col[:, 8:9], T.ta[:, 0:1], BIGP, MID + 8.0, A.mult, A.add, r=["ta"], w=["col8"]),
-        lambda: ts(col[:, 10:11], col[:, 13:14], BIGP, None, A.mult, r=["col13"], w=["col10"]),
-        lambda: ts(col[:, 11:12], col[:, 13:14], BIGP, -1.0, A.mult, A.add, r=["col13"], w=["col11"]),
-        lambda: ts(T.od[:, 0:NB], T.ic[:, 0:NB], 1.0 * MID, None, A.add, r=["ic"], w=["od"]),
     ])
     quant(T.q0, T.s0, 0, 128, T.xt, r=x0, w=["q0.0"])
     send(0)
-    dma("sp", T.vt[:], T.v[:], r=["q0.h"], w=["vt"])
-    dma("sp", T.qw[:].bitcast(dt.uint8), T.wc[:], w=["qw"])
+    dma("sp", T.qw[:].bitcast(dt.uint8), T.wc[:], r=["q0.h"], w=["qw"])
     dma("sp", T.sw[:], T.ws[:], w=["sw"])
+    dma("sp", T.vt[:], T.v[:], w=["vt"])
+    gap(3)
     quant(T.qu, T.su, 0, 128, T.ut, r=["ut"], w=["qu"])
-    gap()
+    gap(1)
+    cp(T.qa[:].bitcast(dt.uint32), T.qu[:].bitcast(dt.uint32).indirect(T.oab[:]), r=["qu", "oab"], w=["qa"])
+    act(T.sa[:], T.su[:].indirect(T.oab[:]), F.Copy, r=["qu", "oab"], w=["sa"])
+    weave(0)
     quant(T.q0, T.s0, 128, C, T.xt, r=x1, w=["q0.1"])
-    for q, s, lo, tok in ((T.qa, T.sa, 0, "a"), (T.qb, T.sb, 8, "b")):
-        cp(q[:, 0:128].bitcast(dt.uint32), T.qu[:, 0:128].bitcast(dt.uint32).indirect(T.oab[:, lo:lo + 8]), r=["qu", "o" + tok], w=["q" + tok])
-        act(s[:, 0:128], T.su[:, 0:128].indirect(T.oab[:, lo:lo + 8]), F.Copy, r=["qu", "o" + tok], w=["s" + tok])
+    diagonal(T.et[:, 3:515:4], 1.0, ["et0"], ["et"])
     iota(T.ic[:], [[1, E]], -MID, 0, ["ic"])
-    for ks in (((0, RADIX), (1, 1.0)), ((3, HIGH),)):
-        for k, wt in ks:
-            iota(T.kt[:, 512 * k:512 * k + 512], [[0, 128], [-2 * int(wt), 4]], 4 * int(wt), 0, ["kt%d" % k])
-        if len(ks) == 1:
-            keep(T.kt[:, 2:512:4], T.one[:, 0:128], [[1, 128]], A.is_equal, 0, -1, ["one"], ["kt0"])
-        for k, wt in ks:
-            x = T.kt[:, 512 * k:512 * k + 512]
-            keep(x, x, [[1, 128], [0, 4]], A.is_equal, 0, -1, [], ["kt%d" % k])
+    diagonals(0)
     iota(dg[:, 2:4 * E:4], [[0, E]], 0, 0, ["dg2a", "dg2b", "dg2l"])
     iota(dg[:, 4 * E:4 * EP], [[0, 4 * (EP - E)]], 0, 0, ["dgp"])
+    for k in range(2):
+        x = T.ct[:, 512 * k:512 * k + 512]
+        keep(x, T.zr[:], 512, -1, -0.5, ["zr"], ["ct%d" % k])
+        if k:
+            keep(T.ct[:, 512:1024:4], T.zr[:, 0:128], 128, -1, -1.0, ["zr"], ["ct1"])
+        keep(x, x, 512, 15, 0.0, [], ["ct%d" % k])
     for x, tok in ((T.rw[:, 0:2], "rw0"), (T.dk[:, 0:2], "dk0")):
         iota(x, [[0, 2]], 0, 0, [tok])
-    act(T.vh0[:, 0:4 * C], T.xt[:], F.Copy, scale=0.5, r=x0 + x1, w=["vh0"])
-    block(T.ct[:, 0:512], "og", -0.5, ["ct0"])
     for k, (cs, wd) in enumerate(TILES):
         lo = 0 if len(cs) < 4 else 16 * min(c for c in cs if c)
         dma("sp", T.tb[:, 4 * (TOFF[k] + lo):4 * (TOFF[k] + wd)], T.zr[:, 0:4 * (wd - lo)], r=["zr"],
-            w=["tb%d.%d" % (k, j) for j in four] + ["in.a", "in.b"] * (k == TD))
+            w=["tb%d.%d" % (k, j) for j in four] + ins * (k == TD))
 
     def unpack(t, banks, products):
         q, s = T["q%d" % t], T["s%d" % t]
@@ -286,66 +298,55 @@ def rank_program(g, core, T, topo):
         act(T.junk[:, lo:hi], dg[:, 4 * lo:4 * hi:4], F.Sign, scale=-1.0, bias=col[:, 5:6], accum_out=T.acc[:, n:n + 1],
             r=["dg0" + part, "col4"], w=["junk" + part, "acc" + part])
 
-    def members(part, lo, hi):
-        ts(T.oh2[:, lo:hi], dg[:, 4 * lo:4 * hi:4], col[:, 4:5], 2.0, A.is_equal, A.mult, r=["dg0" + part, "col4"], w=["oh2" + part])
-        ts(T.oh[:, lo:hi], dg[:, 4 * lo:4 * hi:4], col[:, 4:5], None, A.is_equal, r=["dg0" + part, "col4"], w=["oh" + part])
+    def members(part, lo, hi, up):
+        o = 2 * E if up else 1
+        ts(zf[:, o + lo:o + hi], dg[:, 4 * lo:4 * hi:4], col[:, 4:5], MEM + 2.0 * up, A.is_equal, A.mult, r=["dg0" + part, "col4"], w=[("dn", "up")[up] + part])
 
     mm(0, T.qa, T.sa, 0, T.q0, T.s0, 0, C, r=["qa", "sa", "q0.0", "q0.1"])
-    mm(1, T.qb, T.sb, 0, T.q0, T.s0, 0, C, r=["qb", "sb", "q0.0", "q0.1"])
+    mm(1, T.qa, T.sa, 128, T.q0, T.s0, 0, C, r=["qa", "sa", "q0.0", "q0.1"])
     mm(2, T.qa, T.sa, 0, T.q0, T.s0, E - 128, E, r=["qa", "sa", "q0.1", "q0.h"])
-    mm(3, T.qb, T.sb, 0, T.q0, T.s0, E - 128, E, r=["qb", "sb", "q0.1", "q0.h"])
-    unit(0)
-    gap(3)
-    quant(T.qp, T.sp, 0, 128, T.tp, r=["tp"], w=["qp"])
-    ts(T.a2[:, 0:C], bank(0, 0, C), 0.0, 2.0, A.is_gt, A.mult, r=["p0"], w=["a2o"])
-    ts(T.ab[:, 0:C], bank(1, 0, C), 0.0, 0.5, A.is_gt, A.add, r=["p1"], w=["abo"])
-    gap(3)
-    spread(T.d0h, MID, 1, BIG, ["d0h"])
+    mm(3, T.qa, T.sa, 128, T.q0, T.s0, E - 128, E, r=["qa", "sa", "q0.1", "q0.h"])
+    gap(5)
+    act(T.a2[:, 0:C], bank(0, 0, C), F.Sign, bias=-TINY, r=["p0"], w=["a2o"])
+    ts(T.ab[:, 0:C], bank(1, 0, C), 0.0, 1.5, A.is_gt, A.add, r=["p1"], w=["abo"])
+    act(T.vh0[:, 0:4 * C], T.xt[:], F.Copy, scale=0.5, r=x0 + x1, w=["vh0.0", "vh0.1"])
+    gap(1)
     tt(T.wb[:, 0:C], T.a2[:, 0:C], T.ab[:, 0:C], A.add, r=["a2o", "abo"], w=["wbo"])
-    unit(1)
-    gap()
+    gap(1)
     ts(T.mb[:, 0:C], T.wb[:, 0:C], 4.0, -10.0, A.mult, A.add, r=["wbo"], w=["mbo"])
-    unit(2)
-    gap()
+    gap(1)
     classes("o", 0, C - 2, [])
-    spread(T.d0v, C, 2, BIGV, ["d0v"])
+    weave(1)
     sa, sb = bank(2, 128 - H, 128), bank(3, 128 - H, 128)
     ts(T.a2[:, C:E], sa, 0.0, 2.0, A.is_gt, A.mult, r=["p2"], w=["a2l"])
-    ts(T.ab[:, C:E], sb, 0.0, 0.5, A.is_gt, A.add, r=["p3"], w=["abl"])
     ts(T.a8[:], sa, 0.0, -8.0, A.is_le, A.mult, r=["p2"], w=["a8"])
+    ts(T.ab[:, C:E], sb, 0.0, 0.5, A.is_gt, A.add, r=["p3"], w=["abl"])
     ts(T.b4[:], sb, 0.0, 4.0, A.is_gt, A.mult, r=["p3"], w=["b4"])
     tt(T.wb[:, C:E], T.a2[:, C:E], T.ab[:, C:E], A.add, r=["a2l", "abl"], w=["wbl"])
     tt(T.mb[:, C:E], T.a8[:], T.b4[:], A.add, r=["a8", "b4"], w=["mbl"])
-    members("o", 0, C - 2)
+    members("o", 0, C - 2, 1)
     classes("l", C - 2, E, ["wbl", "mbl", "wb.p"])
+    members("o", 0, C - 2, 0)
+    members("l", C - 2, E - 1, 1)
+    ts(zf[:, 0:1], T.acc[:, 0:1], -1.0, MEM - E, A.mult, A.add, r=["acco"], w=["dn0"])
+    members("l", C - 2, E - 1, 0)
     ts(T.acc[:, 2:3], T.acc[:, 0:1], 1.0 * E, None, A.add, r=["acco"], w=["acc2"])
-    unit(3)
-    members("l", C - 2, E)
-    ts(T.oh2[:, 0:1], T.oh2[:, 0:1], T.acc[:, 2:3], None, A.add, r=["acc2"], w=["oh2o"])
-    HALO0 = ((0, 5), (1, 6), (2, 7), (3, 0))
-    unpack(0, HALO0, True)
+    ts(T.acc[:, 3:4], dg[:, 4 * E - 4:4 * E - 3], col[:, 6:7], None, A.is_equal, r=["dg0l", "col4"], w=["acc3"])
+    spread(T.d0v, C, 1, BIGV, ["d0v"])
     act(T.x32[:], T.xt[:], F.Copy, scale=32.0, r=x0 + x1, w=xs[0] + xs[1])
-    scan(T.pre[:], T.oh2[:], T.oh[:], A.add, A.max, r=["oho", "ohl", "oh2o", "oh2l", "accl"], w=["pre"], first=T.acc[:, 1:2])
-    ts(T.acc[:, 3:4], T.acc[:, 1:2], T.acc[:, 2:3], None, A.add, r=["accl", "acc2"], w=["acc3"])
-    gap()
-    halves = ((0, MID), (MID, E))
-    for h, (a, b) in enumerate(halves):
-        b = min(b, E - 1)
-        tt(T.sel[:, a:b], T.pre[:, a:b], T.oh[:, a:b], A.mult, r=["pre", "oho", "ohl"], w=["sel%d" % h])
-        if h == 0:
-            ts(T.sel[:, E - 1:E], dg[:, 4 * E - 4:4 * E - 3], col[:, 6:7], T.acc[:, 3:4], A.is_equal, A.mult, r=["dg0l", "col4", "acc3"], w=["sel2"])
-    for h, (a, b) in enumerate(halves):
-        ts(T.hl[:, 2 * a:2 * b:2], T.sel[:, a:b], SPLIT, SPLIT, A.add, A.subtract, r=["sel%d" % h] + ["sel2"] * h, w=["hi%d" % h])
-    for h, (a, b) in enumerate(halves):
-        tt(T.hl[:, 2 * a + 1:2 * b:2], T.sel[:, a:b], T.hl[:, 2 * a:2 * b:2], A.subtract, r=["hi%d" % h], w=["lo%d" % h])
-    block(T.ct[:, 512:1024], "o2", -0.5, ["ct1"])
-    gap(2)
-    quant(T.qh, T.sh, 0, MID, T.hl, r=["lo0", "lo1"], w=["qh"])
-    mm(4, T.qp, T.sp, 0, T.qh, T.sh, 0, MID, r=["qp", "qh"])
-    spread(T.d0k, E, 0, BIG, ["d0k"])
+    unit(0)
+    scan(zf[:, E:2 * E - 1], zf[:, 2 * E:3 * E - 1], zf[:, 0:E - 1], A.add, A.subtract,
+         r=["upo", "upl", "dno", "dnl", "dn0", "accl"], w=["z"], first=T.acc[:, 1:2])
+    ts(zf[:, 2 * E - 1:2 * E], T.acc[:, 1:2], T.acc[:, 2:3], T.acc[:, 3:4], A.add, A.mult, r=["accl", "acc2", "acc3"], w=["zl"])
+    unit(1)
+    turn(T.tz[:, 32:32 + 2 * E:2], zf[:, E:2 * E], ["z", "zl"], ["tz0"])
+    turn(T.tz[:, 1:2 * E + 65:2], zf[:, E - 16:2 * E + 16], ["z", "zl", "dnl", "upo"], ["tz1"])
+    unit(2)
+    scan(T.th[:], T.d0t[:], T.tz[:, 32:32 + 2 * E], A.add, A.max, r=["d0t0", "d0t1", "tz0", "tz1"], w=["th"])
+    unit(3)
+    HALO0 = ((0, 4), (1, 5), (2, 6), (3, 7))
+    unpack(0, HALO0, True)
     unpack(0, HALO0, False)
-    quant(T.qc, T.sc, 0, 256, T.ct, r=["ct0", "ct1"], w=["qc"])
-    scan(T.sk[:, 0:MID], T.d0h[:], bank(4, 0, MID), A.add, A.max, r=["d0h"], w=["p4"] + sks)
 
     OWN = {"a": (0, AB), "b": (AB, EB), "l": (EB, NB)}
     SCORE = {"a": 7, "b": 0, "l": 1}
@@ -378,7 +379,7 @@ def rank_program(g, core, T, topo):
         for i, (c, d) in enumerate(terms):
             k, lo, hi = row(t, part)
             mm(k, T.qk, T.sk8, 128 * c, T["qd%d" % u], T["sd%d" % u], lo + d, hi + d,
-               r=["qk%d" % c] + ["qd%d%s" % (u, p) for p in have], start=i == 0 and (old or t == 1), stop=i == 1 and not old)
+               r=["qk%d" % (c // 2)] + ["qd%d%s" % (u, p) for p in have], start=i == 0 and (old or t == 1), stop=i == 1 and not old)
 
     def hold(t, part):
         a, b = (16 * c for c in OWN[part])
@@ -398,10 +399,10 @@ def rank_program(g, core, T, topo):
             ts(T.kw[:, c1:NB], T.sk[:, E - 1:E], T.cc[:, 31 + t:32 + t], STEP[t], A.add, A.add, r=["sk.l", "cc%d" % t], w=["kw.z"])
 
     def inside(t, part):
-        c0, c1 = (0, EB) if part == "ab" else (EB - 1, NB)
+        c0, c1 = {"a": (0, AB - 1), "b": (AB - 1, EB - 1), "l": (EB - 1, NB)}[part]
         o = 4 * TOFF[TD]
         tt(T.tb[:, o + 64 * c0:o + 64 * c1:4], T.kw[:, 0:c1].indirect(T.od[:, c0:c1]), T["kt%d" % t][:, 16 * c0:16 * c1], A.is_gt,
-           r=["kw.a", "kw.b", "tied.a", "tied.b", "od"] + ["kw.l", "kw.z", "tied.l"] * (part == "l"), w=["in.a", "in.b"][:1 + (part == "l")])
+           r=["kw.a", "tied.a", "od"] + ["kw.b", "tied.b"] * (part != "a") + ["kw.l", "kw.z", "tied.l"] * (part == "l"), w=["in." + part])
 
     def lane(c):
         k = [c in cs for cs, _ in TILES].index(True)
@@ -436,7 +437,7 @@ def rank_program(g, core, T, topo):
 
     def fold(c, sums, stop=False):
         k = lane(c)[0]
-        quant(T.qt, T.st, TOFF[k], TOFF[k] + TILES[k][1], T.tb, r=["tb%d.%d" % (k, j) for j in four] + ["in.a", "in.b"] * (k == TD), w=["qt%d" % k])
+        quant(T.qt, T.st, TOFF[k], TOFF[k] + TILES[k][1], T.tb, r=["tb%d.%d" % (k, j) for j in four] + ins * (k == TD), w=["qt%d" % k])
         for x in sums:
             k = lane(x)[0]
             mm(SUM, T.qc, T.sc, 128 if k == TD else 0, T.qt, T.st, TOFF[k], TOFF[k] + (E if k == TF else TILES[k][1]),
@@ -454,38 +455,41 @@ def rank_program(g, core, T, topo):
             ts(out, T.rw[:, c0:c1], 0.5, T.off[:, n:n + 1], A.mult, A.add, r=rs, w=["rc%d" % c0])
         return "rc%d" % c0
 
+    def half(t, h):
+        a, b = CH[h]
+        act(T["vh%d" % t][:, 4 * a:4 * b], T.x32[:, 4 * a:4 * b], F.Copy, scale=0.015625, r=xs[h], w=["vh%d.%d" % (t, h)])
+
     def order(t):
         top = min(c for c in DVS[t] if c >= EB)
         compare(t, (15, 16, 17, 18, 11, 12, 13, 14), False)
-        rowsum(t, (3,))
-        signs(t, "l")
-        fold(3, ())
-        rowsum(t, (4,))
         digits(t, "l")
         keys(t, "l", False)
         keys(t, "all", False)
-        inside(t, "ab")
+        missing(t, 1)
+        fold(3, ())
+        inside(t, "a")
         fold(7, ())
-        rowsum(t, (5,))
+        inside(t, "b")
         hold(t, "l")
         tied(t, "l")
-        rowsum(t, (6,))
+        fold(1, ())
         owned(t, "l")
-        compare(t, range(NB - 1, EB - 1, -1), False)
-        compare(t, (2, 1), False)
-        fold(15, (15, 7, 3))
-        unpack(t, HALO, True)
-        act(T["vh%d" % t][:, 0:4 * C], T.x32[:], F.Copy, scale=0.015625, r=xs[0] + xs[1], w=["vh%d" % t])
-        unpack(t, HALO, False)
-        compare(t, (25, 24, 23, 22), True)
+        compare(t, (19, 20, 21, 22), False)
+        rowsum(t, (6, 5, 4, 3))
+        fold(15, (15, 7, 3, 1))
+        compare(t, (23, 25), True)
         inside(t, "l")
+        compare(t, (24, 22), True)
+        rowsum(t, (23,))
         fold(11, (11,))
-        rowsum(t, (25,))
         fold(25, (25,))
+        rowsum(t, (25, 22))
+        fold(19, (19,), stop=True)
+        half(t, 0)
+        half(t, 1)
+        unpack(t, HALO, True)
+        unpack(t, HALO, False)
         rowsum(t, (24,))
-        fold(19, (19,))
-        fold(1, (1,), stop=True)
-        rowsum(t, (23, 22))
         rcs = [rows(t, c) for c in (3, 0, 7, top)]
         scan(T.ps[:], bank(SUM, 0, E), T.d1k[:, 1:E + 1], A.max, A.add, r=["d1k"] + rcs, w=["ps", "p%d" % SUM], first=-BIGP)
 
@@ -496,21 +500,20 @@ def rank_program(g, core, T, topo):
         if t:
             order(t)
             x, y, c0, c1, rs = T.ps[:, 15:E:16], T.ps[:, 15:C:16], col[:, 10:11], col[:, 11:12], ["ps", "col10", "col11"]
+            ts(T.pos[:, 0:NB], x, c0, None, A.subtract, r=rs, w=poss)
+            ts(T.onm[:, 20:40], y, c1, E - 1.0, A.subtract, A.min, r=rs, w=["om"])
+            ts(T.onm[:, 0:20], y, c0, 1.0, A.subtract, A.subtract, r=rs, w=["on"])
         else:
-            x, y, c0, c1, rs = T.sk[:, 7:MID:8], T.sk[:, 7:C // 2:8], col[:, 1:2], col[:, 1:2], sks + ["col0"]
-        z = float(t == 0)
-        ts(T.pos[:, 0:NB], x, c0, z, A.subtract, A.subtract, r=rs, w=["pos"])
-        ts(T.onm[:, 20:40], y, c1, E - 1.0, A.subtract, A.min, r=rs, w=["om"])
-        ts(T.onm[:, 0:20], y, c0, z + 1.0, A.subtract, A.subtract, r=rs, w=["on"])
-        cp(T.ordr[:, 0:E].indirect(T.pos[:, 0:NB]), T.ic[:], r=["pos", "ic"], w=["ordr"])
-        if not last:
-            ties(u, 0)
-            if t == 0:
-                act(dg[:, 3:4 * E:4], dg[:, 0:4 * E:4], F.Sign, scale=-1.0, bias=dg[:, 4 * E - 4:4 * E - 3], r=["dg0o", "dg0l"], w=["dg3"])
-                gap(3)
-            else:
-                weights(2)
-            ties(u, 1)
+            for k in range(2):
+                ts(T.pos[:, k:NB:2], T.th[:, 31 + 32 * k:2 * E:64], col[:, 14 + k:15 + k], 0.5, A.subtract, A.mult, r=["th", "col%d" % (14 + k)], w=["pos%d" % k])
+            gap(1)
+        cp(T.ordr[:, 0:E].indirect(T.pos[:, 0:NB]), T.ic[:], r=poss + ["ic"], w=["ordr"])
+        if t == 0:
+            ts(T.onm[:, 20:40], T.pos[:, 0:20], 1.0, E - 1.0, A.add, A.min, r=poss, w=["om"])
+            ts(T.onm[:, 0:20], T.pos[:, 0:20], 1.0, None, A.subtract, r=poss, w=["on"])
+            ts(T.od[:, 0:NB], T.ic[:, 0:NB], 1.0 * MID, None, A.add, r=["ic"], w=["od"])
+        elif last:
+            act(T.d0p[:], T.d0k[:], F.Copy, scale=LOW, r=["d0k"], w=["d0p"])
         for h, (a, b) in enumerate(CH):
             act(T.gn[:, a:b], T.ordr[:, 0:E].indirect(T.onm[:, a // 16:b // 16]), F.Copy, r=["ordr", "on"], w=["gn%d" % h])
             cp(T.gm[:, a:b], T.ordr[:, 0:E].indirect(T.onm[:, 20 + a // 16:20 + b // 16]), r=["ordr", "om"], w=["gm%d" % h])
@@ -524,7 +527,7 @@ def rank_program(g, core, T, topo):
             o = 80 * (n == "m")
             ts(T.ov[:, o + a // 4:o + b // 4], T["s" + n][:, a + 3:b:4], 4.0, col[:, 3:4], A.mult, A.add, r=["s%s%d" % (n, h), "col3"], w=["ov%s%d" % (n, h)])
 
-        vr = ["vh%d" % t] + ["vh%d.h%d" % (t, b) for b in four]
+        vr = ["vh%d.0" % t, "vh%d.1" % t] + ["vh%d.h%d" % (t, b) for b in four]
 
         def pick(k, n):
             a, b = PIECES[k]
@@ -584,11 +587,9 @@ def rank_program(g, core, T, topo):
         near(1, "n")
         offs(0, "n")
         if last:
-            scan(T.sk[:], T.d0k[:], T.ordr[:], A.add, A.max, r=["d0k", "ordr"], w=sks)
-        elif t == 1:
-            weights(3)
+            scan(T.th[:, 0:E], T.d0p[:], T.ordr[:], A.add, A.max, r=["d0p", "ordr"], w=["th"])
         else:
-            quant(T.qv, T.sv, 0, 128, T.vt, r=["vt"], w=["qv"])
+            weights(t)
         for part in ("a", "b", "all"):
             keys(u, part, True)
         offs(1, "m")
@@ -597,9 +598,15 @@ def rank_program(g, core, T, topo):
         gather(4, "m")
         gather(5, "n")
         gather(5, "m")
+        if t == 0:
+            act(dg[:, 3:4 * E:4], dg[:, 0:4 * E:4], F.Sign, scale=-1.0, bias=dg[:, 4 * E - 4:4 * E - 3], r=["dg0o", "dg0l"], w=["dg3"])
+            spread(T.d0k, E, 0, BIG, ["d0k"])
+        elif t == 1:
+            ties(u, 0)
+            ties(u, 1)
         most(0)
         if last:
-            ts(T.ow[:, 0:NB], T.sk[:, 15:E:16], col[:, 0:1], 1.0 * MID, A.subtract, A.add, r=sks + ["col0"], w=["ow"])
+            ts(T.ow[:, 0:NB], T.th[:, 15:E:16], col[:, 12:13], None, A.subtract, r=["th", "col12"], w=["ow"])
             act(T.ks[:], T.kt2[:, 0:E].indirect(T.ow[:, 0:NB]), F.Copy, scale=512.0, r=tieds + ["ow"], w=["ks"])
         most(2)
         blend(0)
@@ -619,45 +626,51 @@ def rank_program(g, core, T, topo):
         layer(1, (0, 1))
         state(0, (2, 3))
         layer(1, (2, 3))
-        shrink(0, 2)
-        if t == 0:
-            weights(0)
-        state(1, (0,))
-        shrink(0, 3)
-        state(1, (1,))
-        if not last:
-            missing(u, 0)
-        fresh(0)
         if last:
             break
+        shrink(0, 2)
+        shrink(0, 3)
+        state(1, (0, 1))
+        fresh(0)
         send(u)
         score(u, "a")
         state(1, (2, 3))
         if t == 0:
-            act(T.kt[:, 1024:1536], T.kt[:, 0:512], F.Copy, scale=HIGH, r=["kt0"], w=["kt2"])
+            diagonals(1)
+            ties(u, 0)
+            ties(u, 1)
             spread(T.d1k, E + 16, 0, BIGP, ["d1k"])
-            act(T.off[:], jm[:, 0:16], F.Identity, scale=8.0, bias=col[:, 8:9], r=["jm0", "col8"], w=["off"])
-            weights(1)
+            lin(col[:, 8:9], T.ta[:, 0:1], BIGP, MID + 8.0, ["ta"], ["col8"])
+            lin(col[:, 10:11], col[:, 13:14], BIGP, 0.0, ["col13"], ["col10"])
+            lin(T.off[:], jm[:, 0:16], 8.0, col[:, 8:9], ["jm0", "col8"], ["off"])
+            lin(col[:, 11:12], col[:, 13:14], BIGP, -1.0, ["col13"], ["col11"])
+            lin(col[:, 12:13], col[:, 0:1], LOW, -1.0 * MID, ["col0"], ["col12"])
         shrink(1, 2)
         shrink(1, 3)
         signs(u, "a")
         fresh(1)
         score(u, "b")
-        missing(u, 1)
         digits(u, "a")
         keys(u, "a", False)
+        if t == 0:
+            quant(T.qc, T.sc, 0, 256, T.ct, r=["ct0", "ct1"], w=["qc"])
+        else:
+            quant(T.qv, T.sv, 0, 128, T.vt, r=["vt"], w=["qv"])
         signs(u, "b")
         digits(u, "b")
         keys(u, "b", False)
-        keys(u, "l", True)
         score(u, "l")
+        keys(u, "l", True)
         hold(u, "a")
         tied(u, "a")
+        missing(u, 0)
         owned(u, "a")
-        compare(u, (10, 9, 8, 7), False)
-        compare(u, (3, 4, 5, 6), True)
+        compare(u, (10, 9, 8, 7, 2, 1), False)
+        compare(u, (6, 5), True)
         hold(u, "b")
         tied(u, "b")
+        signs(u, "l")
+        compare(u, (4, 3), True)
         owned(u, "b")
     q, s = T.q3, T.s3
 
@@ -669,23 +682,32 @@ def rank_program(g, core, T, topo):
     def result(h):
         a, b = CH[h]
         act(T.ys[:, a:b], bank(4 + h, 0, b - a), F.Copy, w=["p%d" % (4 + h), "ys%d" % h])
+        dma("act", T.y[:, a:b], T.ys[:, a:b], r=["ys%d" % h])
 
+    def scales(eng, k):
+        dma(eng, T.osc[4 * k:4 * k + 4, :], s[32 * k:32 * k + 4, 0:C], r=["q3.0", "q3.1"])
+
+    shrink(0, 2)
+    state(1, (0,))
+    shrink(0, 3)
+    state(1, (1, 2, 3))
+    fresh(0)
     leave(0)
-    state(1, (2, 3))
     result(0)
-    dma("act", T.y[:, 0:C0], T.ys[:, 0:C0], r=["ys0"])
     shrink(1, 2)
-    tt(T.dk[:, 1:MID], T.ks[:, 1:MID], T.ks[:, 0:MID - 1], A.subtract, r=["ks"], w=["dk0", "dk1"])
     shrink(1, 3)
-    tt(T.dk[:, MID:E], T.ks[:, MID:E], T.ks[:, MID - 1:E - 1], A.subtract, r=["ks"], w=["dk2"])
+    tt(T.dk[:, 1:MID], T.ks[:, 1:MID], T.ks[:, 0:MID - 1], A.subtract, r=["ks"], w=["dk0", "dk1"])
     fresh(1)
     leave(1)
-    scan(T.ls[:], T.dk[:], T.ic[:], A.add, A.min, r=["dk1", "dk2", "ic"], w=["ls"])
-    for k in four:
-        dma(("sp", "act")[k // 2], T.osc[4 * k:4 * k + 4, :], s[32 * k:32 * k + 4, 0:C], r=["q3.0", "q3.1"])
+    scales("sp", 0)
+    tt(T.dk[:, MID:E], T.ks[:, MID:E], T.ks[:, MID - 1:E - 1], A.subtract, r=["ks"], w=["dk2"])
     result(1)
-    ts(T.lr[:], T.ls[:, 0:E].indirect(T.pos[:, 0:NB]), 1.0 * MID, None, A.add, r=["ls", "pos"], w=["lr"])
-    dma("act", T.y[:, C0:C], T.ys[:, C0:C], r=["ys1"])
-    dma("sp", T.lv[:], T.lr[15:128:16, :], r=["lr"])
+    scales("sp", 1)
+    scales("sp", 2)
+    scan(T.ls[:], T.dk[:], T.ic[:], A.add, A.min, r=["dk1", "dk2", "ic"], w=["ls"])
+    ts(T.lr[:, 0:LV], T.ls[:, 0:E].indirect(T.pos[:, 0:LV // 16]), 1.0 * MID, None, A.add, r=["ls"] + poss, w=["lr0"])
+    act(T.lr[:, LV:E], T.ls[:, 0:E].indirect(T.pos[:, LV // 16:NB]), F.Identity, bias=1.0 * MID, r=["ls"] + poss, w=["lr1"])
+    scales("act", 3)
+    dma("sp", T.lv[:], T.lr[15:128:16, :], r=["lr0", "lr1"])
     for sname, v in cnt.items():
         g.wait_ge(T.sem[sname], v)

from concourse.mybir import dt, AluOpType, ActivationFunctionType

A = AluOpType
F = ActivationFunctionType
C, H, E, R = 320, 96, 416, 3
C0 = 192
PIECES, MODE = ((0, 48), (48, 88), (88, 136), (136, C0), (C0, 248), (248, C)), "FDFFFA"
EP = C + 128
NB, AB, EB = 26, 11, 19
RADIX, HIGH = 36.0, 4096.0
STEP = (0.0, 1.0, 0.5)
NONE1, NONE2 = -34.0, -1200.0
BIG, BIGP, BIGV = 11010048.0, 4096.0, 512.0
MEM, LIFT = 1024.0, 2048.0
TINY, LOW = 1e-37, 2.0 ** -13
MID = E // 2
LV = 256
TILES = (((0, 25, 24, 23), 416), ((1, 2), 128), ((3, 4, 5, 6), 128), ((11, 12, 13, 14), 224), ((7, 8, 9, 10), 160),
         ((19, 20, 21, 22), 352), ((15, 16, 17, 18), 288))
TD, TF = 0, 6
DVS = ((), (3, 4, 5, 6, 22, 23, 24, 25), (3, 4, 5, 6, 23, 24, 25))
TOFF = [sum(w for _, w in TILES[:k]) for k in range(len(TILES) + 1)]
Q4, U8, BF, F16, F32, I32, U16 = "float8_e4m3fn_x4", "uint8", "bfloat16", "float16", "float32", "int32", "uint16"


def _sb(n, d):
    return ("sbuf", [128, n], d)


SCRATCH = {
    "xt": _sb(4 * C, BF), "x32": _sb(4 * C, BF), "ut": _sb(512, BF), "vt": _sb(512, BF),
    "qw": _sb(512, Q4), "sw": _sb(512, U8), "qu": _sb(128, Q4), "su": _sb(128, U8),
    "qa": _sb(256, Q4), "sa": _sb(256, U8), "qv": _sb(128, Q4), "sv": _sb(128, U8),
    "et": _sb(516, BF), "qe": _sb(512, Q4), "se": _sb(512, U8),
    "ct": _sb(1024, BF), "qc": _sb(256, Q4), "sc": _sb(256, U8),
    "kt": _sb(2048, BF), "qk": _sb(512, Q4), "sk8": _sb(512, U8),
    "pi": _sb(8, I32), "ci": _sb(8, I32), "cf": _sb(8, F32), "jm": _sb(196, BF), "df": _sb(32, BF), "ta": _sb(32, BF),
    "tc": _sb(32, BF), "tab": _sb(48, BF), "t64": _sb(64, BF), "col": _sb(16, F32), "off": _sb(16, F32), "cc": _sb(36, F32),
    "ic": _sb(E, BF), "zr": _sb(512, BF),
    "oab": _sb(16, U16), "orr": _sb(32, U16), "od": _sb(32, U16), "o64": _sb(52, U16),
    "d0k": _sb(E, BF), "d0t": _sb(2 * E, BF), "d0p": _sb(E, BF), "d0v": _sb(C, BF), "d1k": _sb(E + 16, F32),
    "tie1": _sb(E, BF), "tie2": _sb(E, F32),
    "ab": _sb(E, BF), "a2": _sb(E, BF), "a8": _sb(H, BF), "b4": _sb(H, BF), "wb": _sb(E + 16, BF), "mb": _sb(E, BF),
    "dg": _sb(4 * EP, BF), "qd1": _sb(EP, Q4), "sd1": _sb(EP, U8), "qd2": _sb(EP, Q4), "sd2": _sb(EP, U8),
    "zf": _sb(3 * E, F16), "tz": _sb(2 * E + 66, F16), "th": _sb(2 * E, F16), "junk": _sb(E, BF), "acc": _sb(8, F32),
    "kt1": _sb(E, F16), "kt2": _sb(E, F32), "jk": _sb(8 * E, F16),
    "sk": _sb(E, F32), "ps": _sb(E, F32), "kw": _sb(32, F32), "rw": _sb(32, F32),
    "tb": _sb(4 * TOFF[-1], BF), "qt": _sb(TOFF[-1] + 128, Q4), "st": _sb(TOFF[-1] + 128, U8),
    "pos": _sb(32, U16), "onm": _sb(40, U16), "ordr": _sb(E, BF), "gn": _sb(C, BF), "gm": _sb(C, BF),
    "sn": _sb(C, F16), "sm": _sb(C, F16), "ov": _sb(160, U16),
    "g1": _sb(4 * C, BF), "g3": _sb(4 * C, BF), "g2": _sb(4 * C, BF), "zt": _sb(4 * C, BF), "qz": _sb(C, Q4), "sz": _sb(C, U8),
    "ow": _sb(32, U16), "ks": _sb(E, F32), "dk": _sb(E, BF), "ls": _sb(E, BF), "lr": _sb(E, F32), "ys": _sb(C, F32),
    "pa": ("psum", [128, 2048], F32), "pb": ("psum", [128, 2048], F32),
}
for _t in range(R):
    SCRATCH["vh%d" % _t] = _sb(4 * E, BF)
for _t in range(R + 1):
    SCRATCH["q%d" % _t] = _sb(E, Q4)
    SCRATCH["s%d" % _t] = _sb(E, U8)
SEMAPHORES = ["pe", "dve", "act", "gp", "snd", "arr0", "arr1", "arr2"] + ["d%d" % k for k in range(30)]


def rank_program(g, core, T, topo):
    rank = T.rank_of(core)
    if rank is None:
        return
    cores = list(T.cores)
    before = cores[(rank - 1) % len(cores)]
    rid, pid, _ = topo.addr(before)
    mask = topo.mask(core, before)
    neng = len(topo.engines(core, before))
    V, S, P = g.vector, g.scalar, g.tensor
    queue = {"pe": P, "dve": V, "act": S, "gp": g, "sp": g.sync}
    cnt, know, snap, lastw, readers = {}, {k: {} for k in queue}, {}, {}, {}
    ndma = [0]
    spare = []

    def need(eng, r, w):
        deps = {}
        for t in list(r) + list(w):
            assert t in w or t in lastw, t
            for d in [lastw.get(t)] + (readers.get(t, []) if t in w else []):
                if d is not None and not (eng == "pe" and d[0] == "pe"):
                    deps[d[0]] = max(deps.get(d[0], 0), d[1])
        for s, v in sorted(deps.items(), key=lambda e: e[0] == eng):
            if know[eng].get(s, 0) < v:
                queue[eng].wait_ge(T.sem[s], v)
                know[eng][s] = v
                for s2, v2 in snap.get((s, v), {}).items():
                    know[eng][s2] = max(know[eng].get(s2, 0), v2)

    def done(eng, src, val, r, w):
        snap[(src, val)] = dict(know[eng])
        for t in r:
            readers.setdefault(t, []).append((src, val))
        for t in w:
            lastw[t] = (src, val)
            readers[t] = []

    def op(eng, fn, r=(), w=()):
        need(eng, r, w)
        cnt[eng] = cnt.get(eng, 0) + 1
        fn().then_inc(T.sem[eng], 1)
        done(eng, eng, cnt[eng], r, w)

    def gap(n=1):
        for _ in range(min(n, len(spare))):
            spare.pop(0)()

    def dma(eng, out, in_, r=(), w=()):
        need(eng, r, w)
        s = "d%d" % ndma[0]
        ndma[0] += 1
        cnt[s] = 16
        queue[eng].dma_start(out, in_).then_inc(T.sem[s], 16)
        done(eng, s, 16, r, w)

    def ts(out, in0, s1, s2, o0, o1=None, r=(), w=()):
        if o1 is None:
            op("dve", lambda: V.tensor_scalar(out, in0, s1, None, o0), r, w)
        else:
            op("dve", lambda: V.tensor_scalar(out, in0, s1, s2, o0, o1), r, w)

    def tt(out, a, b, o, r=(), w=()):
        op("dve", lambda: V.tensor_tensor(out, a, b, o), r, w)

    def cp(out, a, r=(), w=()):
        op("dve", lambda: V.tensor_copy(out, a), r, w)

    def ms(out, c, w=()):
        op("dve", lambda: V.memset(out, c), (), w)

    def scan(out, d0, d1, o0, o1, r=(), w=(), first=0.0):
        op("dve", lambda: V.tensor_tensor_scan(out, d0, d1, first, o0, o1), r, w)

    def turn(out, in_, r, w):
        op("dve", lambda: V.transpose(out, in_), r, w)

    def quant(q, s, a, b, tile, r=(), w=(), at=None):
        lo = 4 * a if at is None else at
        op("dve", lambda: V.quantize_mx(q[:, a:b], s[:, a:b], tile[:, lo:lo + 4 * (b - a)]), r, w)

    def act(out, in_, func, r=(), w=(), **kw):
        op("act", lambda: S.activation(out, in_, func, **kw), r, w)

    def lin(out, in_, scale, bias, r, w):
        act(out, in_, F.Identity, r, w, scale=scale, bias=bias)

    def bank(k, a, b):
        return (T.pa, T.pb)[k // 4][:, 512 * (k % 4) + a:512 * (k % 4) + b]

    def mm(k, q, s, a, q2, s2, b0, b1, r=(), start=True, stop=True):
        op("pe", lambda: P.matmul_mx(bank(k, 0, b1 - b0), q[:, a:a + 128], s[:, a:a + 128], q2[:, b0:b1], s2[:, b0:b1], start, stop),
           r, ["p%d" % k])

    def iota(out, pat, base, cm, w, small=True):
        if small:
            op("gp", lambda: g.iota(out, pat, base, cm, allow_small_or_imprecise_dtypes=True), (), w)
        else:
            op("gp", lambda: g.iota(out, pat, base, cm), (), w)

    def keep(out, in_, n, base, fill, r, w):
        op("gp", lambda: g.affine_select(out, in_, [[16, 8], [0, n // 8]], A.is_ge, fill, base, -1), r, w)

    def send(t):
        q, s = T["q%d" % t], T["s%d" % t]
        need("gp", ["q%d.0" % t], [])
        g.remote_dma(q[:, C:E].bitcast(dt.uint8), q[:, 0:H].bitcast(dt.uint8), T.sem["arr%d" % t], T.sem.snd, pid, rid, mask)
        g.remote_dma(s[:, C:E], s[:, 0:H], T.sem["arr%d" % t], T.sem.snd, pid, rid, mask)
        cnt["snd"] = cnt.get("snd", 0) + 2 * neng
        lastw["q%d.h" % t] = ("arr%d" % t, 2 * neng)

    def spread(out, n, k, scale, w):
        act(out[:, 0:n], T.tab[:, 16 * k:16 * k + 16].indirect(T.orr[:, 0:n // 16]), F.Copy, scale=scale, r=["tab%d" % (k // 2), "orr"], w=w)

    def ties(t, step):
        tie = T["tie%d" % t]
        if step == 0:
            spread(tie, E, 2, STEP[t], tie_of[t])
            return
        for k, (a, c) in enumerate((((E - 2, NONE1),), ((E - 6, NONE1), (E - 4, NONE2), (E - 2, NONE2 + HIGH * NONE1)))[t - 1]):
            act(tie[:, a:a + 2], tie[:, a:a + 2], F.Identity, bias=c, w=["tie%d.%d" % (t, k)])

    def missing(t, step):
        if step == 0:
            scan(T.cc[:, 16 * t - 16:16 * t], T.d0k[:, 0:16], T["tie%d" % t][:, E - 16:E], A.add, A.max, r=["d0k"] + tie_of[t], w=["cd%d" % t])
        else:
            ts(T.cc[:, 31 + t:32 + t], T.col[:, 0:1], -2.0, T.cc[:, 16 * t - 1:16 * t], A.mult, A.add, r=["col0", "cd%d" % t], w=["cc%d" % t])

    def weave(h):
        act(T.d0t[:, E * h:E * h + E], T.t64[:].indirect(T.o64[:, NB * h:NB * h + NB]), F.Copy, r=["t64.1", "t64.33", "o64"], w=["d0t%d" % h])

    def diagonal(out, c, r, w):
        op("gp", lambda: g.affine_select(out, T.zr[:, 0:128], [[1, 128]], A.not_equal, c, 0, -1), ["zr"] + r, w)

    def diagonals(h):
        for k, wt in enumerate((4 * RADIX, 2 * RADIX, 1.0, -2 * RADIX, 4.0, 2.0, 0.0, -2.0)):
            o = 1024 * h + 512 * (k // 4)
            diagonal(T.kt[:, o + k % 4:o + 512:4], wt * HIGH ** h, [], ["kt%d.%d" % (h, k)])

    def weights(h):
        quant(T.qk, T.sk8, 256 * h, 256 * h + 256, T.kt, r=["kt%d.%d" % (h, k) for k in range(8)], w=["qk%d" % h])

    def unit(b):
        quant(T.qe, T.se, 128 * b, 128 * (b + 1), T.et, r=["et"], w=["qe%d" % b], at=3 - b)

    CH = ((0, C0), (C0, C))
    PART = {"a": (0, C0), "b": (C0, C), "l": (C, E)}
    cf, col, jm, dg, zf = T.cf, T.col, T.jm, T.dg, T.zf
    four = range(4)
    x0, x1 = (["xt.%d.%d" % (h, b) for b in four] for h in range(2))
    xs = [["x32.%d.%d" % (h, j) for j in four] for h in range(2)]
    tieds = ["tied.a", "tied.b", "tied.l"]
    ins = ["in.a", "in.b", "in.l"]
    tie_of = [["tie%d.%d" % (t, k) for k in range(3)] for t in range(R)]
    dfs, poss = ["df0", "df1"], ["pos0", "pos1"]
    dma("sp", T.xt[:, 0:512], T.x[:, 0:512], w=x0)
    dma("sp", T.ut[:], T.u[:], w=["ut"])
    dma("sp", T.xt[:, 512:4 * C], T.x[:, 512:4 * C], w=x1)
    iota(T.pi[:, 0:2], [[2, 2]], 0, 1, ["pi"], False)
    iota(jm[:, 64:80], [[1, 2], [16, 8]], 0, 0, ["jm4"])
    iota(jm[:, 80:144:2], [[2, 2], [0, 16]], -1, 0, ["jm5"])
    iota(jm[:, 81:144:2], [[-2, 2], [0, 16]], 1, 0, ["jm6"])
    iota(jm[:, 144:196], [[0, 13], [16, 4]], 0, 0, ["jm7"])
    iota(jm[:, 0:16], [[1, 16]], 0, 0, ["jm0"])
    iota(jm[:, 16:32], [[0, 4], [1, 4]], 0, 0, ["jm1"])
    ms(T.zr[:], 0.0, w=["zr"])
    for k, (sh, m) in enumerate(((0, 15), (2, 3), (0, 3), (4, 1))):
        ts(T.ci[:, k:k + 1], T.pi[:, 0:1], sh, m, A.arith_shift_right, A.bitwise_and, r=["pi"], w=["ci%d" % k])
    ms(T.wb[:, E:E + 16], 0.0, w=["wb.p"])
    cp(T.oab[:], jm[:, 64:80], r=["jm4"], w=["oab"])
    cp(cf[:, 0:4], T.ci[:, 0:4], r=["ci%d" % k for k in four], w=["cf"])
    ms(T.et[:], 0.0, w=["et0"])
    lin(col[:, 1:2], cf[:, 3:4], -2.0 * LIFT, LIFT, ["cf"], ["col1"])
    lin(col[:, 7:8], cf[:, 0:1], 1.0, -7.5, ["cf"], ["col7"])
    lin(col[:, 14:15], cf[:, 3:4], -LIFT, LIFT + 2.0, ["cf"], ["col14"])
    lin(T.t64[:], jm[:, 80:144], col[:, 1:2], 0.0, ["jm5", "jm6", "col1"], ["t64"])
    lin(col[:, 15:16], cf[:, 3:4], LIFT, 2.0, ["cf"], ["col15"])
    lin(col[:, 4:7], jm[:, 0:3], -0.25, col[:, 7:8], ["jm0", "col7"], ["col4"])
    for q, sg in ((1, 2.0), (33, -2.0)):
        lin(T.t64[:, q:q + 1], col[:, 1:2], sg, -LIFT, ["col1", "t64"], ["t64.%d" % q])
    spare.extend([
        lambda: ts(T.o64[:], jm[:, 144:196], cf[:, 0:1], None, A.add, r=["jm7", "cf"], w=["o64"]),
        lambda: ts(T.df[:, 0:16], jm[:, 0:16], cf[:, 0:1], None, A.subtract, r=["jm0", "cf"], w=["df0"]),
        lambda: ts(T.df[:, 16:32], jm[:, 16:32], cf[:, 1:2], None, A.subtract, r=["jm1", "cf"], w=["df1"]),
        lambda: ts(T.orr[:], T.zr[:, 0:32], cf[:, 0:1], None, A.add, r=["zr", "cf"], w=["orr"]),
        lambda: ts(T.ta[:], T.df[:], 0.0, -2.0, A.is_equal, A.mult, r=dfs, w=["ta"]),
        lambda: ts(T.tc[:], T.df[:], 1.0, None, A.is_equal, r=dfs, w=["tc"]),
        lambda: quant(T.qt, T.st, TOFF[-1], TOFF[-1] + 128, T.zr, r=["zr"], w=["qt.z"], at=0),
        lambda: ts(col[:, 2:3], T.df[:, 31:32], 0.0, -4.0 * BIGV, A.is_gt, A.mult, r=dfs, w=["col2"]),
        lambda: tt(T.tab[:, 0:32], T.ta[:], T.tc[:], A.add, r=["ta", "tc"], w=["tab0"]),
        lambda: ts(T.tab[:, 32:48], T.df[:, 0:16], 0.0, None, A.is_gt, r=dfs, w=["tab1"]),
        lambda: ts(col[:, 3:4], col[:, 2:3], cf[:, 2:3], 4.0 * MID, A.add, A.add, r=["col2", "cf"], w=["col3"]),
        lambda: ts(col[:, 0:1], T.df[:, 15:16], 0.0, BIG, A.is_gt, A.mult, r=dfs, w=["col0"]),
        lambda: ts(col[:, 13:14], T.df[:, 15:16], 0.0, T.ta[:, 0:1], A.is_gt, A.add, r=dfs + ["ta"], w=["col13"]),
    ])
    quant(T.q0, T.s0, 0, 128, T.xt, r=x0, w=["q0.0"])
    send(0)
    dma("sp", T.qw[:].bitcast(dt.uint8), T.wc[:], r=["q0.h"], w=["qw"])
    dma("sp", T.sw[:], T.ws[:], w=["sw"])
    dma("sp", T.vt[:], T.v[:], w=["vt"])
    gap(3)
    quant(T.qu, T.su, 0, 128, T.ut, r=["ut"], w=["qu"])
    gap(1)
    cp(T.qa[:].bitcast(dt.uint32), T.qu[:].bitcast(dt.uint32).indirect(T.oab[:]), r=["qu", "oab"], w=["qa"])
    act(T.sa[:], T.su[:].indirect(T.oab[:]), F.Copy, r=["qu", "oab"], w=["sa"])
    weave(0)
    quant(T.q0, T.s0, 128, C, T.xt, r=x1, w=["q0.1"])
    diagonal(T.et[:, 3:515:4], 1.0, ["et0"], ["et"])
    iota(T.ic[:], [[1, E]], -MID, 0, ["ic"])
    diagonals(0)
    iota(dg[:, 2:4 * E:4], [[0, E]], 0, 0, ["dg2a", "dg2b", "dg2l"])
    iota(dg[:, 4 * E:4 * EP], [[0, 4 * (EP - E)]], 0, 0, ["dgp"])
    for k in range(2):
        x = T.ct[:, 512 * k:512 * k + 512]
        keep(x, T.zr[:], 512, -1, -0.5, ["zr"], ["ct%d" % k])
        if k:
            keep(T.ct[:, 512:1024:4], T.zr[:, 0:128], 128, -1, -1.0, ["zr"], ["ct1"])
        keep(x, x, 512, 15, 0.0, [], ["ct%d" % k])
    for x, tok in ((T.rw[:, 0:2], "rw0"), (T.dk[:, 0:2], "dk0")):
        iota(x, [[0, 2]], 0, 0, [tok])
    for k, (cs, wd) in enumerate(TILES):
        lo = 0 if len(cs) < 4 else 16 * min(c for c in cs if c)
        dma("sp", T.tb[:, 4 * (TOFF[k] + lo):4 * (TOFF[k] + wd)], T.zr[:, 0:4 * (wd - lo)], r=["zr"],
            w=["tb%d.%d" % (k, j) for j in four] + ins * (k == TD))

    def unpack(t, banks, products):
        q, s = T["q%d" % t], T["s%d" % t]
        for b, k in banks:
            if products:
                mm(k, T.qe, T.se, 128 * b, q, s, E - 128, E, r=["qe%d" % b, "q%d.1" % t, "q%d.h" % t])
            else:
                act(T["vh%d" % t][:, 4 * C + b:4 * E:4], bank(k, 128 - H, 128), F.Copy, scale=0.5, w=["p%d" % k, "vh%d.h%d" % (t, b)])

    def classes(part, lo, hi, more):
        tt(dg[:, 4 * lo:4 * hi:4], T.mb[:, lo:hi], T.wb[:, lo + 1:hi + 1], A.add, r=["wbo", "mbo"] + more, w=["dg0" + part])
        n = int(part == "l")
        act(T.junk[:, lo:hi], dg[:, 4 * lo:4 * hi:4], F.Sign, scale=-1.0, bias=col[:, 5:6], accum_out=T.acc[:, n:n + 1],
            r=["dg0" + part, "col4"], w=["junk" + part, "acc" + part])

    def members(part, lo, hi, up):
        o = 2 * E if up else 1
        ts(zf[:, o + lo:o + hi], dg[:, 4 * lo:4 * hi:4], col[:, 4:5], MEM + 2.0 * up, A.is_equal, A.mult, r=["dg0" + part, "col4"], w=[("dn", "up")[up] + part])

    mm(0, T.qa, T.sa, 0, T.q0, T.s0, 0, C, r=["qa", "sa", "q0.0", "q0.1"])
    mm(1, T.qa, T.sa, 128, T.q0, T.s0, 0, C, r=["qa", "sa", "q0.0", "q0.1"])
    mm(2, T.qa, T.sa, 0, T.q0, T.s0, E - 128, E, r=["qa", "sa", "q0.1", "q0.h"])
    mm(3, T.qa, T.sa, 128, T.q0, T.s0, E - 128, E, r=["qa", "sa", "q0.1", "q0.h"])
    gap(5)
    act(T.a2[:, 0:C], bank(0, 0, C), F.Sign, bias=-TINY, r=["p0"], w=["a2o"])
    ts(T.ab[:, 0:C], bank(1, 0, C), 0.0, 1.5, A.is_gt, A.add, r=["p1"], w=["abo"])
    act(T.vh0[:, 0:4 * C], T.xt[:], F.Copy, scale=0.5, r=x0 + x1, w=["vh0.0", "vh0.1"])
    gap(1)
    tt(T.wb[:, 0:C], T.a2[:, 0:C], T.ab[:, 0:C], A.add, r=["a2o", "abo"], w=["wbo"])
    gap(1)
    ts(T.mb[:, 0:C], T.wb[:, 0:C], 4.0, -10.0, A.mult, A.add, r=["wbo"], w=["mbo"])
    gap(1)
    classes("o", 0, C - 2, [])
    weave(1)
    sa, sb = bank(2, 128 - H, 128), bank(3, 128 - H, 128)
    ts(T.a2[:, C:E], sa, 0.0, 2.0, A.is_gt, A.mult, r=["p2"], w=["a2l"])
    ts(T.a8[:], sa, 0.0, -8.0, A.is_le, A.mult, r=["p2"], w=["a8"])
    ts(T.ab[:, C:E], sb, 0.0, 0.5, A.is_gt, A.add, r=["p3"], w=["abl"])
    ts(T.b4[:], sb, 0.0, 4.0, A.is_gt, A.mult, r=["p3"], w=["b4"])
    tt(T.wb[:, C:E], T.a2[:, C:E], T.ab[:, C:E], A.add, r=["a2l", "abl"], w=["wbl"])
    tt(T.mb[:, C:E], T.a8[:], T.b4[:], A.add, r=["a8", "b4"], w=["mbl"])
    members("o", 0, C - 2, 1)
    classes("l", C - 2, E, ["wbl", "mbl", "wb.p"])
    members("o", 0, C - 2, 0)
    members("l", C - 2, E - 1, 1)
    ts(zf[:, 0:1], T.acc[:, 0:1], -1.0, MEM - E, A.mult, A.add, r=["acco"], w=["dn0"])
    members("l", C - 2, E - 1, 0)
    ts(T.acc[:, 2:3], T.acc[:, 0:1], 1.0 * E, None, A.add, r=["acco"], w=["acc2"])
    ts(T.acc[:, 3:4], dg[:, 4 * E - 4:4 * E - 3], col[:, 6:7], None, A.is_equal, r=["dg0l", "col4"], w=["acc3"])
    spread(T.d0v, C, 1, BIGV, ["d0v"])
    act(T.x32[:], T.xt[:], F.Copy, scale=32.0, r=x0 + x1, w=xs[0] + xs[1])
    unit(0)
    scan(zf[:, E:2 * E - 1], zf[:, 2 * E:3 * E - 1], zf[:, 0:E - 1], A.add, A.subtract,
         r=["upo", "upl", "dno", "dnl", "dn0", "accl"], w=["z"], first=T.acc[:, 1:2])
    ts(zf[:, 2 * E - 1:2 * E], T.acc[:, 1:2], T.acc[:, 2:3], T.acc[:, 3:4], A.add, A.mult, r=["accl", "acc2", "acc3"], w=["zl"])
    unit(1)
    turn(T.tz[:, 32:32 + 2 * E:2], zf[:, E:2 * E], ["z", "zl"], ["tz0"])
    turn(T.tz[:, 1:2 * E + 65:2], zf[:, E - 16:2 * E + 16], ["z", "zl", "dnl", "upo"], ["tz1"])
    unit(2)
    scan(T.th[:], T.d0t[:], T.tz[:, 32:32 + 2 * E], A.add, A.max, r=["d0t0", "d0t1", "tz0", "tz1"], w=["th"])
    unit(3)
    HALO0 = ((0, 4), (1, 5), (2, 6), (3, 7))
    unpack(0, HALO0, True)
    unpack(0, HALO0, False)

    OWN = {"a": (0, AB), "b": (AB, EB), "l": (EB, NB)}
    SCORE = {"a": 7, "b": 0, "l": 1}
    SUM, HALO = 2, ((0, 3), (1, 0), (2, 1), (3, 7))

    def row(t, part):
        top = max(c for c in range(NB) if c not in DVS[t])
        return {"a": (4, 0, 16 * AB), "b": (5, 0, 16 * EB), "l": (7, E - 128, E), "all": (6, 0, 16 * top)}[part]

    def score(t, part):
        a, b = PART[part]
        rs = {"a": [".0"], "b": [".1"], "l": [".1", ".h"]}[part]
        mm(SCORE[part], T.qa, T.sa, 0, T["q%d" % t], T["s%d" % t], min(a, b - 128), b, r=["qa", "sa"] + ["q%d%s" % (t, n) for n in rs])

    def signs(t, part):
        a, b = PART[part]
        k = SCORE[part]
        o = max(0, 128 - (b - a))
        ts(dg[:, 4 * a + t:4 * b:4], bank(k, o, o + b - a), 0.0, None, A.is_gt, w=["p%d" % k, "dg%d%s" % (t, part)])

    def digits(t, part):
        a, b = PART[part]
        quant(T["qd%d" % t], T["sd%d" % t], a, max(b, a + 128), dg,
              r=["dg0o", "dg0l", "dg3", "dgp", "dg1" + part, "dg2" + part], w=["qd%d%s" % (t, part)])

    def keys(t, part, old):
        terms = {(1, False): ((0, 0), (1, 2)), (2, True): ((3, 2), (1, 6)), (2, False): ((2, 0), (0, 4))}.get((t, old), ())
        u = t - old
        have = "abl" if old else {"a": "a", "b": "ab", "l": "bl", "all": "abl"}[part]
        for i, (c, d) in enumerate(terms):
            k, lo, hi = row(t, part)
            mm(k, T.qk, T.sk8, 128 * c, T["qd%d" % u], T["sd%d" % u], lo + d, hi + d,
               r=["qk%d" % (c // 2)] + ["qd%d%s" % (u, p) for p in have], start=i == 0 and (old or t == 1), stop=i == 1 and not old)

    def hold(t, part):
        a, b = (16 * c for c in OWN[part])
        k, lo, _ = row(t, part)
        scan(T.sk[:, a:b], T.d0k[:, a:b], bank(k, a - lo, b - lo), A.add, A.max, r=["d0k", "p%d" % k], w=["sk." + part])

    def tied(t, part):
        a, b = (16 * c for c in OWN[part])
        k, lo, _ = row(t, part)
        tt(T["kt%d" % t][:, a:b], bank(k, a - lo, b - lo), T["tie%d" % t][:, a:b], A.add, r=["p%d" % k] + tie_of[t], w=["tied." + part])

    def owned(t, part):
        c0, c1 = OWN[part]
        c1 = min(c1, NB - 1)
        ts(T.kw[:, c0:c1], T.sk[:, 16 * c0 + 15:16 * c1:16], col[:, 0:1], STEP[t], A.subtract, A.add, r=["sk." + part, "col0"], w=["kw." + part])
        if part == "l":
            ts(T.kw[:, c1:NB], T.sk[:, E - 1:E], T.cc[:, 31 + t:32 + t], STEP[t], A.add, A.add, r=["sk.l", "cc%d" % t], w=["kw.z"])

    def inside(t, part):
        c0, c1 = {"a": (0, AB - 1), "b": (AB - 1, EB - 1), "l": (EB - 1, NB)}[part]
        o = 4 * TOFF[TD]
        tt(T.tb[:, o + 64 * c0:o + 64 * c1:4], T.kw[:, 0:c1].indirect(T.od[:, c0:c1]), T["kt%d" % t][:, 16 * c0:16 * c1], A.is_gt,
           r=["kw.a", "tied.a", "od"] + ["kw.b", "tied.b"] * (part != "a") + ["kw.l", "kw.z", "tied.l"] * (part == "l"), w=["in." + part])

    def lane(c):
        k = [c in cs for cs, _ in TILES].index(True)
        j = TILES[k][0].index(c)
        o = 4 * TOFF[k] + j
        return k, T.tb[:, o:o + 64 * c - j:4], "tb%d.%d" % (k, j)

    def compare(t, cs, mine):
        for c in cs:
            if (c in DVS[t]) != mine:
                continue
            _, out, tok = lane(c)
            own = "kw.z" if c == NB - 1 else "kw.l" if c >= EB else "kw.b" if c >= AB else "kw.a"
            if mine:
                ts(out, T["kt%d" % t][:, 0:16 * c], T.kw[:, c:c + 1], 2.0, A.is_le, A.mult,
                   r=["tied." + p for p in "abl" if OWN[p][0] < c] + [own], w=[tok])
            else:
                kb = row(t, "a" if c <= AB else "b" if c <= EB else "all")[0]
                act(out, bank(kb, 0, 16 * c), F.Sign, scale=-1.0, bias=T.kw[:, c:c + 1], accum_out=T.rw[:, c:c + 1],
                    r=["p%d" % kb, own, "tied.a"] + ["tied.b"] * (c > AB), w=[tok, "rw%d" % c] + ["rw0"] * (c == 1))

    def above(t, c):
        return len([x for x in DVS[t] if x > c])

    def rowsum(t, cs):
        for c in cs:
            if c in DVS[t]:
                _, x, tok = lane(c)
                i = DVS[t].index(c) + 1
                scan(T.jk[:, E * i - 16 * c:E * i], x, T.zr[:, 0:16 * c], A.add, A.add, r=[tok, "zr"], w=["rw%d" % c],
                     first=16.0 * (above(t, c) - c))

    def fold(c, sums, stop=False):
        k = lane(c)[0]
        quant(T.qt, T.st, TOFF[k], TOFF[k] + TILES[k][1], T.tb, r=["tb%d.%d" % (k, j) for j in four] + ins * (k == TD), w=["qt%d" % k])
        for x in sums:
            k = lane(x)[0]
            mm(SUM, T.qc, T.sc, 128 if k == TD else 0, T.qt, T.st, TOFF[k], TOFF[k] + (E if k == TF else TILES[k][1]),
               r=["qc", "qt%d" % k, "qt.z"], start=k == TF, stop=stop)

    def rows(t, c0):
        c1 = min(c for c in range(c0, NB + 1) if c == NB or (c in DVS[t]) != (c0 in DVS[t]))
        out = T.d1k[:, 16 * c0 + 16:16 * c1 + 1:16]
        rs = ["rw%d" % c for c in range(c0, c1)] + ["off", "d1k"]
        if c0 in DVS[t]:
            i = DVS[t].index(c0)
            ts(out, T.jk[:, E * i + E - 1:E * (i + c1 - c0):E], 0.5, T.off[:, 0:1], A.mult, A.add, r=rs, w=["rc%d" % c0])
        else:
            n = above(t, c0)
            ts(out, T.rw[:, c0:c1], 0.5, T.off[:, n:n + 1], A.mult, A.add, r=rs, w=["rc%d" % c0])
        return "rc%d" % c0

    def half(t, h):
        a, b = CH[h]
        act(T["vh%d" % t][:, 4 * a:4 * b], T.x32[:, 4 * a:4 * b], F.Copy, scale=0.015625, r=xs[h], w=["vh%d.%d" % (t, h)])

    def order(t):
        top = min(c for c in DVS[t] if c >= EB)
        compare(t, (15, 16, 17, 18, 11, 12, 13, 14), False)
        digits(t, "l")
        keys(t, "l", False)
        keys(t, "all", False)
        missing(t, 1)
        fold(3, ())
        inside(t, "a")
        fold(7, ())
        inside(t, "b")
        hold(t, "l")
        tied(t, "l")
        fold(1, ())
        owned(t, "l")
        compare(t, (19, 20, 21, 22), False)
        rowsum(t, (6, 5, 4, 3))
        fold(15, (15, 7, 3, 1))
        compare(t, (23, 25), True)
        inside(t, "l")
        compare(t, (24, 22), True)
        rowsum(t, (23,))
        fold(11, (11,))
        fold(25, (25,))
        rowsum(t, (25, 22))
        fold(19, (19,), stop=True)
        half(t, 0)
        half(t, 1)
        unpack(t, HALO, True)
        unpack(t, HALO, False)
        rowsum(t, (24,))
        rcs = [rows(t, c) for c in (3, 0, 7, top)]
        scan(T.ps[:], bank(SUM, 0, E), T.d1k[:, 1:E + 1], A.max, A.add, r=["d1k"] + rcs, w=["ps", "p%d" % SUM], first=-BIGP)

    for t in range(R):
        vh = T["vh%d" % t]
        last = t == R - 1
        u = t + 1
        if t:
            order(t)
            x, y, c0, c1, rs = T.ps[:, 15:E:16], T.ps[:, 15:C:16], col[:, 10:11], col[:, 11:12], ["ps", "col10", "col11"]
            ts(T.pos[:, 0:NB], x, c0, None, A.subtract, r=rs, w=poss)
            ts(T.onm[:, 20:40], y, c1, E - 1.0, A.subtract, A.min, r=rs, w=["om"])
            ts(T.onm[:, 0:20], y, c0, 1.0, A.subtract, A.subtract, r=rs, w=["on"])
        else:
            for k in range(2):
                ts(T.pos[:, k:NB:2], T.th[:, 31 + 32 * k:2 * E:64], col[:, 14 + k:15 + k], 0.5, A.subtract, A.mult, r=["th", "col%d" % (14 + k)], w=["pos%d" % k])
            gap(1)
        cp(T.ordr[:, 0:E].indirect(T.pos[:, 0:NB]), T.ic[:], r=poss + ["ic"], w=["ordr"])
        if t == 0:
            ts(T.onm[:, 20:40], T.pos[:, 0:20], 1.0, E - 1.0, A.add, A.min, r=poss, w=["om"])
            ts(T.onm[:, 0:20], T.pos[:, 0:20], 1.0, None, A.subtract, r=poss, w=["on"])
            ts(T.od[:, 0:NB], T.ic[:, 0:NB], 1.0 * MID, None, A.add, r=["ic"], w=["od"])
        elif last:
            act(T.d0p[:], T.d0k[:], F.Copy, scale=LOW, r=["d0k"], w=["d0p"])
        for h, (a, b) in enumerate(CH):
            act(T.gn[:, a:b], T.ordr[:, 0:E].indirect(T.onm[:, a // 16:b // 16]), F.Copy, r=["ordr", "on"], w=["gn%d" % h])
            cp(T.gm[:, a:b], T.ordr[:, 0:E].indirect(T.onm[:, 20 + a // 16:20 + b // 16]), r=["ordr", "om"], w=["gm%d" % h])

        def near(h, n):
            a, b = CH[h]
            scan(T["s" + n][:, a:b], T.d0v[:, a:b], T["g" + n][:, a:b], A.add, A.max, r=["g%s%d" % (n, h), "d0v"], w=["s%s%d" % (n, h)])

        def offs(h, n):
            a, b = CH[h]
            o = 80 * (n == "m")
            ts(T.ov[:, o + a // 4:o + b // 4], T["s" + n][:, a + 3:b:4], 4.0, col[:, 3:4], A.mult, A.add, r=["s%s%d" % (n, h), "col3"], w=["ov%s%d" % (n, h)])

        vr = ["vh%d.0" % t, "vh%d.1" % t] + ["vh%d.h%d" % (t, b) for b in four]

        def pick(k, n):
            a, b = PIECES[k]
            o = 80 * (n == "m")
            return vh[:, 0:4 * E].indirect(T.ov[:, o + a // 4:o + b // 4]), vr + ["ov%s%d" % (n, a >= C0)]

        def gather(k, n):
            a, b = PIECES[k]
            x, rs = pick(k, n)
            if n == "m":
                act(T.g1[:, 4 * a:4 * b], x, F.Copy, r=rs, w=["g1.%d" % k])
            elif MODE[k] == "A":
                act(T.g3[:, 4 * a:4 * b], x, F.Copy, r=rs, w=["g3.%d" % k])
            else:
                cp(T.g3[:, 4 * a:4 * b], x, r=rs, w=["g3.%d" % k])

        def most(k):
            a, b = PIECES[k]
            x, rs = pick(k, "n") if MODE[k] == "F" else (T.g3[:, 4 * a:4 * b], ["g3.%d" % k])
            tt(T.g2[:, 4 * a:4 * b], x, T.g1[:, 4 * a:4 * b], A.max, r=rs + ["g1.%d" % k], w=["g2.%d" % k])

        def blend(k):
            a, b = PIECES[k]
            tt(T.zt[:, 4 * a:4 * b], T.g2[:, 4 * a:4 * b], vh[:, 4 * a:4 * b], A.add, r=["g2.%d" % k] + vr, w=["zt%d" % k])

        def pack(h):
            a, b = CH[h]
            quant(T.qz, T.sz, a, b, T.zt, r=["zt%d" % k for k, p in enumerate(PIECES) if a <= p[0] < b], w=["qz%d" % h])

        def layer(h, js):
            a, b = CH[h]
            for j in js:
                mm(j, T.qw, T.sw, 128 * j, T.qz, T.sz, a, b, r=["qw", "sw", "qz%d" % h])

        def state(h, js):
            a, b = CH[h]
            for j in js:
                x = T.x32[:, 4 * a + j:4 * b:4]
                tt(x, bank(j, 0, b - a), x, A.add, w=["p%d" % j, "x32.%d.%d" % (h, j)])
                if j < 2:
                    act(T.xt[:, 4 * a + j:4 * b:4], x, F.Copy, scale=0.03125, r=["x32.%d.%d" % (h, j)], w=["xt.%d.%d" % (h, j)])

        def shrink(h, j):
            a, b = CH[h]
            ts(T.xt[:, 4 * a + j:4 * b:4], T.x32[:, 4 * a + j:4 * b:4], 0.03125, None, A.mult, r=["x32.%d.%d" % (h, j)], w=["xt.%d.%d" % (h, j)])

        def fresh(h):
            a, b = CH[h]
            quant(T["q%d" % u], T["s%d" % u], a, b, T.xt, r=(x0, x1)[h], w=["q%d.%d" % (u, h)])

        near(0, "m")
        near(0, "n")
        near(1, "m")
        offs(0, "m")
        for k in (0, 2, 1, 3):
            gather(k, "m")
        near(1, "n")
        offs(0, "n")
        if last:
            scan(T.th[:, 0:E], T.d0p[:], T.ordr[:], A.add, A.max, r=["d0p", "ordr"], w=["th"])
        else:
            weights(t)
        for part in ("a", "b", "all"):
            keys(u, part, True)
        offs(1, "m")
        offs(1, "n")
        gather(1, "n")
        gather(4, "m")
        gather(5, "n")
        gather(5, "m")
        if t == 0:
            act(dg[:, 3:4 * E:4], dg[:, 0:4 * E:4], F.Sign, scale=-1.0, bias=dg[:, 4 * E - 4:4 * E - 3], r=["dg0o", "dg0l"], w=["dg3"])
            spread(T.d0k, E, 0, BIG, ["d0k"])
        elif t == 1:
            ties(u, 0)
            ties(u, 1)
        most(0)
        if last:
            ts(T.ow[:, 0:NB], T.th[:, 15:E:16], col[:, 12:13], None, A.subtract, r=["th", "col12"], w=["ow"])
            act(T.ks[:], T.kt2[:, 0:E].indirect(T.ow[:, 0:NB]), F.Copy, scale=512.0, r=tieds + ["ow"], w=["ks"])
        most(2)
        blend(0)
        most(1)
        most(3)
        blend(2)
        blend(1)
        blend(3)
        most(4)
        pack(0)
        layer(0, four)
        most(5)
        blend(4)
        blend(5)
        state(0, (0, 1))
        pack(1)
        layer(1, (0, 1))
        state(0, (2, 3))
        layer(1, (2, 3))
        if last:
            break
        shrink(0, 2)
        shrink(0, 3)
        state(1, (0, 1))
        fresh(0)
        send(u)
        score(u, "a")
        state(1, (2, 3))
        if t == 0:
            diagonals(1)
            ties(u, 0)
            ties(u, 1)
            spread(T.d1k, E + 16, 0, BIGP, ["d1k"])
            lin(col[:, 8:9], T.ta[:, 0:1], BIGP, MID + 8.0, ["ta"], ["col8"])
            lin(col[:, 10:11], col[:, 13:14], BIGP, 0.0, ["col13"], ["col10"])
            lin(T.off[:], jm[:, 0:16], 8.0, col[:, 8:9], ["jm0", "col8"], ["off"])
            lin(col[:, 11:12], col[:, 13:14], BIGP, -1.0, ["col13"], ["col11"])
            lin(col[:, 12:13], col[:, 0:1], LOW, -1.0 * MID, ["col0"], ["col12"])
        shrink(1, 2)
        shrink(1, 3)
        signs(u, "a")
        fresh(1)
        score(u, "b")
        digits(u, "a")
        keys(u, "a", False)
        if t == 0:
            quant(T.qc, T.sc, 0, 256, T.ct, r=["ct0", "ct1"], w=["qc"])
        else:
            quant(T.qv, T.sv, 0, 128, T.vt, r=["vt"], w=["qv"])
        signs(u, "b")
        digits(u, "b")
        keys(u, "b", False)
        score(u, "l")
        keys(u, "l", True)
        hold(u, "a")
        tied(u, "a")
        missing(u, 0)
        owned(u, "a")
        compare(u, (10, 9, 8, 7, 2, 1), False)
        compare(u, (6, 5), True)
        hold(u, "b")
        tied(u, "b")
        signs(u, "l")
        compare(u, (4, 3), True)
        owned(u, "b")
    q, s = T.q3, T.s3

    def leave(h):
        a, b = CH[h]
        mm(4 + h, T.qv, T.sv, 0, q, s, a, b, r=["qv", "q3.%d" % h])
        dma("sp", T.oc[:, 4 * a:4 * b], q[:, a:b].bitcast(dt.uint8), r=["q3.%d" % h])

    def result(h):
        a, b = CH[h]
        act(T.ys[:, a:b], bank(4 + h, 0, b - a), F.Copy, w=["p%d" % (4 + h), "ys%d" % h])
        dma("act", T.y[:, a:b], T.ys[:, a:b], r=["ys%d" % h])

    def scales(eng, k):
        dma(eng, T.osc[4 * k:4 * k + 4, :], s[32 * k:32 * k + 4, 0:C], r=["q3.0", "q3.1"])

    shrink(0, 2)
    state(1, (0,))
    shrink(0, 3)
    state(1, (1, 2, 3))
    fresh(0)
    leave(0)
    result(0)
    shrink(1, 2)
    shrink(1, 3)
    tt(T.dk[:, 1:MID], T.ks[:, 1:MID], T.ks[:, 0:MID - 1], A.subtract, r=["ks"], w=["dk0", "dk1"])
    fresh(1)
    leave(1)
    scales("sp", 0)
    tt(T.dk[:, MID:E], T.ks[:, MID:E], T.ks[:, MID - 1:E - 1], A.subtract, r=["ks"], w=["dk2"])
    result(1)
    scales("sp", 1)
    scales("sp", 2)
    scan(T.ls[:], T.dk[:], T.ic[:], A.add, A.min, r=["dk1", "dk2", "ic"], w=["ls"])
    ts(T.lr[:, 0:LV], T.ls[:, 0:E].indirect(T.pos[:, 0:LV // 16]), 1.0 * MID, None, A.add, r=["ls"] + poss, w=["lr0"])
    act(T.lr[:, LV:E], T.ls[:, 0:E].indirect(T.pos[:, LV // 16:NB]), F.Identity, bias=1.0 * MID, r=["ls"] + poss, w=["lr1"])
    scales("act", 3)
    dma("sp", T.lv[:], T.lr[15:128:16, :], r=["lr0", "lr1"])
    for sname, v in cnt.items():
        g.wait_ge(T.sem[sname], v)
